import numpy as np
import ml_dtypes


def mxq(x, axis, fmt="e4m3"):
    dtype, down = {"e4m3": (ml_dtypes.float8_e4m3fn, 7), "e5m2": (ml_dtypes.float8_e5m2, 14)}[fmt]
    v = np.moveaxis(np.asarray(x, np.float32).astype(ml_dtypes.bfloat16).astype(np.float64), axis, -1)
    blocks = v.reshape(v.shape[:-1] + (-1, 32))
    amax = np.abs(blocks).max(-1, keepdims=True)
    byte = np.maximum(np.where(amax > 0, np.frexp(amax)[1] - 1 + 127, 0) - down, 1)
    scale = np.exp2(byte - 127.0)
    codes = (blocks / scale).astype(np.float32).astype(dtype).astype(np.float64)
    return np.moveaxis((codes * scale).reshape(v.shape), -1, axis)


WIDE = False


def mx_kscale(k):
    if not WIDE:
        return np.ones(k)
    levels = np.array([10, -10, 5, -5, 0])
    if k % 512:
        return np.exp2(np.random.permutation(np.resize(levels, k // 32))).repeat(32)
    a = np.empty((k // 512, 16))
    for p in range(k // 512):
        a[p, :8] = np.random.permutation(np.resize(levels, 8))
        for g in range(8):
            far = levels[np.abs(levels - a[p, g]) >= 10]
            a[p, g + 8] = far[np.random.randint(len(far))]
    return np.exp2(a.ravel()).repeat(32)


def f64(x):
    return np.asarray(x).astype(np.float64)


def striped(idx):
    return np.tile(idx.reshape(-1, 16).T, (8, 1)).astype(np.uint16)


def unstriped(offs):
    return offs[:16].T.reshape(-1).astype(np.int64)


E2M1 = np.array([0.0, 0.5, 1.0, 1.5, 2.0, 3.0, 4.0, 6.0, -0.0, -0.5, -1.0, -1.5, -2.0, -3.0, -4.0, -6.0])


def pack_weight(w, fmt):
    k, n = w.shape
    w = f64(np.asarray(w, np.float32).astype(ml_dtypes.bfloat16)).reshape(k // 32, 32, n)
    amax = np.abs(w).max(1)
    if fmt == "e4m3":
        byte = np.frexp(amax)[1] - 1 + 127 - 7
    else:
        mant, ex = np.frexp(amax / 6.0)
        byte = np.where(mant > 0.5, ex, ex - 1) + 127
    byte = np.clip(np.where(amax > 0, byte, 1), 1, 254)
    scaled = (w * np.exp2(127.0 - byte)[:, None, :]).reshape(k, n).astype(np.float32)
    by_word = np.ascontiguousarray(scaled.reshape(k // 512, 128, 4, n).transpose(0, 1, 3, 2))
    if fmt == "e4m3":
        words = by_word.astype(ml_dtypes.float8_e4m3fn).view(np.uint8)
    else:
        c = by_word.astype(ml_dtypes.float4_e2m1fn).view(np.uint8) & 0xF
        words = (c[..., 0::2] | (c[..., 1::2] << 4)).reshape(k // 512, 128, 2 * n)
    return np.ascontiguousarray(words), np.ascontiguousarray(byte.astype(np.uint8).reshape(k // 512, 16, n))


def unpack_weight(words, scales, fmt):
    g, _, n = scales.shape
    words = np.ascontiguousarray(words).reshape(g, 128, n, -1)
    if fmt == "e4m3":
        vals = words.view(ml_dtypes.float8_e4m3fn).astype(np.float64)
    else:
        nib = np.empty((g, 128, n, 4), np.uint8)
        nib[..., 0::2] = words & 0xF
        nib[..., 1::2] = words >> 4
        vals = E2M1[nib]
    vals = vals * np.repeat(np.exp2(scales.astype(np.float64) - 127.0), 8, axis=1)[..., None]
    return vals.transpose(0, 1, 3, 2).reshape(g * 512, n)


def gelu(v):
    return 0.5 * v * (1.0 + np.tanh(np.sqrt(2.0 / np.pi) * (v + 0.044715 * v**3)))


K, H, N, T, S, P = 1024, 1024, 512, 2048, 1024, 512

def setup_inputs():
    n = np.random.standard_normal
    s = mx_kscale(K)[:, None]
    u = mx_kscale(H)[:, None]
    tab_words, tab_scales = pack_weight(n((K, T)) * s, "e4m3")
    wg_words, wg_scales = pack_weight(1.2 * n((K, H)) / np.sqrt(K) / s, "e2m1")
    wu = (1.2 * n((K, H)) / np.sqrt(K) / s * u.T).astype(np.float32)
    w2 = (1.5 * n((H, N)) / np.sqrt(H) / u).astype(np.float32)
    offs = striped(np.random.permutation(T)[:S])
    pos1 = striped(np.random.permutation(S)[:P])
    pos2 = striped(np.random.permutation(S)[:P])
    return {"tab_words": tab_words, "tab_scales": tab_scales, "offs": offs,
            "wg_words": wg_words, "wg_scales": wg_scales, "wu": wu, "w2": w2,
            "pos1": pos1, "pos2": pos2}

def reference(tab_words, tab_scales, offs, wg_words, wg_scales, wu, w2, pos1, pos2):
    v = unpack_weight(tab_words, tab_scales, "e4m3")[:, unstriped(offs)]
    wg = unpack_weight(wg_words, wg_scales, "e2m1")
    wuq = mxq(f64(wu), 0, "e4m3")
    w2q = mxq(f64(w2), 0, "e4m3")
    b = wg.T @ v
    a = wuq.T @ v
    h = a * (b / (1.0 + np.exp(-b)))
    z = 0.7 * h[:, unstriped(pos1)] + 0.3 * h[:, unstriped(pos2)]
    zq = mxq(z, 0, "e4m3")
    return w2q.T @ zq

@@ -1,0 +1,288 @@
+from contextlib import ExitStack
+
+import concourse.mybir as mybir
+
+K, H, N, T, S, M = 1024, 1024, 512, 2048, 1024, 512
+FLOPS = 2 * (2 * K * H * S + H * N * M)
+
+F32 = mybir.dt.float32
+BF16 = mybir.dt.bfloat16
+I32 = mybir.dt.int32
+U32 = mybir.dt.uint32
+U16 = mybir.dt.uint16
+U8 = mybir.dt.uint8
+FP8X4 = mybir.dt.float8_e4m3fn_x4
+FP4X4 = mybir.dt.float4_e2m1fn_x4
+ALU = mybir.AluOpType
+ACT = mybir.ActivationFunctionType
+
+P = 128
+PASS = 512
+BANK = 512
+W1, W2 = 0.7, 0.3
+RING = 3
+
+
+def tile_list_gated_token_merge_kernel(tc, tab_words, tab_scales, offs, wg_words, wg_scales, wu, w2, pos1, pos2, out):
+    nc = tc.nc
+    with ExitStack() as ctx:
+        sb = ctx.enter_context(tc.tile_pool(name="sb", bufs=1))
+        ps = ctx.enter_context(tc.psum_pool(name="ps", bufs=1))
+
+        def tile(name, shape, dtype, tag=None):
+            return sb.tile(shape, dtype, name=name, tag=tag or name, align_bytes=64)
+
+        offs_sb = tile("offs_sb", [P, S // 16], U16)
+        pos1_sb = tile("pos1_sb", [P, M // 16], U16)
+        pos2_sb = tile("pos2_sb", [P, M // 16], U16)
+        tab_sc = tile("tab_sc", [P, T], U8, "load3")
+        tab_w = [tile("tab_w%d" % a, [P, T], I32, "load%d" % a) for a in range(2)]
+        v_w = [tile("v_w%d" % a, [P, S], U32) for a in range(2)]
+        v_sc = tile("v_sc", [P, S], U8)
+        v_sc1 = tile("v_sc1", [P, S], U8)
+        wg_raw = {}
+        tab_sc_rows = tile("tab_sc_rows", [P, T // 4], I32, "load2")
+        wg_w = [tile("wg_w%d" % b, [P, 2, 256], I32) for b in range(2)]
+        wg_sc_raw = tile("wg_sc_raw", [P, 2, 256], I32)
+        wg_sc = tile("wg_sc", [P, 512], I32)
+        wu_raw = [{}, {}]
+        wu_bf = [[[tile("wu_bf%d%d%d" % (a, b, u), [P, 1024], BF16) for u in range(2)] for b in range(2)] for a in range(2)]
+        wu_w = [[tile("wu_w%d%d" % (a, b), [P, PASS], U32) for b in range(2)] for a in range(2)]
+        wu_sc = [[tile("wu_sc%d%d" % (a, b), [P, PASS], U8) for b in range(2)] for a in range(2)]
+        w2_raw = {}
+        w2_bf = [tile("w2_bf%d" % b, [P, 4 * N], BF16) for b in range(2)]
+        w2_w = [tile("w2_w%d" % b, [P, N], U32) for b in range(2)]
+        w2_sc = [tile("w2_sc%d" % b, [P, N], U8) for b in range(2)]
+        hs = [tile("hs%d" % r, [P, 2 * S], F32) for r in range(RING - 1)]
+        first = [tile("first%d" % r, [P, M], F32) for r in range(2)]
+        z_f = [tile("z_f%d" % b, [P, 4, M], F32) for b in range(2)]
+        z_bf = [[tile("z_bf%d%d" % (b, u), [P, 2 * M], BF16) for u in range(2)] for b in range(2)]
+        z_w = [[tile("z_w%d%d" % (b, u), [P, M // 2], U32) for u in range(2)] for b in range(2)]
+        z_sc = [[tile("z_sc%d%d" % (b, u), [P, M // 2], U8) for u in range(2)] for b in range(2)]
+        res = [[tile("res%d%d" % (u, i), [P, BANK], F32) for i in range(2)] for u in range(2)]
+        warm = tile("warm", [P, 16], F32)
+        bank_a = [ps.tile([P, BANK], F32, name="bank_a%d" % u) for u in range(2)]
+        bank_b = [ps.tile([P, BANK], F32, name="bank_b%d" % u) for u in range(2)]
+        bank_o = [[ps.tile([P, BANK], F32, name="bank_o%d%d" % (u, i)) for i in range(2)] for u in range(2)]
+
+        nc.vector.memset(tab_sc[:].bitcast(I32), 0)
+        nc.sync.dma_start(offs_sb[:], offs)
+        nc.sync.dma_start(pos1_sb[:], pos1)
+        nc.sync.dma_start(pos2_sb[:], pos2)
+        for q in range(4):
+            nc.sync.dma_start(tab_sc_rows[32 * q : 32 * q + 8, :], tab_scales[:, 4 * q : 4 * q + 4, :].bitcast(I32))
+        nc.vector.memset(warm[:, 0:8], 0.0)
+        nc.scalar.activation(warm[:, 8:16], warm[:, 0:8], ACT.Silu)
+        nc.vector.memset(wg_sc_raw[:], 0)
+        nc.vector.memset(v_sc1[:].bitcast(I32), 0)
+
+        def load_wg(b):
+            wg_raw[b] = tile("wg_raw%d" % b, [P, 2, 256], I32, "wg_raw")
+            nc.sync.dma_start(wg_raw[b][:], wg_words[:, :, 1024 * b : 1024 * (b + 1)].bitcast(I32).rearrange("a p n -> p a n"))
+
+        def load_wu(a, b):
+            wu_raw[a][b] = tile("wu_raw%d%d" % (a, b), [P, 4, PASS], F32, "load%d" % (2 + a - 2 * b))
+            rows = wu[PASS * a : PASS * (a + 1), PASS * b : PASS * (b + 1)]
+            nc.sync.dma_start(wu_raw[a][b][:], rows.rearrange("(p i) c -> p i c", i=4))
+
+        def load_w2(b):
+            w2_raw[b] = tile("w2_raw%d" % b, [P, 4, N], F32, ("load3", "load0")[b])
+            rows = w2[PASS * b : PASS * (b + 1), :].rearrange("(g t j) n -> t g j n", t=4, j=8)
+            for t in range(4):
+                nc.sync.dma_start(w2_raw[b][:, t, :], rows[t])
+
+        for a in range(2):
+            nc.sync.dma_start(tab_w[a][:], tab_words[a].rearrange("p n i -> p (n i)").bitcast(I32))
+        load_wg(0)
+        for q in range(4):
+            nc.sync.dma_start(
+                wg_sc_raw[32 * q : 32 * q + 4, :, :],
+                wg_scales[:, 4 * q : 4 * q + 4, :].bitcast(I32).rearrange("a r n -> r a n"),
+            )
+
+        for q in range(4):
+            nc.vector.tensor_copy(tab_sc[32 * q : 32 * q + 8, :].bitcast(I32), tab_sc_rows[32 * q : 32 * q + 8, :])
+        load_wu(0, 0)
+        nc.vector.tensor_copy(v_sc[:], tab_sc[:].indirect(offs_sb[:]))
+        nc.scalar.dma_start(v_sc1[0:112, :].bitcast(I32), v_sc[4:116, :].bitcast(I32))
+        load_wu(1, 0)
+        for a in range(2):
+            nc.vector.tensor_copy(v_w[a][:], tab_w[a][:].bitcast(U32).indirect(offs_sb[:]))
+            load_wu(a, 1)
+
+        def order_wg(b):
+            nc.vector.tensor_copy(
+                wg_w[b][:].rearrange("p a (t g w) -> p a t g w", t=4, w=4),
+                wg_raw[b][:].rearrange("p a (g t w) -> p a t g w", t=4, w=4),
+            )
+
+        def order_wg_scales():
+            nc.vector.tensor_copy(
+                wg_sc[:].rearrange("p (x t g w) -> p x t g w", x=4, t=4, w=2),
+                wg_sc_raw[:].rearrange("p a (b g t w) -> p (a b) t g w", b=2, t=4, w=2),
+            )
+
+        def cast_wu_scalar(a, b, t):
+            dst = wu_bf[a][b][t // 2][:, 512 * (t % 2) : 512 * (t % 2 + 1)]
+            nc.scalar.copy(
+                dst.rearrange("p (g h j i) -> p g h i j", h=2, j=4, i=4),
+                wu_raw[a][b][:].rearrange("p i (g t h j) -> p t g h i j", t=4, h=2, j=4)[:, t],
+            )
+
+        def cast_wu_vector(a, b, u):
+            nc.vector.tensor_copy(
+                wu_bf[a][b][u][:].rearrange("p (t g j i) -> p t g j i", t=2, j=8, i=4),
+                wu_raw[a][b][:].rearrange("p i (g t j) -> p t g j i", t=4, j=8)[:, 2 * u : 2 * u + 2],
+            )
+
+        def quant_wu(a, b, u):
+            cols = slice(256 * u, 256 * (u + 1))
+            nc.vector.quantize_mx(wu_w[a][b][:, cols].bitcast(FP8X4), wu_sc[a][b][:, cols], wu_bf[a][b][u][:])
+
+        def cast_w2(b, u):
+            nc.scalar.copy(
+                w2_bf[b][:, 1024 * u : 1024 * (u + 1)].rearrange("p (c j t) -> p c t j", j=4, t=4),
+                w2_raw[b][:, :, 256 * u : 256 * (u + 1)].rearrange("p t (c j) -> p c t j", j=4),
+            )
+
+        def quant_w2(b):
+            nc.vector.quantize_mx(w2_w[b][:].bitcast(FP8X4), w2_sc[b][:], w2_bf[b][:])
+
+        def gate(k, u):
+            b, t = divmod(k, 4)
+            cols = slice(BANK * u, BANK * (u + 1))
+            for a in range(2):
+                x = 2 * a + b
+                nc.tensor.matmul_mx(
+                    bank_b[u][:],
+                    lhsT=wg_w[b][:, a, 64 * t : 64 * (t + 1)].bitcast(FP4X4),
+                    lhsT_scale=wg_sc[:, 128 * x + 32 * t : 128 * x + 32 * (t + 1)].bitcast(U8),
+                    rhs=v_w[a][:, cols].bitcast(FP8X4),
+                    rhs_scale=(v_sc, v_sc1)[a][:, cols],
+                    start=(a == 0),
+                    stop=(a == 1),
+                )
+            nc.scalar.activation(hs[(k - 1) % RING][:, S + BANK * u : S + BANK * (u + 1)], bank_b[u][:], ACT.Silu)
+
+        def up(k, u):
+            b, t = divmod(k, 4)
+            cols = slice(BANK * u, BANK * (u + 1))
+            rows = slice(P * t, P * (t + 1))
+            for a in range(2):
+                nc.tensor.matmul_mx(
+                    bank_a[u][:],
+                    lhsT=wu_w[a][b][:, rows].bitcast(FP8X4),
+                    lhsT_scale=wu_sc[a][b][:, rows],
+                    rhs=v_w[a][:, cols].bitcast(FP8X4),
+                    rhs_scale=v_sc[4 * a : P, cols],
+                    start=(a == 0),
+                    stop=(a == 1),
+                )
+
+        def product(k, u):
+            nc.vector.tensor_tensor(
+                hs[k % RING][:, BANK * u : BANK * (u + 1)],
+                bank_a[u][:],
+                hs[(k - 1) % RING][:, S + BANK * u : S + BANK * (u + 1)],
+                ALU.mult,
+            )
+
+        def pick_first(k):
+            nc.vector.tensor_scalar(first[k % 2][:], hs[k % RING][:].indirect(pos1_sb[:]), W1 / W2, 0.0, ALU.mult, ALU.add)
+
+        def pick_second(k):
+            b, t = divmod(k, 4)
+            nc.vector.tensor_tensor(z_f[b][:, t, :], hs[k % RING][:].indirect(pos2_sb[:]), first[k % 2][:], ALU.add)
+
+        def round_z(b, u, on_vector):
+            dst = z_bf[b][u][:].rearrange("p (c j t) -> p c t j", j=4, t=4)
+            src = z_f[b][:, :, 256 * u : 256 * (u + 1)].rearrange("p t (c j) -> p c t j", j=4)
+            if on_vector:
+                nc.vector.tensor_scalar(dst, src, W2, 0.0, ALU.mult, ALU.add)
+            else:
+                nc.scalar.activation(dst, src, ACT.Copy, scale=W2)
+
+        def quant_z(b, u):
+            nc.vector.quantize_mx(z_w[b][u][:].bitcast(FP8X4), z_sc[b][u][:], z_bf[b][u][:])
+
+        def down(b, u):
+            for n in range(4):
+                rows = slice(P * n, P * (n + 1))
+                nc.tensor.matmul_mx(
+                    bank_o[u][n // 2][:, 256 * (n % 2) : 256 * (n % 2 + 1)],
+                    lhsT=w2_w[b][:, rows].bitcast(FP8X4),
+                    lhsT_scale=w2_sc[b][:, rows],
+                    rhs=z_w[b][u][:].bitcast(FP8X4),
+                    rhs_scale=z_sc[b][u][:],
+                    start=(b == 0 and n % 2 == 0),
+                    stop=(b == 1 and n % 2 == 1),
+                )
+
+        def store(u, i):
+            if i == 0:
+                nc.scalar.copy(res[u][i][:], bank_o[u][i][:])
+            else:
+                nc.vector.tensor_copy(res[u][i][:], bank_o[u][i][:])
+            dst = out[256 * i : 256 * (i + 1), 256 * u : 256 * (u + 1)].rearrange("(n p) m -> p n m", p=P)
+            nc.sync.dma_start(dst, res[u][i][:].rearrange("p (n m) -> p n m", n=2))
+
+        order_wg_scales()
+        order_wg(0)
+        load_wg(1)
+        for t in range(4):
+            cast_wu_scalar(0, 0, t)
+        hs.append(tile("hs_last", [P, 2 * S], F32, "load2"))
+        quant_wu(0, 0, 0)
+        for u in range(2):
+            gate(0, u)
+        cast_wu_vector(1, 0, 0)
+        quant_wu(1, 0, 0)
+        for u in range(2):
+            up(0, u)
+            product(0, u)
+        cast_wu_scalar(1, 0, 2)
+        cast_wu_scalar(1, 0, 3)
+        load_w2(0)
+
+        for k in range(8):
+            if k < 7:
+                for u in range(2):
+                    gate(k + 1, u)
+                    up(k + 1, u)
+                product(k + 1, 0)
+            pick_first(k)
+            if k < 7:
+                product(k + 1, 1)
+            pick_second(k)
+            if k == 0:
+                for a in range(2):
+                    quant_wu(a, 0, 1)
+                order_wg(1)
+            if k in (0, 1):
+                for a in range(2):
+                    for t in (2 * k, 2 * k + 1):
+                        cast_wu_scalar(a, 1, t)
+            if k == 1:
+                load_w2(1)
+            if k in (1, 2):
+                for a in range(2):
+                    quant_wu(a, 1, k - 1)
+            if k in (2, 3):
+                for u in range(2):
+                    cast_w2(k - 2, u)
+            if k in (3, 4):
+                quant_w2(k - 3)
+            if k == 4:
+                for u in range(2):
+                    round_z(0, u, False)
+            if k == 5:
+                for u in range(2):
+                    quant_z(0, u)
+                    down(0, u)
+        round_z(1, 0, True)
+        round_z(1, 1, False)
+        for u in range(2):
+            quant_z(1, u)
+            down(1, u)
+            for i in range(2):
+                store(u, i)

@@ -27,21 +27,25 @@ def tile_list_gated_token_merge_kernel(tc, tab_words, tab_scales, offs, wg_words
     nc = tc.nc
     with ExitStack() as ctx:
         sb = ctx.enter_context(tc.tile_pool(name="sb", bufs=1))
+        shared = ctx.enter_context(tc.tile_pool(name="shared", bufs=1))
         ps = ctx.enter_context(tc.psum_pool(name="ps", bufs=1))
 
         def tile(name, shape, dtype, tag=None):
             return sb.tile(shape, dtype, name=name, tag=tag or name, align_bytes=64)
 
+        def placed(name, shape, dtype, kib):
+            return shared.tile(shape, dtype, name=name, align_bytes=64, offset=1024 * kib)
+
         offs_sb = tile("offs_sb", [P, S // 16], U16)
         pos1_sb = tile("pos1_sb", [P, M // 16], U16)
         pos2_sb = tile("pos2_sb", [P, M // 16], U16)
-        tab_sc = tile("tab_sc", [P, T], U8, "load3")
+        tab_sc = placed("tab_sc", [P, T], U8, 23)
         tab_w = [tile("tab_w%d" % a, [P, T], I32, "load%d" % a) for a in range(2)]
-        v_w = [tile("v_w%d" % a, [P, S], U32) for a in range(2)]
+        v_w = [placed("v_w0", [P, S], U32, 24), tile("v_w1", [P, S], U32)]
         v_sc = tile("v_sc", [P, S], U8)
         v_sc1 = tile("v_sc1", [P, S], U8)
         wg_raw = {}
-        tab_sc_rows = tile("tab_sc_rows", [P, T // 4], I32, "load2")
+        tab_sc_rows = placed("tab_sc_rows", [P, T // 4], I32, 4)
         wg_w = [tile("wg_w%d" % b, [P, 2, 256], I32) for b in range(2)]
         wg_sc_raw = tile("wg_sc_raw", [P, 2, 256], I32)
         wg_sc = tile("wg_sc", [P, 512], I32)
@@ -53,17 +57,20 @@ def tile_list_gated_token_merge_kernel(tc, tab_words, tab_scales, offs, wg_words
         w2_bf = [tile("w2_bf%d" % b, [P, 4 * N], BF16) for b in range(2)]
         w2_w = [tile("w2_w%d" % b, [P, N], U32) for b in range(2)]
         w2_sc = [tile("w2_sc%d" % b, [P, N], U8) for b in range(2)]
-        hs = [tile("hs%d" % r, [P, 2 * S], F32) for r in range(RING - 1)]
+        hs = [placed("hs0", [P, 2 * S], F32, 0), tile("hs1", [P, 2 * S], F32), placed("hs2", [P, 2 * S], F32, 8)]
         first = [tile("first%d" % r, [P, M], F32) for r in range(2)]
+        second = [tile("second%d" % r, [P, M], F32) for r in range(2)]
+        a_sb = [tile("a_sb%d" % r, [P, BANK], F32) for r in range(2)]
         z_f = [tile("z_f%d" % b, [P, 4, M], F32) for b in range(2)]
         z_bf = [[tile("z_bf%d%d" % (b, u), [P, 2 * M], BF16) for u in range(2)] for b in range(2)]
         z_w = [[tile("z_w%d%d" % (b, u), [P, M // 2], U32) for u in range(2)] for b in range(2)]
         z_sc = [[tile("z_sc%d%d" % (b, u), [P, M // 2], U8) for u in range(2)] for b in range(2)]
         res = [[tile("res%d%d" % (u, i), [P, BANK], F32) for i in range(2)] for u in range(2)]
         warm = tile("warm", [P, 16], F32)
-        bank_a = [ps.tile([P, BANK], F32, name="bank_a%d" % u) for u in range(2)]
-        bank_b = [ps.tile([P, BANK], F32, name="bank_b%d" % u) for u in range(2)]
-        bank_o = [[ps.tile([P, BANK], F32, name="bank_o%d%d" % (u, i)) for i in range(2)] for u in range(2)]
+        bank_a, bank_b, bank_o = {}, {}, {}
+
+        def bank(name, tag):
+            return ps.tile([P, BANK], F32, name=name, tag=tag)
 
         nc.vector.memset(tab_sc[:].bitcast(I32), 0)
         nc.sync.dma_start(offs_sb[:], offs)
@@ -81,12 +88,18 @@ def tile_list_gated_token_merge_kernel(tc, tab_words, tab_scales, offs, wg_words
             nc.sync.dma_start(wg_raw[b][:], wg_words[:, :, 1024 * b : 1024 * (b + 1)].bitcast(I32).rearrange("a p n -> p a n"))
 
         def load_wu(a, b):
-            wu_raw[a][b] = tile("wu_raw%d%d" % (a, b), [P, 4, PASS], F32, "load%d" % (2 + a - 2 * b))
+            if b == 0:
+                wu_raw[a][b] = placed("wu_raw%d0" % a, [P, 4, PASS], F32, (4, 16)[a])
+            else:
+                wu_raw[a][b] = tile("wu_raw%d1" % a, [P, 4, PASS], F32, "load%d" % a)
             rows = wu[PASS * a : PASS * (a + 1), PASS * b : PASS * (b + 1)]
             nc.sync.dma_start(wu_raw[a][b][:], rows.rearrange("(p i) c -> p i c", i=4))
 
         def load_w2(b):
-            w2_raw[b] = tile("w2_raw%d" % b, [P, 4, N], F32, ("load3", "load0")[b])
+            if b == 0:
+                w2_raw[b] = placed("w2_raw0", [P, 4, N], F32, 16)
+            else:
+                w2_raw[b] = tile("w2_raw1", [P, 4, N], F32, "load0")
             rows = w2[PASS * b : PASS * (b + 1), :].rearrange("(g t j) n -> t g j n", t=4, j=8)
             for t in range(4):
                 nc.sync.dma_start(w2_raw[b][:, t, :], rows[t])
@@ -129,10 +142,16 @@ def tile_list_gated_token_merge_kernel(tc, tab_words, tab_scales, offs, wg_words
                 wu_raw[a][b][:].rearrange("p i (g t h j) -> p t g h i j", t=4, h=2, j=4)[:, t],
             )
 
-        def cast_wu_vector(a, b, u):
+        def cast_wu_vector(a, b, t):
             nc.vector.tensor_copy(
-                wu_bf[a][b][u][:].rearrange("p (t g j i) -> p t g j i", t=2, j=8, i=4),
-                wu_raw[a][b][:].rearrange("p i (g t j) -> p t g j i", t=4, j=8)[:, 2 * u : 2 * u + 2],
+                wu_bf[a][b][t // 2][:, 512 * (t % 2) : 512 * (t % 2 + 1)].rearrange("p (g j i) -> p g j i", j=8, i=4),
+                wu_raw[a][b][:].rearrange("p i (g t j) -> p t g j i", t=4, j=8)[:, t],
+            )
+
+        def quant_wu_slice(a, b, t):
+            cols = slice(P * t, P * (t + 1))
+            nc.vector.quantize_mx(
+                wu_w[a][b][:, cols].bitcast(FP8X4), wu_sc[a][b][:, cols], wu_bf[a][b][t // 2][:, 512 * (t % 2) : 512 * (t % 2 + 1)]
             )
 
         def quant_wu(a, b, u):
@@ -151,6 +170,7 @@ def tile_list_gated_token_merge_kernel(tc, tab_words, tab_scales, offs, wg_words
         def gate(k, u):
             b, t = divmod(k, 4)
             cols = slice(BANK * u, BANK * (u + 1))
+            bank_b[u] = bank("bank_b%d%d" % (k, u), "b%d%d" % (k % 2, u))
             for a in range(2):
                 x = 2 * a + b
                 nc.tensor.matmul_mx(
@@ -168,6 +188,7 @@ def tile_list_gated_token_merge_kernel(tc, tab_words, tab_scales, offs, wg_words
             b, t = divmod(k, 4)
             cols = slice(BANK * u, BANK * (u + 1))
             rows = slice(P * t, P * (t + 1))
+            bank_a[u] = bank("bank_a%d%d" % (k, u), "a%d%d" % (k % 2, u))
             for a in range(2):
                 nc.tensor.matmul_mx(
                     bank_a[u][:],
@@ -186,6 +207,15 @@ def tile_list_gated_token_merge_kernel(tc, tab_words, tab_scales, offs, wg_words
                 hs[(k - 1) % RING][:, S + BANK * u : S + BANK * (u + 1)],
                 ALU.mult,
             )
+
+        def product_aside(k):
+            nc.scalar.copy(a_sb[k % 2][:], bank_a[0][:])
+            nc.gpsimd.tensor_tensor(hs[k % RING][:, 0:BANK], a_sb[k % 2][:], hs[(k - 1) % RING][:, S : S + BANK], ALU.mult)
+
+        def pick_second_aside(k):
+            b, t = divmod(k, 4)
+            nc.vector.tensor_copy(second[k % 2][:], hs[k % RING][:].indirect(pos2_sb[:]))
+            nc.gpsimd.tensor_tensor(z_f[b][:, t, :], second[k % 2][:], first[k % 2][:], ALU.add)
 
         def pick_first(k):
             nc.vector.tensor_scalar(first[k % 2][:], hs[k % RING][:].indirect(pos1_sb[:]), W1 / W2, 0.0, ALU.mult, ALU.add)
@@ -206,6 +236,8 @@ def tile_list_gated_token_merge_kernel(tc, tab_words, tab_scales, offs, wg_words
             nc.vector.quantize_mx(z_w[b][u][:].bitcast(FP8X4), z_sc[b][u][:], z_bf[b][u][:])
 
         def down(b, u):
+            if b == 0:
+                bank_o[u] = [bank("bank_o%d%d" % (u, i), "%s0%d" % ("ba"[u], i)) for i in range(2)]
             for n in range(4):
                 rows = slice(P * n, P * (n + 1))
                 nc.tensor.matmul_mx(
@@ -231,14 +263,16 @@ def tile_list_gated_token_merge_kernel(tc, tab_words, tab_scales, offs, wg_words
         load_wg(1)
         for t in range(4):
             cast_wu_scalar(0, 0, t)
-        hs.append(tile("hs_last", [P, 2 * S], F32, "load2"))
         quant_wu(0, 0, 0)
         for u in range(2):
             gate(0, u)
         cast_wu_vector(1, 0, 0)
-        quant_wu(1, 0, 0)
+        quant_wu_slice(1, 0, 0)
         for u in range(2):
             up(0, u)
+        cast_wu_vector(1, 0, 1)
+        quant_wu_slice(1, 0, 1)
+        for u in range(2):
             product(0, u)
         cast_wu_scalar(1, 0, 2)
         cast_wu_scalar(1, 0, 3)
@@ -246,39 +280,41 @@ def tile_list_gated_token_merge_kernel(tc, tab_words, tab_scales, offs, wg_words
 
         for k in range(8):
             if k < 7:
-                for u in range(2):
-                    gate(k + 1, u)
-                    up(k + 1, u)
-                product(k + 1, 0)
+                gate(k + 1, 0)
+                up(k + 1, 0)
+                product_aside(k + 1)
+                gate(k + 1, 1)
+                up(k + 1, 1)
             pick_first(k)
             if k < 7:
                 product(k + 1, 1)
-            pick_second(k)
+                pick_second_aside(k)
+            else:
+                for u in range(2):
+                    quant_z(0, u)
+                    down(0, u)
+                quant_w2(1)
+                pick_second(k)
             if k == 0:
                 for a in range(2):
                     quant_wu(a, 0, 1)
                 order_wg(1)
-            if k in (0, 1):
+            if k < 4:
                 for a in range(2):
-                    for t in (2 * k, 2 * k + 1):
-                        cast_wu_scalar(a, 1, t)
-            if k == 1:
+                    cast_wu_scalar(a, 1, k)
+            if k == 3:
                 load_w2(1)
-            if k in (1, 2):
+            if k in (2, 4):
                 for a in range(2):
-                    quant_wu(a, 1, k - 1)
-            if k in (2, 3):
-                for u in range(2):
-                    cast_w2(k - 2, u)
-            if k in (3, 4):
-                quant_w2(k - 3)
-            if k == 4:
+                    quant_wu(a, 1, k // 2 - 1)
+            if k in (4, 5):
+                cast_w2(0, k - 4)
+            if k == 6:
+                quant_w2(0)
                 for u in range(2):
                     round_z(0, u, False)
-            if k == 5:
                 for u in range(2):
-                    quant_z(0, u)
-                    down(0, u)
+                    cast_w2(1, u)
         round_z(1, 0, True)
         round_z(1, 1, False)
         for u in range(2):

@@ -41,30 +41,35 @@ def tile_list_gated_token_merge_kernel(tc, tab_words, tab_scales, offs, wg_words
         pos2_sb = tile("pos2_sb", [P, M // 16], U16)
         tab_sc = placed("tab_sc", [P, T], U8, 23)
         tab_w = [tile("tab_w%d" % a, [P, T], I32, "load%d" % a) for a in range(2)]
-        v_w = [placed("v_w0", [P, S], U32, 24), tile("v_w1", [P, S], U32)]
+        v_w = [placed("v_w0", [P, S], U32, 24), placed("v_w1", [P, S], U32, 28)]
         v_sc = tile("v_sc", [P, S], U8)
         v_sc1 = tile("v_sc1", [P, S], U8)
         wg_raw = {}
         tab_sc_rows = placed("tab_sc_rows", [P, T // 4], I32, 4)
         wg_w = [tile("wg_w%d" % b, [P, 2, 256], I32) for b in range(2)]
-        wg_sc_raw = tile("wg_sc_raw", [P, 2, 256], I32)
+        wg_sc_raw = placed("wg_sc_raw", [P, 2, 256], I32, 28)
         wg_sc = tile("wg_sc", [P, 512], I32)
         wu_raw = [{}, {}]
-        wu_bf = [[[tile("wu_bf%d%d%d" % (a, b, u), [P, 1024], BF16) for u in range(2)] for b in range(2)] for a in range(2)]
-        wu_w = [[tile("wu_w%d%d" % (a, b), [P, PASS], U32) for b in range(2)] for a in range(2)]
-        wu_sc = [[tile("wu_sc%d%d" % (a, b), [P, PASS], U8) for b in range(2)] for a in range(2)]
+        wu_bf = {
+            (0, 0): [tile("wu_bf000", [P, 1024], BF16), placed("wu_bf001", [P, 1024], BF16, 37)],
+            (0, 1): [tile("wu_bf010", [P, 1024], BF16), placed("wu_bf011", [P, 1024], BF16, 36)],
+            (1, 0): tile("wu_bf10", [P, 2048], BF16),
+            (1, 1): tile("wu_bf11", [P, 2048], BF16),
+        }
+        wu_w = {(b, u): tile("wu_w%d%d" % (b, u), [P, 512], U32) for b in range(2) for u in range(2)}
+        wu_sc = {(b, u): tile("wu_sc%d%d" % (b, u), [P, 512], U8) for b in range(2) for u in range(2)}
         w2_raw = {}
         w2_bf = [tile("w2_bf%d" % b, [P, 4 * N], BF16) for b in range(2)]
         w2_w = [tile("w2_w%d" % b, [P, N], U32) for b in range(2)]
         w2_sc = [tile("w2_sc%d" % b, [P, N], U8) for b in range(2)]
         hs = [placed("hs0", [P, 2 * S], F32, 0), tile("hs1", [P, 2 * S], F32), placed("hs2", [P, 2 * S], F32, 8)]
-        first = [tile("first%d" % r, [P, M], F32) for r in range(2)]
+        ring = [tile("first%d" % r, [P, M], F32) for r in range(2)]
+        first = [ring[k % 2] for k in range(7)] + [placed("first_last", [P, M], F32, 32)]
         second = [tile("second%d" % r, [P, M], F32) for r in range(2)]
-        a_sb = [tile("a_sb%d" % r, [P, BANK], F32) for r in range(2)]
         z_f = [tile("z_f%d" % b, [P, 4, M], F32) for b in range(2)]
-        z_bf = [[tile("z_bf%d%d" % (b, u), [P, 2 * M], BF16) for u in range(2)] for b in range(2)]
-        z_w = [[tile("z_w%d%d" % (b, u), [P, M // 2], U32) for u in range(2)] for b in range(2)]
-        z_sc = [[tile("z_sc%d%d" % (b, u), [P, M // 2], U8) for u in range(2)] for b in range(2)]
+        z_bf = [placed("z_bf0", [P, 4 * M], BF16, 32), [tile("z_bf1%d" % u, [P, 2 * M], BF16) for u in range(2)]]
+        z_w = [placed("z_w0", [P, M], U32, 0), tile("z_w1", [P, M], U32)]
+        z_sc = [tile("z_sc%d" % b, [P, M], U8) for b in range(2)]
         res = [[tile("res%d%d" % (u, i), [P, BANK], F32) for i in range(2)] for u in range(2)]
         warm = tile("warm", [P, 16], F32)
         bank_a, bank_b, bank_o = {}, {}, {}
@@ -96,10 +101,7 @@ def tile_list_gated_token_merge_kernel(tc, tab_words, tab_scales, offs, wg_words
             nc.sync.dma_start(wu_raw[a][b][:], rows.rearrange("(p i) c -> p i c", i=4))
 
         def load_w2(b):
-            if b == 0:
-                w2_raw[b] = placed("w2_raw0", [P, 4, N], F32, 16)
-            else:
-                w2_raw[b] = tile("w2_raw1", [P, 4, N], F32, "load0")
+            w2_raw[b] = placed("w2_raw%d" % b, [P, 4, N], F32, (38, 16)[b])
             rows = w2[PASS * b : PASS * (b + 1), :].rearrange("(g t j) n -> t g j n", t=4, j=8)
             for t in range(4):
                 nc.sync.dma_start(w2_raw[b][:, t, :], rows[t])
@@ -119,9 +121,8 @@ def tile_list_gated_token_merge_kernel(tc, tab_words, tab_scales, offs, wg_words
         nc.vector.tensor_copy(v_sc[:], tab_sc[:].indirect(offs_sb[:]))
         nc.scalar.dma_start(v_sc1[0:112, :].bitcast(I32), v_sc[4:116, :].bitcast(I32))
         load_wu(1, 0)
-        for a in range(2):
-            nc.vector.tensor_copy(v_w[a][:], tab_w[a][:].bitcast(U32).indirect(offs_sb[:]))
-            load_wu(a, 1)
+        nc.vector.tensor_copy(v_w[0][:], tab_w[0][:].bitcast(U32).indirect(offs_sb[:]))
+        load_wu(0, 1)
 
         def order_wg(b):
             nc.vector.tensor_copy(
@@ -135,28 +136,42 @@ def tile_list_gated_token_merge_kernel(tc, tab_words, tab_scales, offs, wg_words
                 wg_sc_raw[:].rearrange("p a (b g t w) -> p (a b) t g w", b=2, t=4, w=2),
             )
 
+        def rounded_wu(a, b, t):
+            u, e = divmod(t, 2)
+            if b == 0:
+                return wu_bf[b, u][a][:, 512 * e : 512 * (e + 1)]
+            return wu_bf[b, u][:, 1024 * a + 512 * e : 1024 * a + 512 * (e + 1)]
+
+        def wu_cols(a, t):
+            return slice(256 * a + P * (t % 2), 256 * a + P * (t % 2 + 1))
+
         def cast_wu_scalar(a, b, t):
-            dst = wu_bf[a][b][t // 2][:, 512 * (t % 2) : 512 * (t % 2 + 1)]
             nc.scalar.copy(
-                dst.rearrange("p (g h j i) -> p g h i j", h=2, j=4, i=4),
+                rounded_wu(a, b, t).rearrange("p (g h j i) -> p g h i j", h=2, j=4, i=4),
                 wu_raw[a][b][:].rearrange("p i (g t h j) -> p t g h i j", t=4, h=2, j=4)[:, t],
             )
 
         def cast_wu_vector(a, b, t):
             nc.vector.tensor_copy(
-                wu_bf[a][b][t // 2][:, 512 * (t % 2) : 512 * (t % 2 + 1)].rearrange("p (g j i) -> p g j i", j=8, i=4),
+                rounded_wu(a, b, t).rearrange("p (g j i) -> p g j i", j=8, i=4),
                 wu_raw[a][b][:].rearrange("p i (g t j) -> p t g j i", t=4, j=8)[:, t],
             )
 
-        def quant_wu_slice(a, b, t):
-            cols = slice(P * t, P * (t + 1))
-            nc.vector.quantize_mx(
-                wu_w[a][b][:, cols].bitcast(FP8X4), wu_sc[a][b][:, cols], wu_bf[a][b][t // 2][:, 512 * (t % 2) : 512 * (t % 2 + 1)]
+        def cast_wu_gpsimd(a, b, t):
+            nc.gpsimd.tensor_scalar(
+                rounded_wu(a, b, t).rearrange("p (g j i) -> p g j i", j=8, i=4),
+                wu_raw[a][b][:].rearrange("p i (g t j) -> p t g j i", t=4, j=8)[:, t],
+                1.0,
+                0.0,
+                ALU.mult,
+                ALU.add,
             )
 
-        def quant_wu(a, b, u):
-            cols = slice(256 * u, 256 * (u + 1))
-            nc.vector.quantize_mx(wu_w[a][b][:, cols].bitcast(FP8X4), wu_sc[a][b][:, cols], wu_bf[a][b][u][:])
+        def quant_wu_first(u, cols, rounded):
+            nc.vector.quantize_mx(wu_w[0, u][:, cols].bitcast(FP8X4), wu_sc[0, u][:, cols], rounded)
+
+        def quant_wu(b, u):
+            nc.vector.quantize_mx(wu_w[b, u][:].bitcast(FP8X4), wu_sc[b, u][:], wu_bf[b, u][:])
 
         def cast_w2(b, u):
             nc.scalar.copy(
@@ -167,73 +182,77 @@ def tile_list_gated_token_merge_kernel(tc, tab_words, tab_scales, offs, wg_words
         def quant_w2(b):
             nc.vector.quantize_mx(w2_w[b][:].bitcast(FP8X4), w2_sc[b][:], w2_bf[b][:])
 
-        def gate(k, u):
+        def gate_pass(k, u, a):
             b, t = divmod(k, 4)
             cols = slice(BANK * u, BANK * (u + 1))
-            bank_b[u] = bank("bank_b%d%d" % (k, u), "b%d%d" % (k % 2, u))
-            for a in range(2):
-                x = 2 * a + b
-                nc.tensor.matmul_mx(
-                    bank_b[u][:],
-                    lhsT=wg_w[b][:, a, 64 * t : 64 * (t + 1)].bitcast(FP4X4),
-                    lhsT_scale=wg_sc[:, 128 * x + 32 * t : 128 * x + 32 * (t + 1)].bitcast(U8),
-                    rhs=v_w[a][:, cols].bitcast(FP8X4),
-                    rhs_scale=(v_sc, v_sc1)[a][:, cols],
-                    start=(a == 0),
-                    stop=(a == 1),
-                )
-            nc.scalar.activation(hs[(k - 1) % RING][:, S + BANK * u : S + BANK * (u + 1)], bank_b[u][:], ACT.Silu)
+            if a == 0:
+                bank_b[k, u] = bank("bank_b%d%d" % (k, u), "b%d%d" % (k % 2, u))
+            x = 2 * a + b
+            nc.tensor.matmul_mx(
+                bank_b[k, u][:],
+                lhsT=wg_w[b][:, a, 64 * t : 64 * (t + 1)].bitcast(FP4X4),
+                lhsT_scale=wg_sc[:, 128 * x + 32 * t : 128 * x + 32 * (t + 1)].bitcast(U8),
+                rhs=v_w[a][:, cols].bitcast(FP8X4),
+                rhs_scale=(v_sc, v_sc1)[a][:, cols],
+                start=(a == 0),
+                stop=(a == 1),
+            )
+            if a == 1:
+                nc.scalar.activation(hs[(k - 1) % RING][:, S + BANK * u : S + BANK * (u + 1)], bank_b[k, u][:], ACT.Silu)
 
-        def up(k, u):
+        def up_pass(k, u, a):
             b, t = divmod(k, 4)
             cols = slice(BANK * u, BANK * (u + 1))
-            rows = slice(P * t, P * (t + 1))
-            bank_a[u] = bank("bank_a%d%d" % (k, u), "a%d%d" % (k % 2, u))
-            for a in range(2):
-                nc.tensor.matmul_mx(
-                    bank_a[u][:],
-                    lhsT=wu_w[a][b][:, rows].bitcast(FP8X4),
-                    lhsT_scale=wu_sc[a][b][:, rows],
-                    rhs=v_w[a][:, cols].bitcast(FP8X4),
-                    rhs_scale=v_sc[4 * a : P, cols],
-                    start=(a == 0),
-                    stop=(a == 1),
-                )
+            if a == 0:
+                bank_a[k, u] = bank("bank_a%d%d" % (k, u), "a%d%d" % (k % 2, u))
+            nc.tensor.matmul_mx(
+                bank_a[k, u][:],
+                lhsT=wu_w[b, t // 2][:, wu_cols(a, t)].bitcast(FP8X4),
+                lhsT_scale=wu_sc[b, t // 2][:, wu_cols(a, t)],
+                rhs=v_w[a][:, cols].bitcast(FP8X4),
+                rhs_scale=v_sc[4 * a : P, cols],
+                start=(a == 0),
+                stop=(a == 1),
+            )
 
         def product(k, u):
             nc.vector.tensor_tensor(
                 hs[k % RING][:, BANK * u : BANK * (u + 1)],
-                bank_a[u][:],
+                bank_a[k, u][:],
                 hs[(k - 1) % RING][:, S + BANK * u : S + BANK * (u + 1)],
                 ALU.mult,
             )
 
         def product_aside(k):
-            nc.scalar.copy(a_sb[k % 2][:], bank_a[0][:])
-            nc.gpsimd.tensor_tensor(hs[k % RING][:, 0:BANK], a_sb[k % 2][:], hs[(k - 1) % RING][:, S : S + BANK], ALU.mult)
+            parked = z_f[(k - 1) // 4][:, (k - 1) % 4, :]
+            nc.scalar.copy(parked, bank_a[k, 0][:])
+            nc.gpsimd.tensor_tensor(hs[k % RING][:, 0:BANK], parked, hs[(k - 1) % RING][:, S : S + BANK], ALU.mult)
 
         def pick_second_aside(k):
             b, t = divmod(k, 4)
             nc.vector.tensor_copy(second[k % 2][:], hs[k % RING][:].indirect(pos2_sb[:]))
-            nc.gpsimd.tensor_tensor(z_f[b][:, t, :], second[k % 2][:], first[k % 2][:], ALU.add)
+            nc.gpsimd.tensor_tensor(z_f[b][:, t, :], second[k % 2][:], first[k][:], ALU.add)
 
         def pick_first(k):
-            nc.vector.tensor_scalar(first[k % 2][:], hs[k % RING][:].indirect(pos1_sb[:]), W1 / W2, 0.0, ALU.mult, ALU.add)
+            nc.vector.tensor_scalar(first[k][:], hs[k % RING][:].indirect(pos1_sb[:]), W1 / W2, 0.0, ALU.mult, ALU.add)
 
-        def pick_second(k):
+        def pick_second(k, u):
             b, t = divmod(k, 4)
-            nc.vector.tensor_tensor(z_f[b][:, t, :], hs[k % RING][:].indirect(pos2_sb[:]), first[k % 2][:], ALU.add)
+            cols = slice(256 * u, 256 * (u + 1))
+            picked = hs[k % RING][:].indirect(pos2_sb[:, 16 * u : 16 * (u + 1)])
+            nc.vector.tensor_tensor(z_f[b][:, t, cols], picked, first[k][:, cols], ALU.add)
 
         def round_z(b, u, on_vector):
-            dst = z_bf[b][u][:].rearrange("p (c j t) -> p c t j", j=4, t=4)
+            rounded = z_bf[0][:, 1024 * u : 1024 * (u + 1)] if b == 0 else z_bf[1][u][:]
+            dst = rounded.rearrange("p (c j t) -> p c t j", j=4, t=4)
             src = z_f[b][:, :, 256 * u : 256 * (u + 1)].rearrange("p t (c j) -> p c t j", j=4)
             if on_vector:
                 nc.vector.tensor_scalar(dst, src, W2, 0.0, ALU.mult, ALU.add)
             else:
                 nc.scalar.activation(dst, src, ACT.Copy, scale=W2)
 
-        def quant_z(b, u):
-            nc.vector.quantize_mx(z_w[b][u][:].bitcast(FP8X4), z_sc[b][u][:], z_bf[b][u][:])
+        def quant_z(b, cols, rounded):
+            nc.vector.quantize_mx(z_w[b][:, cols].bitcast(FP8X4), z_sc[b][:, cols], rounded)
 
         def down(b, u):
             if b == 0:
@@ -244,8 +263,8 @@ def tile_list_gated_token_merge_kernel(tc, tab_words, tab_scales, offs, wg_words
                     bank_o[u][n // 2][:, 256 * (n % 2) : 256 * (n % 2 + 1)],
                     lhsT=w2_w[b][:, rows].bitcast(FP8X4),
                     lhsT_scale=w2_sc[b][:, rows],
-                    rhs=z_w[b][u][:].bitcast(FP8X4),
-                    rhs_scale=z_sc[b][u][:],
+                    rhs=z_w[b][:, 256 * u : 256 * (u + 1)].bitcast(FP8X4),
+                    rhs_scale=z_sc[b][:, 256 * u : 256 * (u + 1)],
                     start=(b == 0 and n % 2 == 0),
                     stop=(b == 1 and n % 2 == 1),
                 )
@@ -258,67 +277,83 @@ def tile_list_gated_token_merge_kernel(tc, tab_words, tab_scales, offs, wg_words
             dst = out[256 * i : 256 * (i + 1), 256 * u : 256 * (u + 1)].rearrange("(n p) m -> p n m", p=P)
             nc.sync.dma_start(dst, res[u][i][:].rearrange("p (n m) -> p n m", n=2))
 
-        order_wg_scales()
         order_wg(0)
+        order_wg_scales()
         load_wg(1)
+        for k in range(2):
+            for u in range(2):
+                gate_pass(k, u, 0)
         for t in range(4):
             cast_wu_scalar(0, 0, t)
-        quant_wu(0, 0, 0)
         for u in range(2):
-            gate(0, u)
-        cast_wu_vector(1, 0, 0)
-        quant_wu_slice(1, 0, 0)
+            nc.vector.tensor_copy(
+                v_w[1][:, BANK * u : BANK * (u + 1)], tab_w[1][:].bitcast(U32).indirect(offs_sb[:, 32 * u : 32 * (u + 1)])
+            )
+            gate_pass(0, u, 1)
+        load_wu(1, 1)
+        quant_wu_first(0, slice(0, 256), wu_bf[0, 0][0][:])
         for u in range(2):
-            up(0, u)
-        cast_wu_vector(1, 0, 1)
-        quant_wu_slice(1, 0, 1)
+            up_pass(0, u, 0)
+        for u in range(2):
+            gate_pass(1, u, 1)
+        for t in range(2):
+            cast_wu_vector(1, 0, t)
+            quant_wu_first(0, wu_cols(1, t), rounded_wu(1, 0, t))
+            if t == 0:
+                for u in range(2):
+                    up_pass(0, u, 1)
+        quant_wu_first(1, slice(0, 256), wu_bf[0, 1][0][:])
+        load_w2(0)
+        for t in (2, 3):
+            cast_wu_gpsimd(1, 0, t)
+        load_w2(1)
         for u in range(2):
             product(0, u)
-        cast_wu_scalar(1, 0, 2)
-        cast_wu_scalar(1, 0, 3)
-        load_w2(0)
 
         for k in range(8):
             if k < 7:
-                gate(k + 1, 0)
-                up(k + 1, 0)
+                for u in range(2):
+                    for a in range(2):
+                        if k > 0:
+                            gate_pass(k + 1, u, a)
+                for u in (1, 0):
+                    for a in range(2):
+                        up_pass(k + 1, u, a)
+                if 1 <= k <= 3:
+                    for a in range(2):
+                        cast_wu_scalar(a, 1, k)
+                if k in (4, 5):
+                    cast_w2(k - 4, 0)
                 product_aside(k + 1)
-                gate(k + 1, 1)
-                up(k + 1, 1)
+                if k == 0:
+                    for a in range(2):
+                        cast_wu_scalar(a, 1, k)
+                if k in (4, 5):
+                    cast_w2(k - 4, 1)
+                if k == 6:
+                    for u in range(2):
+                        round_z(0, u, False)
+            if k == 7:
+                quant_z(0, slice(0, M), z_bf[0][:])
+                for u in range(2):
+                    down(0, u)
             pick_first(k)
             if k < 7:
                 product(k + 1, 1)
                 pick_second_aside(k)
-            else:
-                for u in range(2):
-                    quant_z(0, u)
-                    down(0, u)
-                quant_w2(1)
-                pick_second(k)
             if k == 0:
-                for a in range(2):
-                    quant_wu(a, 0, 1)
+                quant_wu_first(1, slice(256, 512), wu_bf[0, 1][1][:])
                 order_wg(1)
-            if k < 4:
-                for a in range(2):
-                    cast_wu_scalar(a, 1, k)
-            if k == 3:
-                load_w2(1)
-            if k in (2, 4):
-                for a in range(2):
-                    quant_wu(a, 1, k // 2 - 1)
-            if k in (4, 5):
-                cast_w2(0, k - 4)
-            if k == 6:
-                quant_w2(0)
-                for u in range(2):
-                    round_z(0, u, False)
-                for u in range(2):
-                    cast_w2(1, u)
-        round_z(1, 0, True)
-        round_z(1, 1, False)
+            if k in (1, 3):
+                quant_wu(1, k // 2)
+            if k in (5, 6):
+                quant_w2(k - 5)
+        pick_second(7, 0)
+        round_z(1, 0, False)
+        pick_second(7, 1)
+        round_z(1, 1, True)
         for u in range(2):
-            quant_z(1, u)
+            quant_z(1, slice(256 * u, 256 * (u + 1)), z_bf[1][u][:])
             down(1, u)
             for i in range(2):
                 store(u, i)

@@ -20,7 +20,6 @@ P = 128
 PASS = 512
 BANK = 512
 W1, W2 = 0.7, 0.3
-RING = 3
 
 
 def tile_list_gated_token_merge_kernel(tc, tab_words, tab_scales, offs, wg_words, wg_scales, wu, w2, pos1, pos2, out):
@@ -39,36 +38,53 @@ def tile_list_gated_token_merge_kernel(tc, tab_words, tab_scales, offs, wg_words
         offs_sb = tile("offs_sb", [P, S // 16], U16)
         pos1_sb = tile("pos1_sb", [P, M // 16], U16)
         pos2_sb = tile("pos2_sb", [P, M // 16], U16)
-        tab_sc = placed("tab_sc", [P, T], U8, 23)
-        tab_w = [tile("tab_w%d" % a, [P, T], I32, "load%d" % a) for a in range(2)]
-        v_w = [placed("v_w0", [P, S], U32, 24), placed("v_w1", [P, S], U32, 28)]
+        tab_sc = placed("tab_sc", [P, T], U8, 8)
+        tab_w = [placed("tab_w0", [P, T], I32, 41), tile("tab_w1", [P, T], I32, "load1")]
+        v_w = [
+            [placed("v_w00", [P, BANK], U32, 9), tile("v_w01", [P, BANK], U32)],
+            [tile("v_w1%d" % u, [P, BANK], U32) for u in range(2)],
+        ]
         v_sc = tile("v_sc", [P, S], U8)
         v_sc1 = tile("v_sc1", [P, S], U8)
         wg_raw = {}
-        tab_sc_rows = placed("tab_sc_rows", [P, T // 4], I32, 4)
-        wg_w = [tile("wg_w%d" % b, [P, 2, 256], I32) for b in range(2)]
-        wg_sc_raw = placed("wg_sc_raw", [P, 2, 256], I32, 28)
-        wg_sc = tile("wg_sc", [P, 512], I32)
+        tab_sc_rows = placed("tab_sc_rows", [P, T // 4], I32, 16)
+        wg_w1 = tile("wg_w1", [P, 2, 256], I32)
+        wg_sc_raw = tile("wg_sc_raw", [P, 2, 256], I32)
+        wg_sc1 = placed("wg_sc1", [P, 2, 128], I32, 13)
         wu_raw = [{}, {}]
+        wu_halves = placed("wu_halves", [P, 2048], F32, 1)
+        wu_half = [wu_halves[:, 1024 * u : 1024 * (u + 1)].rearrange("p (i c) -> p i c", i=4) for u in range(2)]
         wu_bf = {
-            (0, 0): [tile("wu_bf000", [P, 1024], BF16), placed("wu_bf001", [P, 1024], BF16, 37)],
-            (0, 1): [tile("wu_bf010", [P, 1024], BF16), placed("wu_bf011", [P, 1024], BF16, 36)],
-            (1, 0): tile("wu_bf10", [P, 2048], BF16),
-            (1, 1): tile("wu_bf11", [P, 2048], BF16),
+            (0, 0): tile("wu_bf00", [P, 1024], BF16),
+            (0, 1): placed("wu_bf01", [P, 2048], BF16, 52),
+            (1, 0): placed("wu_bf10", [P, 2048], BF16, 56),
+            (1, 1): placed("wu_bf11", [P, 2048], BF16, 60),
         }
-        wu_w = {(b, u): tile("wu_w%d%d" % (b, u), [P, 512], U32) for b in range(2) for u in range(2)}
+        wu_bf_late = placed("wu_bf_late", [P, 512], BF16, 13)
+        wu_w = {
+            (0, 0): tile("wu_w00", [P, 512], U32),
+            (0, 1): tile("wu_w01", [P, 512], U32),
+            (1, 0): placed("wu_w10", [P, 512], U32, 24 + 2 * 1),
+            (1, 1): placed("wu_w11", [P, 512], U32, 24 + 2 * 3),
+        }
         wu_sc = {(b, u): tile("wu_sc%d%d" % (b, u), [P, 512], U8) for b in range(2) for u in range(2)}
         w2_raw = {}
-        w2_bf = [tile("w2_bf%d" % b, [P, 4 * N], BF16) for b in range(2)]
-        w2_w = [tile("w2_w%d" % b, [P, N], U32) for b in range(2)]
+        w2_bf = [placed("w2_bf%d" % b, [P, 4 * N], BF16, 64 + 4 * b) for b in range(2)]
+        w2_w = [placed("w2_w%d" % b, [P, N], U32, 24 + 2 * (5 + b)) for b in range(2)]
         w2_sc = [tile("w2_sc%d" % b, [P, N], U8) for b in range(2)]
-        hs = [placed("hs0", [P, 2 * S], F32, 0), tile("hs1", [P, 2 * S], F32), placed("hs2", [P, 2 * S], F32, 8)]
-        ring = [tile("first%d" % r, [P, M], F32) for r in range(2)]
-        first = [ring[k % 2] for k in range(7)] + [placed("first_last", [P, M], F32, 32)]
-        second = [tile("second%d" % r, [P, M], F32) for r in range(2)]
-        z_f = [tile("z_f%d" % b, [P, 4, M], F32) for b in range(2)]
-        z_bf = [placed("z_bf0", [P, 4 * M], BF16, 32), [tile("z_bf1%d" % u, [P, 2 * M], BF16) for u in range(2)]]
-        z_w = [placed("z_w0", [P, M], U32, 0), tile("z_w1", [P, M], U32)]
+        hs = [placed("hs%d" % k, [P, 2 * S], F32, 72 + 8 * k) for k in range(8)]
+        ring = [tile("first%d" % k, [P, M], F32) for k in (3, 5)]
+        first_at = {0: 52, 2: 56, 4: 60, 6: 64}
+        first = [placed("first_at%d" % k, [P, M], F32, first_at[k]) if k in first_at else ring[k // 2 % 2] for k in range(8)]
+        second = [hs[k + 1][:, S + BANK : 2 * S] for k in range(7)]
+        silu = [[hs[0][:, S + BANK : 2 * S], hs[0][:, S : S + BANK]]]
+        for k in range(1, 8):
+            silu.append([placed("silu%d" % k, [P, BANK], F32, 24 + 2 * k)[:], hs[k][:, S : S + BANK]])
+        z_rows = [tile("z_rows%d" % k, [P, M], F32) for k in range(4)]
+        z_late = tile("z_late", [P, 5 * M], F32)
+        z_f = [tile("z_f0", [P, 4, M], F32)[:], z_late[:, 0 : 4 * M].rearrange("p (t m) -> p t m", t=4)]
+        z_bf = [z_late[:, 3 * M : 5 * M].bitcast(BF16), [tile("z_bf1%d" % u, [P, 2 * M], BF16) for u in range(2)]]
+        z_w = [tile("z_w0", [P, M], U32), tile("z_w1", [P, M], U32)]
         z_sc = [tile("z_sc%d" % b, [P, M], U8) for b in range(2)]
         res = [[tile("res%d%d" % (u, i), [P, BANK], F32) for i in range(2)] for u in range(2)]
         warm = tile("warm", [P, 16], F32)
@@ -77,90 +93,114 @@ def tile_list_gated_token_merge_kernel(tc, tab_words, tab_scales, offs, wg_words
         def bank(name, tag):
             return ps.tile([P, BANK], F32, name=name, tag=tag)
 
+        nc.vector.memset(wg_sc_raw[:], 0)
         nc.vector.memset(tab_sc[:].bitcast(I32), 0)
         nc.sync.dma_start(offs_sb[:], offs)
-        nc.sync.dma_start(pos1_sb[:], pos1)
-        nc.sync.dma_start(pos2_sb[:], pos2)
         for q in range(4):
             nc.sync.dma_start(tab_sc_rows[32 * q : 32 * q + 8, :], tab_scales[:, 4 * q : 4 * q + 4, :].bitcast(I32))
         nc.vector.memset(warm[:, 0:8], 0.0)
         nc.scalar.activation(warm[:, 8:16], warm[:, 0:8], ACT.Silu)
-        nc.vector.memset(wg_sc_raw[:], 0)
         nc.vector.memset(v_sc1[:].bitcast(I32), 0)
 
+        def load_tab(a):
+            nc.sync.dma_start(tab_w[a][:], tab_words[a].rearrange("p n i -> p (n i)").bitcast(I32))
+
         def load_wg(b):
-            wg_raw[b] = tile("wg_raw%d" % b, [P, 2, 256], I32, "wg_raw")
+            wg_raw[b] = tile("wg_raw0", [P, 2, 256], I32) if b == 0 else placed("wg_raw1", [P, 2, 256], I32, 40)
             nc.sync.dma_start(wg_raw[b][:], wg_words[:, :, 1024 * b : 1024 * (b + 1)].bitcast(I32).rearrange("a p n -> p a n"))
 
         def load_wu(a, b):
             if b == 0:
-                wu_raw[a][b] = placed("wu_raw%d0" % a, [P, 4, PASS], F32, (4, 16)[a])
+                wu_raw[a][b] = placed("wu_raw00", [P, 4, PASS], F32, 16)
             else:
-                wu_raw[a][b] = tile("wu_raw%d1" % a, [P, 4, PASS], F32, "load%d" % a)
+                wu_raw[a][b] = placed("wu_raw01", [P, 4, PASS], F32, 42) if a == 0 else tile("wu_raw11", [P, 4, PASS], F32, "load1")
             rows = wu[PASS * a : PASS * (a + 1), PASS * b : PASS * (b + 1)]
             nc.sync.dma_start(wu_raw[a][b][:], rows.rearrange("(p i) c -> p i c", i=4))
 
+        def load_wu_half(u):
+            rows = wu[PASS : 2 * PASS, 256 * u : 256 * (u + 1)]
+            nc.sync.dma_start(wu_half[u], rows.rearrange("(p i) c -> p i c", i=4))
+
         def load_w2(b):
-            w2_raw[b] = placed("w2_raw%d" % b, [P, 4, N], F32, (38, 16)[b])
+            w2_raw[b] = placed("w2_raw%d" % b, [P, 4, N], F32, (16, 1)[b])
+            if b == 0:
+                nc.sync.dma_start(w2_raw[b][:], w2[0:PASS, :].rearrange("(p t) n -> p t n", t=4))
+                return
             rows = w2[PASS * b : PASS * (b + 1), :].rearrange("(g t j) n -> t g j n", t=4, j=8)
             for t in range(4):
                 nc.sync.dma_start(w2_raw[b][:, t, :], rows[t])
 
-        for a in range(2):
-            nc.sync.dma_start(tab_w[a][:], tab_words[a].rearrange("p n i -> p (n i)").bitcast(I32))
+        load_tab(0)
         load_wg(0)
+        load_tab(1)
         for q in range(4):
             nc.sync.dma_start(
                 wg_sc_raw[32 * q : 32 * q + 4, :, :],
                 wg_scales[:, 4 * q : 4 * q + 4, :].bitcast(I32).rearrange("a r n -> r a n"),
             )
 
+        nc.sync.dma_start(pos1_sb[:], pos1)
+        nc.sync.dma_start(pos2_sb[:], pos2)
+
         for q in range(4):
             nc.vector.tensor_copy(tab_sc[32 * q : 32 * q + 8, :].bitcast(I32), tab_sc_rows[32 * q : 32 * q + 8, :])
         load_wu(0, 0)
         nc.vector.tensor_copy(v_sc[:], tab_sc[:].indirect(offs_sb[:]))
-        nc.scalar.dma_start(v_sc1[0:112, :].bitcast(I32), v_sc[4:116, :].bitcast(I32))
-        load_wu(1, 0)
-        nc.vector.tensor_copy(v_w[0][:], tab_w[0][:].bitcast(U32).indirect(offs_sb[:]))
+        nc.sync.dma_start(v_sc1[0:112, :].bitcast(I32), v_sc[4:116, :].bitcast(I32))
+        for u in range(2):
+            load_wu_half(u)
+
+        def gather_words(a, u):
+            nc.vector.tensor_copy(v_w[a][u][:], tab_w[a][:].bitcast(U32).indirect(offs_sb[:, 32 * u : 32 * (u + 1)]))
+
+        gather_words(0, 0)
+        load_wg(1)
         load_wu(0, 1)
 
-        def order_wg(b):
+        def order_wg():
             nc.vector.tensor_copy(
-                wg_w[b][:].rearrange("p a (t g w) -> p a t g w", t=4, w=4),
-                wg_raw[b][:].rearrange("p a (g t w) -> p a t g w", t=4, w=4),
+                wg_w1[:].rearrange("p a (t g w) -> p a t g w", t=4, w=4),
+                wg_raw[1][:].rearrange("p a (g t w) -> p a t g w", t=4, w=4),
             )
 
         def order_wg_scales():
             nc.vector.tensor_copy(
-                wg_sc[:].rearrange("p (x t g w) -> p x t g w", x=4, t=4, w=2),
-                wg_sc_raw[:].rearrange("p a (b g t w) -> p (a b) t g w", b=2, t=4, w=2),
+                wg_sc1[:].rearrange("p a (t g w) -> p a t g w", t=4, w=2),
+                wg_sc_raw[:, :, 128:256].rearrange("p a (g t w) -> p a t g w", t=4, w=2),
             )
 
         def rounded_wu(a, b, t):
             u, e = divmod(t, 2)
-            if b == 0:
-                return wu_bf[b, u][a][:, 512 * e : 512 * (e + 1)]
+            if (a, b, t) == (1, 0, 0):
+                return wu_bf_late[:]
+            if (a, b, t) == (1, 0, 1):
+                return wu_bf[0, 1][:, 1536:2048]
             return wu_bf[b, u][:, 1024 * a + 512 * e : 1024 * a + 512 * (e + 1)]
 
         def wu_cols(a, t):
             return slice(256 * a + P * (t % 2), 256 * a + P * (t % 2 + 1))
 
+        def raw_wu(a, t):
+            if a == 0:
+                return wu_raw[0][0][:, :, P * t : P * (t + 1)]
+            return wu_half[t // 2][:, :, P * (t % 2) : P * (t % 2 + 1)]
+
         def cast_wu_scalar(a, b, t):
-            nc.scalar.copy(
-                rounded_wu(a, b, t).rearrange("p (g h j i) -> p g h i j", h=2, j=4, i=4),
-                wu_raw[a][b][:].rearrange("p i (g t h j) -> p t g h i j", t=4, h=2, j=4)[:, t],
-            )
+            dst = rounded_wu(a, b, t).rearrange("p (g h j i) -> p g h i j", h=2, j=4, i=4)
+            if b == 0:
+                nc.scalar.copy(dst, raw_wu(a, t).rearrange("p i (g h j) -> p g h i j", h=2, j=4))
+            else:
+                nc.scalar.copy(dst, wu_raw[a][b][:].rearrange("p i (g t h j) -> p t g h i j", t=4, h=2, j=4)[:, t])
 
-        def cast_wu_vector(a, b, t):
+        def cast_wu_vector(a, t):
             nc.vector.tensor_copy(
-                rounded_wu(a, b, t).rearrange("p (g j i) -> p g j i", j=8, i=4),
-                wu_raw[a][b][:].rearrange("p i (g t j) -> p t g j i", t=4, j=8)[:, t],
+                rounded_wu(a, 0, t).rearrange("p (c i) -> p c i", i=4), raw_wu(a, t).rearrange("p i c -> p c i")
             )
 
-        def cast_wu_gpsimd(a, b, t):
+        def cast_wu_gpsimd(a, t):
             nc.gpsimd.tensor_scalar(
-                rounded_wu(a, b, t).rearrange("p (g j i) -> p g j i", j=8, i=4),
-                wu_raw[a][b][:].rearrange("p i (g t j) -> p t g j i", t=4, j=8)[:, t],
+                rounded_wu(a, 0, t).rearrange("p (c i) -> p c i", i=4),
+                raw_wu(a, t).rearrange("p i c -> p c i"),
                 1.0,
                 0.0,
                 ALU.mult,
@@ -187,18 +227,17 @@ def tile_list_gated_token_merge_kernel(tc, tab_words, tab_scales, offs, wg_words
             cols = slice(BANK * u, BANK * (u + 1))
             if a == 0:
                 bank_b[k, u] = bank("bank_b%d%d" % (k, u), "b%d%d" % (k % 2, u))
-            x = 2 * a + b
             nc.tensor.matmul_mx(
                 bank_b[k, u][:],
-                lhsT=wg_w[b][:, a, 64 * t : 64 * (t + 1)].bitcast(FP4X4),
-                lhsT_scale=wg_sc[:, 128 * x + 32 * t : 128 * x + 32 * (t + 1)].bitcast(U8),
-                rhs=v_w[a][:, cols].bitcast(FP8X4),
+                lhsT=(wg_raw[0], wg_w1)[b][:, a, 64 * t : 64 * (t + 1)].bitcast(FP4X4),
+                lhsT_scale=(wg_sc_raw, wg_sc1)[b][:, a, 32 * t : 32 * (t + 1)].bitcast(U8),
+                rhs=v_w[a][u][:].bitcast(FP8X4),
                 rhs_scale=(v_sc, v_sc1)[a][:, cols],
                 start=(a == 0),
                 stop=(a == 1),
             )
             if a == 1:
-                nc.scalar.activation(hs[(k - 1) % RING][:, S + BANK * u : S + BANK * (u + 1)], bank_b[k, u][:], ACT.Silu)
+                nc.scalar.activation(silu[k][u], bank_b[k, u][:], ACT.Silu)
 
         def up_pass(k, u, a):
             b, t = divmod(k, 4)
@@ -209,7 +248,7 @@ def tile_list_gated_token_merge_kernel(tc, tab_words, tab_scales, offs, wg_words
                 bank_a[k, u][:],
                 lhsT=wu_w[b, t // 2][:, wu_cols(a, t)].bitcast(FP8X4),
                 lhsT_scale=wu_sc[b, t // 2][:, wu_cols(a, t)],
-                rhs=v_w[a][:, cols].bitcast(FP8X4),
+                rhs=v_w[a][u][:].bitcast(FP8X4),
                 rhs_scale=v_sc[4 * a : P, cols],
                 start=(a == 0),
                 stop=(a == 1),
@@ -217,29 +256,32 @@ def tile_list_gated_token_merge_kernel(tc, tab_words, tab_scales, offs, wg_words
 
         def product(k, u):
             nc.vector.tensor_tensor(
-                hs[k % RING][:, BANK * u : BANK * (u + 1)],
+                hs[k][:, BANK * u : BANK * (u + 1)],
                 bank_a[k, u][:],
-                hs[(k - 1) % RING][:, S + BANK * u : S + BANK * (u + 1)],
+                silu[k][u],
                 ALU.mult,
             )
 
         def product_aside(k):
-            parked = z_f[(k - 1) // 4][:, (k - 1) % 4, :]
+            parked = z_rows[k - 1][:] if k <= 4 else z_f[1][:, k - 5, :]
             nc.scalar.copy(parked, bank_a[k, 0][:])
-            nc.gpsimd.tensor_tensor(hs[k % RING][:, 0:BANK], parked, hs[(k - 1) % RING][:, S : S + BANK], ALU.mult)
+            nc.gpsimd.tensor_tensor(hs[k][:, 0:BANK], parked, silu[k][0], ALU.mult)
 
         def pick_second_aside(k):
             b, t = divmod(k, 4)
-            nc.vector.tensor_copy(second[k % 2][:], hs[k % RING][:].indirect(pos2_sb[:]))
-            nc.gpsimd.tensor_tensor(z_f[b][:, t, :], second[k % 2][:], first[k][:], ALU.add)
+            nc.vector.tensor_copy(second[k], hs[k][:].indirect(pos2_sb[:]))
+            nc.gpsimd.tensor_tensor(z_rows[t][:] if b == 0 else z_f[1][:, t, :], second[k], first[k][:], ALU.add)
+            if b == 0:
+                for i in range(4):
+                    nc.sync.dma_start(z_f[0][32 * t : 32 * (t + 1), i, :], z_rows[t][i:P:4, :])
 
         def pick_first(k):
-            nc.vector.tensor_scalar(first[k][:], hs[k % RING][:].indirect(pos1_sb[:]), W1 / W2, 0.0, ALU.mult, ALU.add)
+            nc.vector.tensor_scalar(first[k][:], hs[k][:].indirect(pos1_sb[:]), W1 / W2, 0.0, ALU.mult, ALU.add)
 
         def pick_second(k, u):
             b, t = divmod(k, 4)
             cols = slice(256 * u, 256 * (u + 1))
-            picked = hs[k % RING][:].indirect(pos2_sb[:, 16 * u : 16 * (u + 1)])
+            picked = hs[k][:].indirect(pos2_sb[:, 16 * u : 16 * (u + 1)])
             nc.vector.tensor_tensor(z_f[b][:, t, cols], picked, first[k][:, cols], ALU.add)
 
         def round_z(b, u, on_vector):
@@ -277,77 +319,82 @@ def tile_list_gated_token_merge_kernel(tc, tab_words, tab_scales, offs, wg_words
             dst = out[256 * i : 256 * (i + 1), 256 * u : 256 * (u + 1)].rearrange("(n p) m -> p n m", p=P)
             nc.sync.dma_start(dst, res[u][i][:].rearrange("p (n m) -> p n m", n=2))
 
-        order_wg(0)
-        order_wg_scales()
-        load_wg(1)
-        for k in range(2):
-            for u in range(2):
-                gate_pass(k, u, 0)
-        for t in range(4):
-            cast_wu_scalar(0, 0, t)
+        gather_words(0, 1)
         for u in range(2):
-            nc.vector.tensor_copy(
-                v_w[1][:, BANK * u : BANK * (u + 1)], tab_w[1][:].bitcast(U32).indirect(offs_sb[:, 32 * u : 32 * (u + 1)])
-            )
-            gate_pass(0, u, 1)
+            for k in range(2):
+                gate_pass(k, u, 0)
+        for u in range(2):
+            gather_words(1, u)
+        for t in range(2):
+            cast_wu_scalar(0, 0, t)
+        cast_wu_gpsimd(0, 2)
+        quant_wu_first(0, slice(0, 256), wu_bf[0, 0][:])
         load_wu(1, 1)
-        quant_wu_first(0, slice(0, 256), wu_bf[0, 0][0][:])
+        for u in range(2):
+            gate_pass(0, u, 1)
         for u in range(2):
             up_pass(0, u, 0)
+        cast_wu_vector(1, 0)
+        quant_wu_first(0, wu_cols(1, 0), rounded_wu(1, 0, 0))
+        for u in range(2):
+            up_pass(0, u, 1)
         for u in range(2):
             gate_pass(1, u, 1)
-        for t in range(2):
-            cast_wu_vector(1, 0, t)
-            quant_wu_first(0, wu_cols(1, t), rounded_wu(1, 0, t))
-            if t == 0:
-                for u in range(2):
-                    up_pass(0, u, 1)
-        quant_wu_first(1, slice(0, 256), wu_bf[0, 1][0][:])
+        for u in range(2):
+            up_pass(1, u, 0)
+        cast_wu_vector(1, 1)
+        order_wg_scales()
+        quant_wu_first(0, wu_cols(1, 1), rounded_wu(1, 0, 1))
+        for u in range(2):
+            up_pass(1, u, 1)
+        cast_wu_scalar(0, 0, 3)
         load_w2(0)
-        for t in (2, 3):
-            cast_wu_gpsimd(1, 0, t)
+        cast_wu_vector(1, 2)
+        cast_wu_scalar(1, 0, 3)
         load_w2(1)
         for u in range(2):
             product(0, u)
+        order_wg()
+        quant_wu(0, 1)
+        product(1, 1)
 
+        later_wu = [[(0, 0), (0, 1), (1, 0), (1, 1)], [(0, 2)], [(0, 3), (1, 2), (1, 3)], [], [], [], []]
         for k in range(8):
             if k < 7:
-                for u in range(2):
+                if k > 0:
                     for a in range(2):
-                        if k > 0:
-                            gate_pass(k + 1, u, a)
-                for u in (1, 0):
+                        gate_pass(k + 1, 0, a)
                     for a in range(2):
-                        up_pass(k + 1, u, a)
-                if 1 <= k <= 3:
-                    for a in range(2):
-                        cast_wu_scalar(a, 1, k)
-                if k in (4, 5):
-                    cast_w2(k - 4, 0)
+                        up_pass(k + 1, 0, a)
                 product_aside(k + 1)
-                if k == 0:
+                if k < 6:
                     for a in range(2):
-                        cast_wu_scalar(a, 1, k)
+                        gate_pass(k + 2, 1, a)
+                for a, t in later_wu[k]:
+                    cast_wu_scalar(a, 1, t)
+                if k == 3:
+                    for u in range(2):
+                        cast_w2(0, u)
                 if k in (4, 5):
-                    cast_w2(k - 4, 1)
+                    cast_w2(1, k - 4)
                 if k == 6:
                     for u in range(2):
                         round_z(0, u, False)
-            if k == 7:
-                quant_z(0, slice(0, M), z_bf[0][:])
-                for u in range(2):
-                    down(0, u)
             pick_first(k)
             if k < 7:
-                product(k + 1, 1)
                 pick_second_aside(k)
-            if k == 0:
-                quant_wu_first(1, slice(256, 512), wu_bf[0, 1][1][:])
-                order_wg(1)
             if k in (1, 3):
                 quant_wu(1, k // 2)
             if k in (5, 6):
                 quant_w2(k - 5)
+            if k < 6:
+                for a in range(2):
+                    up_pass(k + 2, 1, a)
+                product(k + 2, 1)
+            if k == 7:
+                quant_z(0, slice(0, M), z_bf[0])
+                for u in range(2):
+                    down(0, u)
         pick_second(7, 0)
         round_z(1, 0, False)
         pick_second(7, 1)

@@ -20,6 +20,7 @@ P = 128
 PASS = 512
 BANK = 512
 W1, W2 = 0.7, 0.3
+RING = 4
 
 
 def tile_list_gated_token_merge_kernel(tc, tab_words, tab_scales, offs, wg_words, wg_scales, wu, w2, pos1, pos2, out):
@@ -64,22 +65,20 @@ def tile_list_gated_token_merge_kernel(tc, tab_words, tab_scales, offs, wg_words
         wu_w = {
             (0, 0): tile("wu_w00", [P, 512], U32),
             (0, 1): tile("wu_w01", [P, 512], U32),
-            (1, 0): placed("wu_w10", [P, 512], U32, 24 + 2 * 1),
-            (1, 1): placed("wu_w11", [P, 512], U32, 24 + 2 * 3),
+            (1, 0): tile("wu_w10", [P, 512], U32),
+            (1, 1): tile("wu_w11", [P, 512], U32),
         }
         wu_sc = {(b, u): tile("wu_sc%d%d" % (b, u), [P, 512], U8) for b in range(2) for u in range(2)}
         w2_raw = {}
         w2_bf = [placed("w2_bf%d" % b, [P, 4 * N], BF16, 64 + 4 * b) for b in range(2)]
-        w2_w = [placed("w2_w%d" % b, [P, N], U32, 24 + 2 * (5 + b)) for b in range(2)]
+        w2_w = [tile("w2_w%d" % b, [P, N], U32) for b in range(2)]
         w2_sc = [tile("w2_sc%d" % b, [P, N], U8) for b in range(2)]
-        hs = [placed("hs%d" % k, [P, 2 * S], F32, 72 + 8 * k) for k in range(8)]
-        ring = [tile("first%d" % k, [P, M], F32) for k in (3, 5)]
-        first_at = {0: 52, 2: 56, 4: 60, 6: 64}
-        first = [placed("first_at%d" % k, [P, M], F32, first_at[k]) if k in first_at else ring[k // 2 % 2] for k in range(8)]
-        second = [hs[k + 1][:, S + BANK : 2 * S] for k in range(7)]
+        ring = [tile("hs%d" % r, [P, 2 * S], F32) for r in range(RING)]
+        hs = [ring[k % RING] for k in range(10)]
+        first = [hs[k + 2][:, 0:M] for k in range(8)]
         silu = [[hs[0][:, S + BANK : 2 * S], hs[0][:, S : S + BANK]]]
         for k in range(1, 8):
-            silu.append([placed("silu%d" % k, [P, BANK], F32, 24 + 2 * k)[:], hs[k][:, S : S + BANK]])
+            silu.append([hs[k + 1][:, BANK:S], hs[k][:, S : S + BANK]])
         z_rows = [tile("z_rows%d" % k, [P, M], F32) for k in range(4)]
         z_late = tile("z_late", [P, 5 * M], F32)
         z_f = [tile("z_f0", [P, 4, M], F32)[:], z_late[:, 0 : 4 * M].rearrange("p (t m) -> p t m", t=4)]
@@ -175,9 +174,13 @@ def tile_list_gated_token_merge_kernel(tc, tab_words, tab_scales, offs, wg_words
                 return wu_bf_late[:]
             if (a, b, t) == (1, 0, 1):
                 return wu_bf[0, 1][:, 1536:2048]
+            if b == 1:
+                return wu_bf[b, u][:, 1024 * e + 512 * a : 1024 * e + 512 * (a + 1)]
             return wu_bf[b, u][:, 1024 * a + 512 * e : 1024 * a + 512 * (e + 1)]
 
-        def wu_cols(a, t):
+        def wu_cols(a, t, b=0):
+            if b == 1:
+                return slice(256 * (t % 2) + P * a, 256 * (t % 2) + P * (a + 1))
             return slice(256 * a + P * (t % 2), 256 * a + P * (t % 2 + 1))
 
         def raw_wu(a, t):
@@ -213,6 +216,11 @@ def tile_list_gated_token_merge_kernel(tc, tab_words, tab_scales, offs, wg_words
         def quant_wu(b, u):
             nc.vector.quantize_mx(wu_w[b, u][:].bitcast(FP8X4), wu_sc[b, u][:], wu_bf[b, u][:])
 
+        def quant_wu_slice(t):
+            u, e = divmod(t, 2)
+            cols = slice(256 * e, 256 * (e + 1))
+            nc.vector.quantize_mx(wu_w[1, u][:, cols].bitcast(FP8X4), wu_sc[1, u][:, cols], wu_bf[1, u][:, 1024 * e : 1024 * (e + 1)])
+
         def cast_w2(b, u):
             nc.scalar.copy(
                 w2_bf[b][:, 1024 * u : 1024 * (u + 1)].rearrange("p (c j t) -> p c t j", j=4, t=4),
@@ -246,8 +254,8 @@ def tile_list_gated_token_merge_kernel(tc, tab_words, tab_scales, offs, wg_words
                 bank_a[k, u] = bank("bank_a%d%d" % (k, u), "a%d%d" % (k % 2, u))
             nc.tensor.matmul_mx(
                 bank_a[k, u][:],
-                lhsT=wu_w[b, t // 2][:, wu_cols(a, t)].bitcast(FP8X4),
-                lhsT_scale=wu_sc[b, t // 2][:, wu_cols(a, t)],
+                lhsT=wu_w[b, t // 2][:, wu_cols(a, t, b)].bitcast(FP8X4),
+                lhsT_scale=wu_sc[b, t // 2][:, wu_cols(a, t, b)],
                 rhs=v_w[a][u][:].bitcast(FP8X4),
                 rhs_scale=v_sc[4 * a : P, cols],
                 start=(a == 0),
@@ -263,20 +271,20 @@ def tile_list_gated_token_merge_kernel(tc, tab_words, tab_scales, offs, wg_words
             )
 
         def product_aside(k):
-            parked = z_rows[k - 1][:] if k <= 4 else z_f[1][:, k - 5, :]
+            parked = hs[k][:, S + BANK : 2 * S]
             nc.scalar.copy(parked, bank_a[k, 0][:])
             nc.gpsimd.tensor_tensor(hs[k][:, 0:BANK], parked, silu[k][0], ALU.mult)
 
         def pick_second_aside(k):
             b, t = divmod(k, 4)
-            nc.vector.tensor_copy(second[k], hs[k][:].indirect(pos2_sb[:]))
-            nc.gpsimd.tensor_tensor(z_rows[t][:] if b == 0 else z_f[1][:, t, :], second[k], first[k][:], ALU.add)
+            total = z_rows[t][:] if b == 0 else z_f[1][:, t, :]
+            nc.vector.tensor_tensor(total, hs[k][:].indirect(pos2_sb[:]), first[k], ALU.add)
             if b == 0:
                 for i in range(4):
                     nc.sync.dma_start(z_f[0][32 * t : 32 * (t + 1), i, :], z_rows[t][i:P:4, :])
 
         def pick_first(k):
-            nc.vector.tensor_scalar(first[k][:], hs[k][:].indirect(pos1_sb[:]), W1 / W2, 0.0, ALU.mult, ALU.add)
+            nc.vector.tensor_scalar(first[k], hs[k][:].indirect(pos1_sb[:]), W1 / W2, 0.0, ALU.mult, ALU.add)
 
         def pick_second(k, u):
             b, t = divmod(k, 4)
@@ -356,9 +364,8 @@ def tile_list_gated_token_merge_kernel(tc, tab_words, tab_scales, offs, wg_words
             product(0, u)
         order_wg()
         quant_wu(0, 1)
-        product(1, 1)
 
-        later_wu = [[(0, 0), (0, 1), (1, 0), (1, 1)], [(0, 2)], [(0, 3), (1, 2), (1, 3)], [], [], [], []]
+        later_wu = [[(a, 2 * u), (a, 2 * u + 1)] for u in range(2) for a in range(2)] + [[], [], []]
         for k in range(8):
             if k < 7:
                 if k > 0:
@@ -372,25 +379,24 @@ def tile_list_gated_token_merge_kernel(tc, tab_words, tab_scales, offs, wg_words
                         gate_pass(k + 2, 1, a)
                 for a, t in later_wu[k]:
                     cast_wu_scalar(a, 1, t)
-                if k == 3:
-                    for u in range(2):
-                        cast_w2(0, u)
                 if k in (4, 5):
-                    cast_w2(1, k - 4)
+                    cast_w2(0, k - 4)
                 if k == 6:
+                    for u in range(2):
+                        cast_w2(1, u)
                     for u in range(2):
                         round_z(0, u, False)
             pick_first(k)
             if k < 7:
+                if k > 0:
+                    for a in range(2):
+                        up_pass(k + 1, 1, a)
+                product(k + 1, 1)
                 pick_second_aside(k)
-            if k in (1, 3):
-                quant_wu(1, k // 2)
+            if 1 <= k <= 4:
+                quant_wu_slice(k - 1)
             if k in (5, 6):
                 quant_w2(k - 5)
-            if k < 6:
-                for a in range(2):
-                    up_pass(k + 2, 1, a)
-                product(k + 2, 1)
             if k == 7:
                 quant_z(0, slice(0, M), z_bf[0])
                 for u in range(2):
@@ -399,7 +405,7 @@ def tile_list_gated_token_merge_kernel(tc, tab_words, tab_scales, offs, wg_words
         round_z(1, 0, False)
         pick_second(7, 1)
         round_z(1, 1, True)
-        for u in range(2):
+        for u in (1, 0):
             quant_z(1, slice(256 * u, 256 * (u + 1)), z_bf[1][u][:])
             down(1, u)
             for i in range(2):

@@ -19,6 +19,8 @@ ACT = mybir.ActivationFunctionType
 P = 128
 PASS = 512
 BANK = 512
+SLICES = H // P
+PART = M // 2
 W1, W2 = 0.7, 0.3
 RING = 4
 
@@ -39,6 +41,7 @@ def tile_list_gated_token_merge_kernel(tc, tab_words, tab_scales, offs, wg_words
         offs_sb = tile("offs_sb", [P, S // 16], U16)
         pos1_sb = tile("pos1_sb", [P, M // 16], U16)
         pos2_sb = tile("pos2_sb", [P, M // 16], U16)
+
         tab_sc = placed("tab_sc", [P, T], U8, 8)
         tab_w = [placed("tab_w0", [P, T], I32, 41), tile("tab_w1", [P, T], I32, "load1")]
         v_w = [
@@ -62,28 +65,24 @@ def tile_list_gated_token_merge_kernel(tc, tab_words, tab_scales, offs, wg_words
             (1, 1): placed("wu_bf11", [P, 2048], BF16, 60),
         }
         wu_bf_late = placed("wu_bf_late", [P, 512], BF16, 13)
-        wu_w = {
-            (0, 0): tile("wu_w00", [P, 512], U32),
-            (0, 1): tile("wu_w01", [P, 512], U32),
-            (1, 0): tile("wu_w10", [P, 512], U32),
-            (1, 1): tile("wu_w11", [P, 512], U32),
-        }
+        wu_w = {(b, u): tile("wu_w%d%d" % (b, u), [P, 512], U32) for b in range(2) for u in range(2)}
         wu_sc = {(b, u): tile("wu_sc%d%d" % (b, u), [P, 512], U8) for b in range(2) for u in range(2)}
         w2_raw = {}
         w2_bf = [placed("w2_bf%d" % b, [P, 4 * N], BF16, 64 + 4 * b) for b in range(2)]
         w2_w = [tile("w2_w%d" % b, [P, N], U32) for b in range(2)]
         w2_sc = [tile("w2_sc%d" % b, [P, N], U8) for b in range(2)]
+
         ring = [tile("hs%d" % r, [P, 2 * S], F32) for r in range(RING)]
-        hs = [ring[k % RING] for k in range(10)]
-        first = [hs[k + 2][:, 0:M] for k in range(8)]
+        hs = [ring[k % RING] for k in range(SLICES + 2)]
+        first = [hs[k + 2][:, 0:M] for k in range(SLICES)]
         silu = [[hs[0][:, S + BANK : 2 * S], hs[0][:, S : S + BANK]]]
-        for k in range(1, 8):
+        for k in range(1, SLICES):
             silu.append([hs[k + 1][:, BANK:S], hs[k][:, S : S + BANK]])
         z_rows = [tile("z_rows%d" % k, [P, M], F32) for k in range(4)]
         z_late = tile("z_late", [P, 5 * M], F32)
         z_f = [tile("z_f0", [P, 4, M], F32)[:], z_late[:, 0 : 4 * M].rearrange("p (t m) -> p t m", t=4)]
-        z_bf = [z_late[:, 3 * M : 5 * M].bitcast(BF16), [tile("z_bf1%d" % u, [P, 2 * M], BF16) for u in range(2)]]
-        z_w = [tile("z_w0", [P, M], U32), tile("z_w1", [P, M], U32)]
+        z_bf = [z_late[:, 2 * M + PART : 4 * M + PART].bitcast(BF16), tile("z_bf1", [P, 3 * M], BF16)[:]]
+        z_w = [tile("z_w%d" % b, [P, M], U32) for b in range(2)]
         z_sc = [tile("z_sc%d" % b, [P, M], U8) for b in range(2)]
         res = [[tile("res%d%d" % (u, i), [P, BANK], F32) for i in range(2)] for u in range(2)]
         warm = tile("warm", [P, 16], F32)
@@ -111,8 +110,10 @@ def tile_list_gated_token_merge_kernel(tc, tab_words, tab_scales, offs, wg_words
         def load_wu(a, b):
             if b == 0:
                 wu_raw[a][b] = placed("wu_raw00", [P, 4, PASS], F32, 16)
+            elif a == 0:
+                wu_raw[a][b] = placed("wu_raw01", [P, 4, PASS], F32, 42)
             else:
-                wu_raw[a][b] = placed("wu_raw01", [P, 4, PASS], F32, 42) if a == 0 else tile("wu_raw11", [P, 4, PASS], F32, "load1")
+                wu_raw[a][b] = tile("wu_raw11", [P, 4, PASS], F32, "load1")
             rows = wu[PASS * a : PASS * (a + 1), PASS * b : PASS * (b + 1)]
             nc.sync.dma_start(wu_raw[a][b][:], rows.rearrange("(p i) c -> p i c", i=4))
 
@@ -124,10 +125,10 @@ def tile_list_gated_token_merge_kernel(tc, tab_words, tab_scales, offs, wg_words
             w2_raw[b] = placed("w2_raw%d" % b, [P, 4, N], F32, (16, 1)[b])
             if b == 0:
                 nc.sync.dma_start(w2_raw[b][:], w2[0:PASS, :].rearrange("(p t) n -> p t n", t=4))
-                return
-            rows = w2[PASS * b : PASS * (b + 1), :].rearrange("(g t j) n -> t g j n", t=4, j=8)
-            for t in range(4):
-                nc.sync.dma_start(w2_raw[b][:, t, :], rows[t])
+            else:
+                rows = w2[PASS:H, :].rearrange("(g t j) n -> t g j n", t=4, j=8)
+                for t in range(4):
+                    nc.sync.dma_start(w2_raw[b][:, t, :], rows[t])
 
         load_tab(0)
         load_wg(0)
@@ -137,7 +138,6 @@ def tile_list_gated_token_merge_kernel(tc, tab_words, tab_scales, offs, wg_words
                 wg_sc_raw[32 * q : 32 * q + 4, :, :],
                 wg_scales[:, 4 * q : 4 * q + 4, :].bitcast(I32).rearrange("a r n -> r a n"),
             )
-
         nc.sync.dma_start(pos1_sb[:], pos1)
         nc.sync.dma_start(pos2_sb[:], pos2)
 
@@ -173,34 +173,33 @@ def tile_list_gated_token_merge_kernel(tc, tab_words, tab_scales, offs, wg_words
             if (a, b, t) == (1, 0, 0):
                 return wu_bf_late[:]
             if (a, b, t) == (1, 0, 1):
-                return wu_bf[0, 1][:, 1536:2048]
+                return rounded_wu(1, 0, 3)
             if b == 1:
                 return wu_bf[b, u][:, 1024 * e + 512 * a : 1024 * e + 512 * (a + 1)]
             return wu_bf[b, u][:, 1024 * a + 512 * e : 1024 * a + 512 * (e + 1)]
 
-        def wu_cols(a, t, b=0):
-            if b == 1:
-                return slice(256 * (t % 2) + P * a, 256 * (t % 2) + P * (a + 1))
-            return slice(256 * a + P * (t % 2), 256 * a + P * (t % 2 + 1))
+        def wu_cols(a, b, t):
+            at = 256 * (t % 2) + P * a if b == 1 else 256 * a + P * (t % 2)
+            return slice(at, at + P)
 
         def raw_wu(a, t):
             if a == 0:
                 return wu_raw[0][0][:, :, P * t : P * (t + 1)]
             return wu_half[t // 2][:, :, P * (t % 2) : P * (t % 2 + 1)]
 
-        def cast_wu_scalar(a, b, t):
+        def round_wu_scalar(a, b, t):
             dst = rounded_wu(a, b, t).rearrange("p (g h j i) -> p g h i j", h=2, j=4, i=4)
             if b == 0:
                 nc.scalar.copy(dst, raw_wu(a, t).rearrange("p i (g h j) -> p g h i j", h=2, j=4))
             else:
                 nc.scalar.copy(dst, wu_raw[a][b][:].rearrange("p i (g t h j) -> p t g h i j", t=4, h=2, j=4)[:, t])
 
-        def cast_wu_vector(a, t):
+        def round_wu_vector(a, t):
             nc.vector.tensor_copy(
                 rounded_wu(a, 0, t).rearrange("p (c i) -> p c i", i=4), raw_wu(a, t).rearrange("p i c -> p c i")
             )
 
-        def cast_wu_gpsimd(a, t):
+        def round_wu_gpsimd(a, t):
             nc.gpsimd.tensor_scalar(
                 rounded_wu(a, 0, t).rearrange("p (c i) -> p c i", i=4),
                 raw_wu(a, t).rearrange("p i c -> p c i"),
@@ -210,18 +209,14 @@ def tile_list_gated_token_merge_kernel(tc, tab_words, tab_scales, offs, wg_words
                 ALU.add,
             )
 
-        def quant_wu_first(u, cols, rounded):
-            nc.vector.quantize_mx(wu_w[0, u][:, cols].bitcast(FP8X4), wu_sc[0, u][:, cols], rounded)
-
-        def quant_wu(b, u):
-            nc.vector.quantize_mx(wu_w[b, u][:].bitcast(FP8X4), wu_sc[b, u][:], wu_bf[b, u][:])
+        def quant_wu(b, u, cols, rounded):
+            nc.vector.quantize_mx(wu_w[b, u][:, cols].bitcast(FP8X4), wu_sc[b, u][:, cols], rounded)
 
         def quant_wu_slice(t):
             u, e = divmod(t, 2)
-            cols = slice(256 * e, 256 * (e + 1))
-            nc.vector.quantize_mx(wu_w[1, u][:, cols].bitcast(FP8X4), wu_sc[1, u][:, cols], wu_bf[1, u][:, 1024 * e : 1024 * (e + 1)])
+            quant_wu(1, u, slice(256 * e, 256 * (e + 1)), wu_bf[1, u][:, 1024 * e : 1024 * (e + 1)])
 
-        def cast_w2(b, u):
+        def round_w2(b, u):
             nc.scalar.copy(
                 w2_bf[b][:, 1024 * u : 1024 * (u + 1)].rearrange("p (c j t) -> p c t j", j=4, t=4),
                 w2_raw[b][:, :, 256 * u : 256 * (u + 1)].rearrange("p t (c j) -> p c t j", j=4),
@@ -254,28 +249,26 @@ def tile_list_gated_token_merge_kernel(tc, tab_words, tab_scales, offs, wg_words
                 bank_a[k, u] = bank("bank_a%d%d" % (k, u), "a%d%d" % (k % 2, u))
             nc.tensor.matmul_mx(
                 bank_a[k, u][:],
-                lhsT=wu_w[b, t // 2][:, wu_cols(a, t, b)].bitcast(FP8X4),
-                lhsT_scale=wu_sc[b, t // 2][:, wu_cols(a, t, b)],
+                lhsT=wu_w[b, t // 2][:, wu_cols(a, b, t)].bitcast(FP8X4),
+                lhsT_scale=wu_sc[b, t // 2][:, wu_cols(a, b, t)],
                 rhs=v_w[a][u][:].bitcast(FP8X4),
                 rhs_scale=v_sc[4 * a : P, cols],
                 start=(a == 0),
                 stop=(a == 1),
             )
 
-        def product(k, u):
-            nc.vector.tensor_tensor(
-                hs[k][:, BANK * u : BANK * (u + 1)],
-                bank_a[k, u][:],
-                silu[k][u],
-                ALU.mult,
-            )
+        def product_vector(k, u):
+            nc.vector.tensor_tensor(hs[k][:, BANK * u : BANK * (u + 1)], bank_a[k, u][:], silu[k][u], ALU.mult)
 
-        def product_aside(k):
+        def product_gpsimd(k):
             parked = hs[k][:, S + BANK : 2 * S]
             nc.scalar.copy(parked, bank_a[k, 0][:])
             nc.gpsimd.tensor_tensor(hs[k][:, 0:BANK], parked, silu[k][0], ALU.mult)
 
-        def pick_second_aside(k):
+        def pick_first(k):
+            nc.vector.tensor_scalar(first[k], hs[k][:].indirect(pos1_sb[:]), W1 / W2, 0.0, ALU.mult, ALU.add)
+
+        def pick_second(k):
             b, t = divmod(k, 4)
             total = z_rows[t][:] if b == 0 else z_f[1][:, t, :]
             nc.vector.tensor_tensor(total, hs[k][:].indirect(pos2_sb[:]), first[k], ALU.add)
@@ -283,26 +276,25 @@ def tile_list_gated_token_merge_kernel(tc, tab_words, tab_scales, offs, wg_words
                 for i in range(4):
                     nc.sync.dma_start(z_f[0][32 * t : 32 * (t + 1), i, :], z_rows[t][i:P:4, :])
 
-        def pick_first(k):
-            nc.vector.tensor_scalar(first[k], hs[k][:].indirect(pos1_sb[:]), W1 / W2, 0.0, ALU.mult, ALU.add)
-
-        def pick_second(k, u):
-            b, t = divmod(k, 4)
-            cols = slice(256 * u, 256 * (u + 1))
+        def pick_second_part(k, u):
+            cols = slice(PART * u, PART * (u + 1))
             picked = hs[k][:].indirect(pos2_sb[:, 16 * u : 16 * (u + 1)])
-            nc.vector.tensor_tensor(z_f[b][:, t, cols], picked, first[k][:, cols], ALU.add)
+            nc.vector.tensor_tensor(z_f[1][:, k - 4, cols], picked, first[k][:, cols], ALU.add)
 
-        def round_z(b, u, on_vector):
-            rounded = z_bf[0][:, 1024 * u : 1024 * (u + 1)] if b == 0 else z_bf[1][u][:]
-            dst = rounded.rearrange("p (c j t) -> p c t j", j=4, t=4)
-            src = z_f[b][:, :, 256 * u : 256 * (u + 1)].rearrange("p t (c j) -> p c t j", j=4)
+        def rounded_z(b, m0, m1):
+            at = 4 * m0 - (2 * PART if b == 1 and m0 >= PART else 0)
+            return z_bf[b][:, at : at + 4 * (m1 - m0)]
+
+        def round_z(b, m0, m1, on_vector):
+            dst = rounded_z(b, m0, m1).rearrange("p (c j t) -> p c t j", j=4, t=4)
+            src = z_f[b][:, :, m0:m1].rearrange("p t (c j) -> p c t j", j=4)
             if on_vector:
                 nc.vector.tensor_scalar(dst, src, W2, 0.0, ALU.mult, ALU.add)
             else:
                 nc.scalar.activation(dst, src, ACT.Copy, scale=W2)
 
-        def quant_z(b, cols, rounded):
-            nc.vector.quantize_mx(z_w[b][:, cols].bitcast(FP8X4), z_sc[b][:, cols], rounded)
+        def quant_z(b, m0, m1):
+            nc.vector.quantize_mx(z_w[b][:, m0:m1].bitcast(FP8X4), z_sc[b][:, m0:m1], rounded_z(b, m0, m1))
 
         def down(b, u):
             if b == 0:
@@ -310,21 +302,21 @@ def tile_list_gated_token_merge_kernel(tc, tab_words, tab_scales, offs, wg_words
             for n in range(4):
                 rows = slice(P * n, P * (n + 1))
                 nc.tensor.matmul_mx(
-                    bank_o[u][n // 2][:, 256 * (n % 2) : 256 * (n % 2 + 1)],
+                    bank_o[u][n // 2][:, PART * (n % 2) : PART * (n % 2 + 1)],
                     lhsT=w2_w[b][:, rows].bitcast(FP8X4),
                     lhsT_scale=w2_sc[b][:, rows],
-                    rhs=z_w[b][:, 256 * u : 256 * (u + 1)].bitcast(FP8X4),
-                    rhs_scale=z_sc[b][:, 256 * u : 256 * (u + 1)],
+                    rhs=z_w[b][:, PART * u : PART * (u + 1)].bitcast(FP8X4),
+                    rhs_scale=z_sc[b][:, PART * u : PART * (u + 1)],
                     start=(b == 0 and n % 2 == 0),
                     stop=(b == 1 and n % 2 == 1),
                 )
 
-        def store(u, i):
-            if i == 0:
-                nc.scalar.copy(res[u][i][:], bank_o[u][i][:])
-            else:
+        def store(u, i, on_vector):
+            if on_vector:
                 nc.vector.tensor_copy(res[u][i][:], bank_o[u][i][:])
-            dst = out[256 * i : 256 * (i + 1), 256 * u : 256 * (u + 1)].rearrange("(n p) m -> p n m", p=P)
+            else:
+                nc.scalar.copy(res[u][i][:], bank_o[u][i][:])
+            dst = out[2 * P * i : 2 * P * (i + 1), PART * u : PART * (u + 1)].rearrange("(n p) m -> p n m", p=P)
             nc.sync.dma_start(dst, res[u][i][:].rearrange("p (n m) -> p n m", n=2))
 
         gather_words(0, 1)
@@ -334,79 +326,79 @@ def tile_list_gated_token_merge_kernel(tc, tab_words, tab_scales, offs, wg_words
         for u in range(2):
             gather_words(1, u)
         for t in range(2):
-            cast_wu_scalar(0, 0, t)
-        cast_wu_gpsimd(0, 2)
-        quant_wu_first(0, slice(0, 256), wu_bf[0, 0][:])
+            round_wu_scalar(0, 0, t)
+        round_wu_gpsimd(0, 2)
+        quant_wu(0, 0, slice(0, 256), wu_bf[0, 0][:])
         load_wu(1, 1)
-        for u in range(2):
-            gate_pass(0, u, 1)
-        for u in range(2):
-            up_pass(0, u, 0)
-        cast_wu_vector(1, 0)
-        quant_wu_first(0, wu_cols(1, 0), rounded_wu(1, 0, 0))
-        for u in range(2):
-            up_pass(0, u, 1)
-        for u in range(2):
-            gate_pass(1, u, 1)
-        for u in range(2):
-            up_pass(1, u, 0)
-        cast_wu_vector(1, 1)
-        order_wg_scales()
-        quant_wu_first(0, wu_cols(1, 1), rounded_wu(1, 0, 1))
-        for u in range(2):
-            up_pass(1, u, 1)
-        cast_wu_scalar(0, 0, 3)
+        for k in range(2):
+            for u in range(2):
+                gate_pass(k, u, 1)
+            for u in range(2):
+                up_pass(k, u, 0)
+            round_wu_vector(1, k)
+            if k == 1:
+                order_wg_scales()
+            quant_wu(0, 0, wu_cols(1, 0, k), rounded_wu(1, 0, k))
+            for u in range(2):
+                up_pass(k, u, 1)
+        round_wu_scalar(0, 0, 3)
         load_w2(0)
-        cast_wu_vector(1, 2)
-        cast_wu_scalar(1, 0, 3)
+        round_wu_vector(1, 2)
+        round_wu_scalar(1, 0, 3)
         load_w2(1)
         for u in range(2):
-            product(0, u)
+            product_vector(0, u)
         order_wg()
-        quant_wu(0, 1)
+        quant_wu(0, 1, slice(0, 512), wu_bf[0, 1][:])
 
-        later_wu = [[(a, 2 * u), (a, 2 * u + 1)] for u in range(2) for a in range(2)] + [[], [], []]
-        for k in range(8):
-            if k < 7:
+        for k in range(SLICES):
+            if k + 1 < SLICES:
                 if k > 0:
                     for a in range(2):
                         gate_pass(k + 1, 0, a)
                     for a in range(2):
                         up_pass(k + 1, 0, a)
-                product_aside(k + 1)
-                if k < 6:
+                product_gpsimd(k + 1)
+                if k + 2 < SLICES:
                     for a in range(2):
                         gate_pass(k + 2, 1, a)
-                for a, t in later_wu[k]:
-                    cast_wu_scalar(a, 1, t)
-                if k in (4, 5):
-                    cast_w2(0, k - 4)
-                if k == 6:
+                if k < 4:
+                    for e in range(2):
+                        round_wu_scalar(k % 2, 1, 2 * (k // 2) + e)
+                elif k + 2 < SLICES:
+                    round_w2(0, k - 4)
+                else:
                     for u in range(2):
-                        cast_w2(1, u)
+                        round_w2(1, u)
                     for u in range(2):
-                        round_z(0, u, False)
+                        round_z(0, PART * u, PART * (u + 1), False)
             pick_first(k)
-            if k < 7:
+            if k + 1 < SLICES:
                 if k > 0:
                     for a in range(2):
                         up_pass(k + 1, 1, a)
-                product(k + 1, 1)
-                pick_second_aside(k)
+                product_vector(k + 1, 1)
+            if k + 2 < SLICES:
+                pick_second(k)
+            elif k + 1 < SLICES:
+                pick_second_part(k, 0)
             if 1 <= k <= 4:
                 quant_wu_slice(k - 1)
             if k in (5, 6):
                 quant_w2(k - 5)
-            if k == 7:
-                quant_z(0, slice(0, M), z_bf[0])
-                for u in range(2):
-                    down(0, u)
-        pick_second(7, 0)
-        round_z(1, 0, False)
-        pick_second(7, 1)
-        round_z(1, 1, True)
-        for u in (1, 0):
-            quant_z(1, slice(256 * u, 256 * (u + 1)), z_bf[1][u][:])
+
+        quant_z(0, 0, M)
+        for u in range(2):
+            down(0, u)
+        pick_second_part(SLICES - 1, 0)
+        round_z(1, 0, PART, False)
+        for k in (SLICES - 2, SLICES - 1):
+            pick_second_part(k, 1)
+        round_z(1, PART + P, M, False)
+        for u in range(2):
+            if u == 1:
+                round_z(1, PART, PART + P, True)
+            quant_z(1, PART * u, PART * (u + 1))
             down(1, u)
             for i in range(2):
-                store(u, i)
+                store(u, i, (u, i) == (1, 0))

@@ -36,53 +36,74 @@ def tile_list_gated_token_merge_kernel(tc, tab_words, tab_scales, offs, wg_words
             return sb.tile(shape, dtype, name=name, tag=tag or name, align_bytes=64)
 
         def placed(name, shape, dtype, kib):
-            return shared.tile(shape, dtype, name=name, align_bytes=64, offset=1024 * kib)
+            return shared.tile(shape, dtype, name=name, align_bytes=64, offset=int(1024 * kib))
 
         offs_sb = tile("offs_sb", [P, S // 16], U16)
         pos1_sb = tile("pos1_sb", [P, M // 16], U16)
         pos2_sb = tile("pos2_sb", [P, M // 16], U16)
 
-        tab_sc = placed("tab_sc", [P, T], U8, 8)
-        tab_w = [placed("tab_w0", [P, T], I32, 41), tile("tab_w1", [P, T], I32, "load1")]
-        v_w = [
-            [placed("v_w00", [P, BANK], U32, 9), tile("v_w01", [P, BANK], U32)],
-            [tile("v_w1%d" % u, [P, BANK], U32) for u in range(2)],
-        ]
+        tab_sc = placed("tab_sc", [P, T], U8, 1)
+        tab_w = [tile("tab_w0", [P, T], I32), tile("tab_w1", [P, T], I32)]
+        v_w = [[tile("v_w%d%d" % (a, u), [P, BANK], U32) for u in range(2)] for a in range(2)]
         v_sc = tile("v_sc", [P, S], U8)
         v_sc1 = tile("v_sc1", [P, S], U8)
-        wg_raw = {}
-        tab_sc_rows = placed("tab_sc_rows", [P, T // 4], I32, 16)
+        wg_raw = [tile("wg_raw0", [P, 2, 256], I32), placed("wg_raw1", [P, 2, 256], I32, 0)]
         wg_w1 = tile("wg_w1", [P, 2, 256], I32)
         wg_sc_raw = tile("wg_sc_raw", [P, 2, 256], I32)
-        wg_sc1 = placed("wg_sc1", [P, 2, 128], I32, 13)
-        wu_raw = [{}, {}]
-        wu_halves = placed("wu_halves", [P, 2048], F32, 1)
-        wu_half = [wu_halves[:, 1024 * u : 1024 * (u + 1)].rearrange("p (i c) -> p i c", i=4) for u in range(2)]
-        wu_bf = {
-            (0, 0): tile("wu_bf00", [P, 1024], BF16),
-            (0, 1): placed("wu_bf01", [P, 2048], BF16, 52),
-            (1, 0): placed("wu_bf10", [P, 2048], BF16, 56),
-            (1, 1): placed("wu_bf11", [P, 2048], BF16, 60),
-        }
-        wu_bf_late = placed("wu_bf_late", [P, 512], BF16, 13)
-        wu_w = {(b, u): tile("wu_w%d%d" % (b, u), [P, 512], U32) for b in range(2) for u in range(2)}
-        wu_sc = {(b, u): tile("wu_sc%d%d" % (b, u), [P, 512], U8) for b in range(2) for u in range(2)}
-        w2_raw = {}
-        w2_bf = [placed("w2_bf%d" % b, [P, 4 * N], BF16, 64 + 4 * b) for b in range(2)]
-        w2_w = [tile("w2_w%d" % b, [P, N], U32) for b in range(2)]
-        w2_sc = [tile("w2_sc%d" % b, [P, N], U8) for b in range(2)]
+        wg_sc1 = tile("wg_sc1", [P, 2, 128], I32)
+        raw = placed("raw", [P, 10240], F32, 2)
 
+        def raw_part(at, width):
+            return raw[:, at : at + 4 * width].rearrange("p (i c) -> p i c", i=4)
+
+        wu_first = tile("wu_first", [P, 4, 256], F32)
+        wu_pair = [wu_first[:], raw_part(0, 256)]
+        wu_one = {(a, k): raw_part(1024 + 512 * (2 * k + a - 4), P) for a, k in ((0, 2), (1, 2))}
+        wu_one.update({(a, 3): placed("wu_one%d3" % a, [P, 4, P], F32, 48 + 2 * a)[:] for a in range(2)})
+        wu_late = [raw_part(2048 + 2048 * a, PASS) for a in range(2)]
+        w2_raw = [raw_part(6144 + 2048 * b, N) for b in range(2)]
         ring = [tile("hs%d" % r, [P, 2 * S], F32) for r in range(RING)]
         hs = [ring[k % RING] for k in range(SLICES + 2)]
-        first = [hs[k + 2][:, 0:M] for k in range(SLICES)]
-        silu = [[hs[0][:, S + BANK : 2 * S], hs[0][:, S : S + BANK]]]
+        first = [hs[k + 2][:, S : S + M] for k in range(SLICES)]
+        first[1] = hs[3][:, 0:M]
+        first[4] = hs[6][:, S + PART : S + PART + M]
+        first[6:8] = [tile("first%d" % k, [P, M], F32)[:] for k in (6, 7)]
+        z_late = tile("z_late", [P, 5 * M + P], F32)
+        z_rows = [placed("z_rows0", [P, M], F32, 51)[:]] + [tile("z_rows%d" % k, [P, M], F32)[:] for k in (1, 2)]
+        z_rows.append(placed("z_rows3", [P, M], F32, 60)[:])
+        parked = [None, placed("parked1", [P, BANK], F32, 52)[:]] + z_rows[1:3] + [None]
+        parked += [z_late[:, M * t : M * (t + 1)] for t in range(3)]
+        silu = [[hs[0][:, S + BANK : 2 * S], hs[2][:, 256:768]]]
         for k in range(1, SLICES):
-            silu.append([hs[k + 1][:, BANK:S], hs[k][:, S : S + BANK]])
-        z_rows = [tile("z_rows%d" % k, [P, M], F32) for k in range(4)]
-        z_late = tile("z_late", [P, 5 * M], F32)
-        z_f = [tile("z_f0", [P, 4, M], F32)[:], z_late[:, 0 : 4 * M].rearrange("p (t m) -> p t m", t=4)]
-        z_bf = [z_late[:, 2 * M + PART : 4 * M + PART].bitcast(BF16), tile("z_bf1", [P, 3 * M], BF16)[:]]
-        z_w = [tile("z_w%d" % b, [P, M], U32) for b in range(2)]
+            silu.append([placed("silu%d" % k, [P, BANK], F32, 54 + 2 * k + 8 * (k == 7))[:], hs[k - 1][:, S : S + BANK]])
+        wu_bf = {k: hs[k - 1][:, 256:768].bitcast(BF16) for k in (2, 3, 6, 7)}
+        wu_bf.update({k: tile("wu_bf%d" % k, [P, 1024], BF16)[:] for k in (0, 1)})
+        wu_bf[4] = placed("wu_bf4", [P, 1024], BF16, 70)[:]
+        wu_bf[5] = first[3].bitcast(BF16)
+        wu_w = {k: placed("wu_w%d" % k, [P, 256], U32, at) for k, at in ((3, 56), (4, 60), (6, 62), (7, 64))}
+        wu_w.update({k: tile("wu_w%d" % k, [P, 256], U32) for k in (0, 1, 2, 5)})
+        wu_sc = {k: tile("wu_sc%d" % k, [P, 256], U8) for k in range(SLICES)}
+        w2_bf1 = tile("w2_bf1", [P, 4 * N], BF16)
+        w2_bf = [
+            [hs[7][:, 256:768].bitcast(BF16), placed("w2_bf01", [P, 1024], BF16, 70)[:]],
+            [w2_bf1[:, 0:1024], w2_bf1[:, 1024:2048]],
+        ]
+        w2_w1 = placed("w2_w1", [P, N], U32, 77.5)
+        w2_w = [
+            [placed("w2_w00", [P, 256], U32, 66)[:], placed("w2_w01", [P, 256], U32, 76.5)[:]],
+            [w2_w1[:, 0:256], w2_w1[:, 256:N]],
+        ]
+        w2_sc = [tile("w2_sc%d" % b, [P, N], U8) for b in range(2)]
+        z_f0 = tile("z_f0", [P, 4, M], F32)
+        z_f = [
+            [z_f0[:, :, PART * u : PART * (u + 1)] for u in range(2)],
+            [
+                z_late[:, 0 : 4 * M].rearrange("p (t m) -> p t m", t=4)[:, :, 0:PART],
+                z_late[:, 3 * M + P :].rearrange("p (t m) -> p t m", t=4),
+            ],
+        ]
+        z_bf = [z_late[:, 3 * M + P :].bitcast(BF16), tile("z_bf1", [P, 4 * M], BF16)[:]]
+        z_w = [placed("z_w0", [P, M], U32, 74.5), tile("z_w1", [P, M], U32)]
         z_sc = [tile("z_sc%d" % b, [P, M], U8) for b in range(2)]
         res = [[tile("res%d%d" % (u, i), [P, BANK], F32) for i in range(2)] for u in range(2)]
         warm = tile("warm", [P, 16], F32)
@@ -91,70 +112,50 @@ def tile_list_gated_token_merge_kernel(tc, tab_words, tab_scales, offs, wg_words
         def bank(name, tag):
             return ps.tile([P, BANK], F32, name=name, tag=tag)
 
-        nc.vector.memset(wg_sc_raw[:], 0)
         nc.vector.memset(tab_sc[:].bitcast(I32), 0)
-        nc.sync.dma_start(offs_sb[:], offs)
-        for q in range(4):
-            nc.sync.dma_start(tab_sc_rows[32 * q : 32 * q + 8, :], tab_scales[:, 4 * q : 4 * q + 4, :].bitcast(I32))
+        nc.vector.memset(wg_sc_raw[:], 0)
+        for sb_list, dram_list in ((offs_sb, offs), (pos1_sb, pos1), (pos2_sb, pos2)):
+            nc.sync.dma_start(sb_list[:], dram_list)
+        rows_by_r = tab_scales.rearrange("a (q r) n -> r q a n", r=4)
+        for r in range(4):
+            nc.sync.dma_start(tab_sc[r:P:16, :].bitcast(I32), rows_by_r[r].bitcast(I32))
         nc.vector.memset(warm[:, 0:8], 0.0)
         nc.scalar.activation(warm[:, 8:16], warm[:, 0:8], ACT.Silu)
         nc.vector.memset(v_sc1[:].bitcast(I32), 0)
+        for r in (1, 2, 3):
+            nc.vector.memset(ring[r][:, S + BANK : 2 * S], 0.0)
 
-        def load_tab(a):
+        def load_wg(dst, c0, c1):
+            nc.sync.dma_start(dst[:], wg_words[:, :, 2 * c0 : 2 * c1].bitcast(I32).rearrange("a p n -> p a n"))
+
+        def load_wu(dst, a, c0, c1):
+            nc.sync.dma_start(dst, wu[PASS * a : PASS * (a + 1), c0:c1].rearrange("(p i) c -> p i c", i=4))
+
+        for a in range(2):
             nc.sync.dma_start(tab_w[a][:], tab_words[a].rearrange("p n i -> p (n i)").bitcast(I32))
+        load_wg(wg_raw[0], 0, PASS)
+        wg_rows_by_r = wg_scales.rearrange("a (q r) n -> r q a n", r=4)
+        for r in range(4):
+            nc.sync.dma_start(wg_sc_raw[r:P:32, :, :], wg_rows_by_r[r].bitcast(I32))
+        load_wu(wu_pair[0], 0, 0, 256)
 
-        def load_wg(b):
-            wg_raw[b] = tile("wg_raw0", [P, 2, 256], I32) if b == 0 else placed("wg_raw1", [P, 2, 256], I32, 40)
-            nc.sync.dma_start(wg_raw[b][:], wg_words[:, :, 1024 * b : 1024 * (b + 1)].bitcast(I32).rearrange("a p n -> p a n"))
-
-        def load_wu(a, b):
-            if b == 0:
-                wu_raw[a][b] = placed("wu_raw00", [P, 4, PASS], F32, 16)
-            elif a == 0:
-                wu_raw[a][b] = placed("wu_raw01", [P, 4, PASS], F32, 42)
-            else:
-                wu_raw[a][b] = tile("wu_raw11", [P, 4, PASS], F32, "load1")
-            rows = wu[PASS * a : PASS * (a + 1), PASS * b : PASS * (b + 1)]
-            nc.sync.dma_start(wu_raw[a][b][:], rows.rearrange("(p i) c -> p i c", i=4))
-
-        def load_wu_half(u):
-            rows = wu[PASS : 2 * PASS, 256 * u : 256 * (u + 1)]
-            nc.sync.dma_start(wu_half[u], rows.rearrange("(p i) c -> p i c", i=4))
-
-        def load_w2(b):
-            w2_raw[b] = placed("w2_raw%d" % b, [P, 4, N], F32, (16, 1)[b])
-            if b == 0:
-                nc.sync.dma_start(w2_raw[b][:], w2[0:PASS, :].rearrange("(p t) n -> p t n", t=4))
-            else:
-                rows = w2[PASS:H, :].rearrange("(g t j) n -> t g j n", t=4, j=8)
-                for t in range(4):
-                    nc.sync.dma_start(w2_raw[b][:, t, :], rows[t])
-
-        load_tab(0)
-        load_wg(0)
-        load_tab(1)
-        for q in range(4):
-            nc.sync.dma_start(
-                wg_sc_raw[32 * q : 32 * q + 4, :, :],
-                wg_scales[:, 4 * q : 4 * q + 4, :].bitcast(I32).rearrange("a r n -> r a n"),
-            )
-        nc.sync.dma_start(pos1_sb[:], pos1)
-        nc.sync.dma_start(pos2_sb[:], pos2)
-
-        for q in range(4):
-            nc.vector.tensor_copy(tab_sc[32 * q : 32 * q + 8, :].bitcast(I32), tab_sc_rows[32 * q : 32 * q + 8, :])
-        load_wu(0, 0)
         nc.vector.tensor_copy(v_sc[:], tab_sc[:].indirect(offs_sb[:]))
-        nc.sync.dma_start(v_sc1[0:112, :].bitcast(I32), v_sc[4:116, :].bitcast(I32))
-        for u in range(2):
-            load_wu_half(u)
+        nc.sync.dma_start(v_sc1[0:112, :].bitcast(I32), v_sc[16:P, :].bitcast(I32))
+        for a in range(2):
+            for u in range(2):
+                nc.vector.tensor_copy(v_w[a][u][:], tab_w[a][:].bitcast(U32).indirect(offs_sb[:, 32 * u : 32 * (u + 1)]))
 
-        def gather_words(a, u):
-            nc.vector.tensor_copy(v_w[a][u][:], tab_w[a][:].bitcast(U32).indirect(offs_sb[:, 32 * u : 32 * (u + 1)]))
-
-        gather_words(0, 0)
-        load_wg(1)
-        load_wu(0, 1)
+        load_wu(wu_pair[1], 1, 0, 256)
+        load_wg(wg_raw[1], PASS, H)
+        for k in (2, 3):
+            for a in range(2):
+                load_wu(wu_one[a, k], a, P * k, P * (k + 1))
+        for a in range(2):
+            load_wu(wu_late[a], a, PASS, H)
+        nc.sync.dma_start(w2_raw[0], w2[0:PASS, :].rearrange("(p t) n -> p t n", t=4))
+        w2_rows = w2[PASS:H, :].rearrange("(g t j) n -> t g j n", t=4, j=8)
+        for t in range(4):
+            nc.sync.dma_start(w2_raw[1][:, t, :], w2_rows[t])
 
         def order_wg():
             nc.vector.tensor_copy(
@@ -168,62 +169,39 @@ def tile_list_gated_token_merge_kernel(tc, tab_words, tab_scales, offs, wg_words
                 wg_sc_raw[:, :, 128:256].rearrange("p a (g t w) -> p a t g w", t=4, w=2),
             )
 
-        def rounded_wu(a, b, t):
-            u, e = divmod(t, 2)
-            if (a, b, t) == (1, 0, 0):
-                return wu_bf_late[:]
-            if (a, b, t) == (1, 0, 1):
-                return rounded_wu(1, 0, 3)
-            if b == 1:
-                return wu_bf[b, u][:, 1024 * e + 512 * a : 1024 * e + 512 * (a + 1)]
-            return wu_bf[b, u][:, 1024 * a + 512 * e : 1024 * a + 512 * (e + 1)]
-
-        def wu_cols(a, b, t):
-            at = 256 * (t % 2) + P * a if b == 1 else 256 * a + P * (t % 2)
-            return slice(at, at + P)
-
-        def raw_wu(a, t):
-            if a == 0:
-                return wu_raw[0][0][:, :, P * t : P * (t + 1)]
-            return wu_half[t // 2][:, :, P * (t % 2) : P * (t % 2 + 1)]
-
-        def round_wu_scalar(a, b, t):
-            dst = rounded_wu(a, b, t).rearrange("p (g h j i) -> p g h i j", h=2, j=4, i=4)
-            if b == 0:
-                nc.scalar.copy(dst, raw_wu(a, t).rearrange("p i (g h j) -> p g h i j", h=2, j=4))
+        def round_wu(a, k, engine):
+            dst = wu_bf[k][:, 512 * a : 512 * (a + 1)]
+            if k < 4:
+                src = wu_pair[a][:, :, P * k : P * (k + 1)] if k < 2 else wu_one[a, k]
+                if engine is nc.gpsimd:
+                    return round_gpsimd(dst, src)
+                src = src.rearrange("p i (g h j) -> p g h i j", h=2, j=4)
             else:
-                nc.scalar.copy(dst, wu_raw[a][b][:].rearrange("p i (g t h j) -> p t g h i j", t=4, h=2, j=4)[:, t])
+                src = wu_late[a].rearrange("p i (g t h j) -> p t g h i j", t=4, h=2, j=4)[:, k - 4]
+            dst = dst.rearrange("p (g h j i) -> p g h i j", h=2, j=4, i=4)
+            if engine is nc.scalar:
+                return nc.scalar.copy(dst, src)
+            return nc.vector.tensor_copy(dst, src)
 
-        def round_wu_vector(a, t):
-            nc.vector.tensor_copy(
-                rounded_wu(a, 0, t).rearrange("p (c i) -> p c i", i=4), raw_wu(a, t).rearrange("p i c -> p c i")
-            )
+        def quant_wu_pass(k, a):
+            cols = slice(P * a, P * (a + 1))
+            nc.vector.quantize_mx(wu_w[k][:, cols].bitcast(FP8X4), wu_sc[k][:, cols], wu_bf[k][:, 512 * a : 512 * (a + 1)])
 
-        def round_wu_gpsimd(a, t):
-            nc.gpsimd.tensor_scalar(
-                rounded_wu(a, 0, t).rearrange("p (c i) -> p c i", i=4),
-                raw_wu(a, t).rearrange("p i c -> p c i"),
-                1.0,
-                0.0,
-                ALU.mult,
-                ALU.add,
-            )
-
-        def quant_wu(b, u, cols, rounded):
-            nc.vector.quantize_mx(wu_w[b, u][:, cols].bitcast(FP8X4), wu_sc[b, u][:, cols], rounded)
-
-        def quant_wu_slice(t):
-            u, e = divmod(t, 2)
-            quant_wu(1, u, slice(256 * e, 256 * (e + 1)), wu_bf[1, u][:, 1024 * e : 1024 * (e + 1)])
+        def quant_wu(k):
+            nc.vector.quantize_mx(wu_w[k][:].bitcast(FP8X4), wu_sc[k][:], wu_bf[k])
 
         def round_w2(b, u):
             nc.scalar.copy(
-                w2_bf[b][:, 1024 * u : 1024 * (u + 1)].rearrange("p (c j t) -> p c t j", j=4, t=4),
+                w2_bf[b][u].rearrange("p (c j t) -> p c t j", j=4, t=4),
                 w2_raw[b][:, :, 256 * u : 256 * (u + 1)].rearrange("p t (c j) -> p c t j", j=4),
             )
 
-        def quant_w2(b):
-            nc.vector.quantize_mx(w2_w[b][:].bitcast(FP8X4), w2_sc[b][:], w2_bf[b][:])
+        def round_gpsimd(dst, src):
+            dst, src = dst.rearrange("p (c i) -> p c i", i=4), src.rearrange("p i c -> p c i")
+            nc.gpsimd.tensor_scalar(dst, src, 1.0, 0.0, ALU.mult, ALU.add)
+
+        def quant_w2(words, scales, rounded):
+            nc.vector.quantize_mx(words.bitcast(FP8X4), scales, rounded)
 
         def gate_pass(k, u, a):
             b, t = divmod(k, 4)
@@ -243,16 +221,15 @@ def tile_list_gated_token_merge_kernel(tc, tab_words, tab_scales, offs, wg_words
                 nc.scalar.activation(silu[k][u], bank_b[k, u][:], ACT.Silu)
 
         def up_pass(k, u, a):
-            b, t = divmod(k, 4)
-            cols = slice(BANK * u, BANK * (u + 1))
+            cols = slice(P * a, P * (a + 1))
             if a == 0:
                 bank_a[k, u] = bank("bank_a%d%d" % (k, u), "a%d%d" % (k % 2, u))
             nc.tensor.matmul_mx(
                 bank_a[k, u][:],
-                lhsT=wu_w[b, t // 2][:, wu_cols(a, b, t)].bitcast(FP8X4),
-                lhsT_scale=wu_sc[b, t // 2][:, wu_cols(a, b, t)],
+                lhsT=wu_w[k][:, cols].bitcast(FP8X4),
+                lhsT_scale=wu_sc[k][:, cols],
                 rhs=v_w[a][u][:].bitcast(FP8X4),
-                rhs_scale=v_sc[4 * a : P, cols],
+                rhs_scale=(v_sc, v_sc1)[a][:, BANK * u : BANK * (u + 1)],
                 start=(a == 0),
                 stop=(a == 1),
             )
@@ -260,34 +237,31 @@ def tile_list_gated_token_merge_kernel(tc, tab_words, tab_scales, offs, wg_words
         def product_vector(k, u):
             nc.vector.tensor_tensor(hs[k][:, BANK * u : BANK * (u + 1)], bank_a[k, u][:], silu[k][u], ALU.mult)
 
+        def park(k):
+            nc.scalar.copy(parked[k], bank_a[k, 0][:])
+
         def product_gpsimd(k):
-            parked = hs[k][:, S + BANK : 2 * S]
-            nc.scalar.copy(parked, bank_a[k, 0][:])
-            nc.gpsimd.tensor_tensor(hs[k][:, 0:BANK], parked, silu[k][0], ALU.mult)
+            nc.gpsimd.tensor_tensor(hs[k][:, 0:BANK], parked[k], silu[k][0], ALU.mult)
 
         def pick_first(k):
             nc.vector.tensor_scalar(first[k], hs[k][:].indirect(pos1_sb[:]), W1 / W2, 0.0, ALU.mult, ALU.add)
 
         def pick_second(k):
-            b, t = divmod(k, 4)
-            total = z_rows[t][:] if b == 0 else z_f[1][:, t, :]
-            nc.vector.tensor_tensor(total, hs[k][:].indirect(pos2_sb[:]), first[k], ALU.add)
-            if b == 0:
-                for i in range(4):
-                    nc.sync.dma_start(z_f[0][32 * t : 32 * (t + 1), i, :], z_rows[t][i:P:4, :])
+            nc.vector.tensor_tensor(z_rows[k], hs[k][:].indirect(pos2_sb[:]), first[k], ALU.add)
+            for i in range(4):
+                nc.sync.dma_start(z_f0[32 * k : 32 * (k + 1), i, :], z_rows[k][i:P:4, :])
 
         def pick_second_part(k, u):
-            cols = slice(PART * u, PART * (u + 1))
             picked = hs[k][:].indirect(pos2_sb[:, 16 * u : 16 * (u + 1)])
-            nc.vector.tensor_tensor(z_f[1][:, k - 4, cols], picked, first[k][:, cols], ALU.add)
+            nc.vector.tensor_tensor(z_f[1][u][:, k - 4, :], picked, first[k][:, PART * u : PART * (u + 1)], ALU.add)
 
         def rounded_z(b, m0, m1):
-            at = 4 * m0 - (2 * PART if b == 1 and m0 >= PART else 0)
-            return z_bf[b][:, at : at + 4 * (m1 - m0)]
+            return z_bf[b][:, 4 * m0 : 4 * m1]
 
         def round_z(b, m0, m1, on_vector):
             dst = rounded_z(b, m0, m1).rearrange("p (c j t) -> p c t j", j=4, t=4)
-            src = z_f[b][:, :, m0:m1].rearrange("p t (c j) -> p c t j", j=4)
+            u = m0 // PART
+            src = z_f[b][u][:, :, m0 - PART * u : m1 - PART * u].rearrange("p t (c j) -> p c t j", j=4)
             if on_vector:
                 nc.vector.tensor_scalar(dst, src, W2, 0.0, ALU.mult, ALU.add)
             else:
@@ -303,7 +277,7 @@ def tile_list_gated_token_merge_kernel(tc, tab_words, tab_scales, offs, wg_words
                 rows = slice(P * n, P * (n + 1))
                 nc.tensor.matmul_mx(
                     bank_o[u][n // 2][:, PART * (n % 2) : PART * (n % 2 + 1)],
-                    lhsT=w2_w[b][:, rows].bitcast(FP8X4),
+                    lhsT=w2_w[b][n // 2][:, P * (n % 2) : P * (n % 2 + 1)].bitcast(FP8X4),
                     lhsT_scale=w2_sc[b][:, rows],
                     rhs=z_w[b][:, PART * u : PART * (u + 1)].bitcast(FP8X4),
                     rhs_scale=z_sc[b][:, PART * u : PART * (u + 1)],
@@ -319,86 +293,101 @@ def tile_list_gated_token_merge_kernel(tc, tab_words, tab_scales, offs, wg_words
             dst = out[2 * P * i : 2 * P * (i + 1), PART * u : PART * (u + 1)].rearrange("(n p) m -> p n m", p=P)
             nc.sync.dma_start(dst, res[u][i][:].rearrange("p (n m) -> p n m", n=2))
 
-        gather_words(0, 1)
+        for a in range(2):
+            for u in range(2):
+                gate_pass(0, u, a)
+        round_wu(0, 0, nc.scalar)
+        round_wu(0, 1, nc.gpsimd)
+        quant_wu_pass(0, 0)
         for u in range(2):
-            for k in range(2):
-                gate_pass(k, u, 0)
-        for u in range(2):
-            gather_words(1, u)
-        for t in range(2):
-            round_wu_scalar(0, 0, t)
-        round_wu_gpsimd(0, 2)
-        quant_wu(0, 0, slice(0, 256), wu_bf[0, 0][:])
-        load_wu(1, 1)
+            up_pass(0, u, 0)
         for k in range(2):
-            for u in range(2):
-                gate_pass(k, u, 1)
-            for u in range(2):
-                up_pass(k, u, 0)
-            round_wu_vector(1, k)
-            if k == 1:
-                order_wg_scales()
-            quant_wu(0, 0, wu_cols(1, 0, k), rounded_wu(1, 0, k))
-            for u in range(2):
-                up_pass(k, u, 1)
-        round_wu_scalar(0, 0, 3)
-        load_w2(0)
-        round_wu_vector(1, 2)
-        round_wu_scalar(1, 0, 3)
-        load_w2(1)
+            round_wu(1, k, nc.vector)
+        quant_wu_pass(0, 1)
+        for u in range(2):
+            up_pass(0, u, 1)
+        quant_wu(1)
+        for u in range(2):
+            for a in range(2):
+                gate_pass(1, u, a)
+        order_wg_scales()
+        order_wg()
         for u in range(2):
             product_vector(0, u)
-        order_wg()
-        quant_wu(0, 1, slice(0, 512), wu_bf[0, 1][:])
+        round_wu(0, 2, nc.gpsimd)
+        round_wu(1, 2, nc.scalar)
+        quant_wu(2)
 
+        for a in range(2):
+            up_pass(1, 0, a)
+        park(1)
+        product_gpsimd(1)
         for k in range(SLICES):
-            if k + 1 < SLICES:
-                if k > 0:
-                    for a in range(2):
-                        gate_pass(k + 1, 0, a)
-                    for a in range(2):
-                        up_pass(k + 1, 0, a)
-                product_gpsimd(k + 1)
-                if k + 2 < SLICES:
-                    for a in range(2):
-                        gate_pass(k + 2, 1, a)
-                if k < 4:
-                    for e in range(2):
-                        round_wu_scalar(k % 2, 1, 2 * (k // 2) + e)
-                elif k + 2 < SLICES:
-                    round_w2(0, k - 4)
-                else:
-                    for u in range(2):
-                        round_w2(1, u)
-                    for u in range(2):
-                        round_z(0, PART * u, PART * (u + 1), False)
             pick_first(k)
             if k + 1 < SLICES:
-                if k > 0:
+                for u in (0, 1) if k + 1 == 4 else (1,):
                     for a in range(2):
-                        up_pass(k + 1, 1, a)
-                product_vector(k + 1, 1)
+                        up_pass(k + 1, u, a)
+                    product_vector(k + 1, u)
             if k + 2 < SLICES:
+                for a in range(2):
+                    gate_pass(k + 2, 0, a)
+                if k + 2 != 4:
+                    for a in range(2):
+                        up_pass(k + 2, 0, a)
+                    park(k + 2)
+            if k < 4:
                 pick_second(k)
             elif k + 1 < SLICES:
                 pick_second_part(k, 0)
-            if 1 <= k <= 4:
-                quant_wu_slice(k - 1)
-            if k in (5, 6):
-                quant_w2(k - 5)
+            if k == 2:
+                for a in range(2):
+                    for j in (4, 5):
+                        round_wu(a, j, nc.scalar)
+                quant_wu(4)
+                round_gpsimd(w2_bf[0][1], w2_raw[0][:, :, 256:N])
+            elif k == 0:
+                for a in range(2):
+                    round_wu(a, 3, nc.scalar)
+            if k in (0, 2, 3, 4):
+                quant_wu(k + 3)
+            elif k == 5:
+                quant_w2(w2_w[0][0], w2_sc[0][:, 0:256], w2_bf[0][0])
+            elif k == 6:
+                quant_w2(w2_w[0][1], w2_sc[0][:, 256:N], w2_bf[0][1])
+            elif k == 7:
+                quant_z(0, 0, M)
+                quant_w2(w2_w1[:], w2_sc[1][:], w2_bf1[:])
+            if k + 2 < SLICES:
+                if k + 2 != 4:
+                    product_gpsimd(k + 2)
+                for a in range(2):
+                    gate_pass(k + 2, 1, a)
+            if k == 2:
+                for j in (6, 7):
+                    for a in range(2):
+                        round_wu(a, j, nc.scalar)
+            if k == 4:
+                round_w2(0, 0)
+            if k == 5:
+                for u in range(2):
+                    round_z(0, PART * u, PART * (u + 1), False)
+                for u in range(2):
+                    round_w2(1, u)
 
-        quant_z(0, 0, M)
-        for u in range(2):
-            down(0, u)
         pick_second_part(SLICES - 1, 0)
         round_z(1, 0, PART, False)
-        for k in (SLICES - 2, SLICES - 1):
-            pick_second_part(k, 1)
-        round_z(1, PART + P, M, False)
         for u in range(2):
-            if u == 1:
-                round_z(1, PART, PART + P, True)
-            quant_z(1, PART * u, PART * (u + 1))
-            down(1, u)
-            for i in range(2):
-                store(u, i, (u, i) == (1, 0))
+            down(0, u)
+        for k in (5, 6, 7):
+            pick_second_part(k, 1)
+        quant_z(1, 0, PART)
+        down(1, 0)
+        for i in range(2):
+            store(0, i, False)
+        pick_second_part(4, 1)
+        round_z(1, PART, M, True)
+        quant_z(1, PART, M)
+        down(1, 1)
+        for i in range(2):
+            store(1, i, i == 0)

@@ -64,35 +64,26 @@ def tile_list_gated_token_merge_kernel(tc, tab_words, tab_scales, offs, wg_words
         w2_raw = [raw_part(6144 + 2048 * b, N) for b in range(2)]
         ring = [tile("hs%d" % r, [P, 2 * S], F32) for r in range(RING)]
         hs = [ring[k % RING] for k in range(SLICES + 2)]
-        first = [hs[k + 2][:, S : S + M] for k in range(SLICES)]
-        first[1] = hs[3][:, 0:M]
-        first[4] = hs[6][:, S + PART : S + PART + M]
-        first[6:8] = [tile("first%d" % k, [P, M], F32)[:] for k in (6, 7)]
+        first = [hs[k + 2][:, BANK:S] for k in range(4)] + [hs[k + 2][:, S - PART : S + PART] for k in (4, 5)]
+        first += [placed("first6", [P, M], F32, 66)[:], tile("first7", [P, M], F32)[:]]
         z_late = tile("z_late", [P, 5 * M + P], F32)
         z_rows = [placed("z_rows0", [P, M], F32, 51)[:]] + [tile("z_rows%d" % k, [P, M], F32)[:] for k in (1, 2)]
-        z_rows.append(placed("z_rows3", [P, M], F32, 60)[:])
-        parked = [None, placed("parked1", [P, BANK], F32, 52)[:]] + z_rows[1:3] + [None]
-        parked += [z_late[:, M * t : M * (t + 1)] for t in range(3)]
-        silu = [[hs[0][:, S + BANK : 2 * S], hs[2][:, 256:768]]]
-        for k in range(1, SLICES):
-            silu.append([placed("silu%d" % k, [P, BANK], F32, 54 + 2 * k + 8 * (k == 7))[:], hs[k - 1][:, S : S + BANK]])
-        wu_bf = {k: hs[k - 1][:, 256:768].bitcast(BF16) for k in (2, 3, 6, 7)}
+        z_rows.append(placed("z_rows3", [P, M], F32, 61)[:])
+        parked = [hs[k][:, S : S + BANK] for k in range(6)] + [tile("parked%d" % k, [P, BANK], F32)[:] for k in (6, 7)]
+        silu = [[hs[0][:, S : S + BANK], hs[2][:, 0:BANK]]]
+        for k, at in zip(range(1, SLICES), (56, 58, 62, 63, 66, 68, 76)):
+            own = placed("silu%d" % k, [P, S if k == 7 else BANK], F32, at)
+            silu.append([hs[k - 1][:, S + BANK : 2 * S], own[:, 0:BANK]])
+        wu_bf = {k: hs[k - 1][:, 0:BANK].bitcast(BF16) for k in (3, 6, 7)}
         wu_bf.update({k: tile("wu_bf%d" % k, [P, 1024], BF16)[:] for k in (0, 1)})
+        wu_bf[2] = hs[1][:, 256:768].bitcast(BF16)
         wu_bf[4] = placed("wu_bf4", [P, 1024], BF16, 70)[:]
         wu_bf[5] = first[3].bitcast(BF16)
-        wu_w = {k: placed("wu_w%d" % k, [P, 256], U32, at) for k, at in ((3, 56), (4, 60), (6, 62), (7, 64))}
+        wu_w = {k: placed("wu_w%d" % k, [P, 256], U32, at) for k, at in ((3, 56), (4, 62), (6, 64), (7, 66))}
         wu_w.update({k: tile("wu_w%d" % k, [P, 256], U32) for k in (0, 1, 2, 5)})
         wu_sc = {k: tile("wu_sc%d" % k, [P, 256], U8) for k in range(SLICES)}
-        w2_bf1 = tile("w2_bf1", [P, 4 * N], BF16)
-        w2_bf = [
-            [hs[7][:, 256:768].bitcast(BF16), placed("w2_bf01", [P, 1024], BF16, 70)[:]],
-            [w2_bf1[:, 0:1024], w2_bf1[:, 1024:2048]],
-        ]
-        w2_w1 = placed("w2_w1", [P, N], U32, 77.5)
-        w2_w = [
-            [placed("w2_w00", [P, 256], U32, 66)[:], placed("w2_w01", [P, 256], U32, 76.5)[:]],
-            [w2_w1[:, 0:256], w2_w1[:, 256:N]],
-        ]
+        w2_bf = [placed("w2_bf0", [P, 4 * N], BF16, 70), tile("w2_bf1", [P, 4 * N], BF16)]
+        w2_w = [placed("w2_w%d" % b, [P, N], U32, 77 + 2.5 * b) for b in range(2)]
         w2_sc = [tile("w2_sc%d" % b, [P, N], U8) for b in range(2)]
         z_f0 = tile("z_f0", [P, 4, M], F32)
         z_f = [
@@ -114,7 +105,7 @@ def tile_list_gated_token_merge_kernel(tc, tab_words, tab_scales, offs, wg_words
 
         nc.vector.memset(tab_sc[:].bitcast(I32), 0)
         nc.vector.memset(wg_sc_raw[:], 0)
-        for sb_list, dram_list in ((offs_sb, offs), (pos1_sb, pos1), (pos2_sb, pos2)):
+        for sb_list, dram_list in ((offs_sb, offs), (pos1_sb, pos1)):
             nc.sync.dma_start(sb_list[:], dram_list)
         rows_by_r = tab_scales.rearrange("a (q r) n -> r q a n", r=4)
         for r in range(4):
@@ -122,8 +113,6 @@ def tile_list_gated_token_merge_kernel(tc, tab_words, tab_scales, offs, wg_words
         nc.vector.memset(warm[:, 0:8], 0.0)
         nc.scalar.activation(warm[:, 8:16], warm[:, 0:8], ACT.Silu)
         nc.vector.memset(v_sc1[:].bitcast(I32), 0)
-        for r in (1, 2, 3):
-            nc.vector.memset(ring[r][:, S + BANK : 2 * S], 0.0)
 
         def load_wg(dst, c0, c1):
             nc.sync.dma_start(dst[:], wg_words[:, :, 2 * c0 : 2 * c1].bitcast(I32).rearrange("a p n -> p a n"))
@@ -147,6 +136,7 @@ def tile_list_gated_token_merge_kernel(tc, tab_words, tab_scales, offs, wg_words
 
         load_wu(wu_pair[1], 1, 0, 256)
         load_wg(wg_raw[1], PASS, H)
+        nc.sync.dma_start(pos2_sb[:], pos2)
         for k in (2, 3):
             for a in range(2):
                 load_wu(wu_one[a, k], a, P * k, P * (k + 1))
@@ -192,7 +182,7 @@ def tile_list_gated_token_merge_kernel(tc, tab_words, tab_scales, offs, wg_words
 
         def round_w2(b, u):
             nc.scalar.copy(
-                w2_bf[b][u].rearrange("p (c j t) -> p c t j", j=4, t=4),
+                w2_bf[b][:, 1024 * u : 1024 * (u + 1)].rearrange("p (c j t) -> p c t j", j=4, t=4),
                 w2_raw[b][:, :, 256 * u : 256 * (u + 1)].rearrange("p t (c j) -> p c t j", j=4),
             )
 
@@ -200,14 +190,14 @@ def tile_list_gated_token_merge_kernel(tc, tab_words, tab_scales, offs, wg_words
             dst, src = dst.rearrange("p (c i) -> p c i", i=4), src.rearrange("p i c -> p c i")
             nc.gpsimd.tensor_scalar(dst, src, 1.0, 0.0, ALU.mult, ALU.add)
 
-        def quant_w2(words, scales, rounded):
-            nc.vector.quantize_mx(words.bitcast(FP8X4), scales, rounded)
+        def quant_w2(b):
+            nc.vector.quantize_mx(w2_w[b][:].bitcast(FP8X4), w2_sc[b][:], w2_bf[b][:])
 
         def gate_pass(k, u, a):
             b, t = divmod(k, 4)
             cols = slice(BANK * u, BANK * (u + 1))
             if a == 0:
-                bank_b[k, u] = bank("bank_b%d%d" % (k, u), "b%d%d" % (k % 2, u))
+                bank_b[k, u] = bank("bank_b%d%d" % (k, u), "%d%d%d" % (k >= 2, k % 2, u))
             nc.tensor.matmul_mx(
                 bank_b[k, u][:],
                 lhsT=(wg_raw[0], wg_w1)[b][:, a, 64 * t : 64 * (t + 1)].bitcast(FP4X4),
@@ -223,7 +213,7 @@ def tile_list_gated_token_merge_kernel(tc, tab_words, tab_scales, offs, wg_words
         def up_pass(k, u, a):
             cols = slice(P * a, P * (a + 1))
             if a == 0:
-                bank_a[k, u] = bank("bank_a%d%d" % (k, u), "a%d%d" % (k % 2, u))
+                bank_a[k, u] = bank("bank_a%d%d" % (k, u), "%d%d%d" % (k < 2, k % 2, u))
             nc.tensor.matmul_mx(
                 bank_a[k, u][:],
                 lhsT=wu_w[k][:, cols].bitcast(FP8X4),
@@ -238,10 +228,10 @@ def tile_list_gated_token_merge_kernel(tc, tab_words, tab_scales, offs, wg_words
             nc.vector.tensor_tensor(hs[k][:, BANK * u : BANK * (u + 1)], bank_a[k, u][:], silu[k][u], ALU.mult)
 
         def park(k):
-            nc.scalar.copy(parked[k], bank_a[k, 0][:])
+            nc.scalar.copy(parked[k], bank_a[k, 1][:])
 
         def product_gpsimd(k):
-            nc.gpsimd.tensor_tensor(hs[k][:, 0:BANK], parked[k], silu[k][0], ALU.mult)
+            nc.gpsimd.tensor_tensor(hs[k][:, BANK:S], parked[k], silu[k][1], ALU.mult)
 
         def pick_first(k):
             nc.vector.tensor_scalar(first[k], hs[k][:].indirect(pos1_sb[:]), W1 / W2, 0.0, ALU.mult, ALU.add)
@@ -272,12 +262,12 @@ def tile_list_gated_token_merge_kernel(tc, tab_words, tab_scales, offs, wg_words
 
         def down(b, u):
             if b == 0:
-                bank_o[u] = [bank("bank_o%d%d" % (u, i), "%s0%d" % ("ba"[u], i)) for i in range(2)]
+                bank_o[u] = [bank("bank_o%d%d" % (u, i), "%d0%d" % (1 - u, i)) for i in range(2)]
             for n in range(4):
                 rows = slice(P * n, P * (n + 1))
                 nc.tensor.matmul_mx(
                     bank_o[u][n // 2][:, PART * (n % 2) : PART * (n % 2 + 1)],
-                    lhsT=w2_w[b][n // 2][:, P * (n % 2) : P * (n % 2 + 1)].bitcast(FP8X4),
+                    lhsT=w2_w[b][:, rows].bitcast(FP8X4),
                     lhsT_scale=w2_sc[b][:, rows],
                     rhs=z_w[b][:, PART * u : PART * (u + 1)].bitcast(FP8X4),
                     rhs_scale=z_sc[b][:, PART * u : PART * (u + 1)],
@@ -307,7 +297,7 @@ def tile_list_gated_token_merge_kernel(tc, tab_words, tab_scales, offs, wg_words
         for u in range(2):
             up_pass(0, u, 1)
         quant_wu(1)
-        for u in range(2):
+        for u in (1, 0):
             for a in range(2):
                 gate_pass(1, u, a)
         order_wg_scales()
@@ -319,22 +309,22 @@ def tile_list_gated_token_merge_kernel(tc, tab_words, tab_scales, offs, wg_words
         quant_wu(2)
 
         for a in range(2):
-            up_pass(1, 0, a)
+            up_pass(1, 1, a)
         park(1)
         product_gpsimd(1)
         for k in range(SLICES):
             pick_first(k)
             if k + 1 < SLICES:
-                for u in (0, 1) if k + 1 == 4 else (1,):
+                for u in (0, 1) if k + 1 == 4 else (0,):
                     for a in range(2):
                         up_pass(k + 1, u, a)
                     product_vector(k + 1, u)
             if k + 2 < SLICES:
                 for a in range(2):
-                    gate_pass(k + 2, 0, a)
+                    gate_pass(k + 2, 1, a)
                 if k + 2 != 4:
                     for a in range(2):
-                        up_pass(k + 2, 0, a)
+                        up_pass(k + 2, 1, a)
                     park(k + 2)
             if k < 4:
                 pick_second(k)
@@ -345,31 +335,28 @@ def tile_list_gated_token_merge_kernel(tc, tab_words, tab_scales, offs, wg_words
                     for j in (4, 5):
                         round_wu(a, j, nc.scalar)
                 quant_wu(4)
-                round_gpsimd(w2_bf[0][1], w2_raw[0][:, :, 256:N])
+                round_gpsimd(w2_bf[0][:, 1024:2048], w2_raw[0][:, :, 256:N])
             elif k == 0:
                 for a in range(2):
                     round_wu(a, 3, nc.scalar)
             if k in (0, 2, 3, 4):
                 quant_wu(k + 3)
-            elif k == 5:
-                quant_w2(w2_w[0][0], w2_sc[0][:, 0:256], w2_bf[0][0])
             elif k == 6:
-                quant_w2(w2_w[0][1], w2_sc[0][:, 256:N], w2_bf[0][1])
+                quant_w2(0)
             elif k == 7:
                 quant_z(0, 0, M)
-                quant_w2(w2_w1[:], w2_sc[1][:], w2_bf1[:])
+                quant_w2(1)
             if k + 2 < SLICES:
                 if k + 2 != 4:
                     product_gpsimd(k + 2)
                 for a in range(2):
-                    gate_pass(k + 2, 1, a)
+                    gate_pass(k + 2, 0, a)
             if k == 2:
                 for j in (6, 7):
                     for a in range(2):
                         round_wu(a, j, nc.scalar)
-            if k == 4:
-                round_w2(0, 0)
             if k == 5:
+                round_w2(0, 0)
                 for u in range(2):
                     round_z(0, PART * u, PART * (u + 1), False)
                 for u in range(2):

@@ -22,6 +22,7 @@ BANK = 512
 SLICES = H // P
 PART = M // 2
 W1, W2 = 0.7, 0.3
+EARLY, MIDDLE, LAST = PARTS = (0, 256, 2), (384, 512, 1), (256, 384, 2)
 RING = 4
 
 
@@ -65,38 +66,40 @@ def tile_list_gated_token_merge_kernel(tc, tab_words, tab_scales, offs, wg_words
         ring = [tile("hs%d" % r, [P, 2 * S], F32) for r in range(RING)]
         hs = [ring[k % RING] for k in range(SLICES + 2)]
         first = [hs[k + 2][:, BANK:S] for k in range(4)] + [hs[k + 2][:, S - PART : S + PART] for k in (4, 5)]
+        first[2] = placed("first2", [P, M], F32, 56)[:]
         first += [placed("first6", [P, M], F32, 66)[:], tile("first7", [P, M], F32)[:]]
-        z_late = tile("z_late", [P, 5 * M + P], F32)
+        z_late = tile("z_late", [P, 7 * M - P], F32)
         z_rows = [placed("z_rows0", [P, M], F32, 51)[:]] + [tile("z_rows%d" % k, [P, M], F32)[:] for k in (1, 2)]
-        z_rows.append(placed("z_rows3", [P, M], F32, 61)[:])
-        parked = [hs[k][:, S : S + BANK] for k in range(6)] + [tile("parked%d" % k, [P, BANK], F32)[:] for k in (6, 7)]
+        z_rows.append(placed("z_rows3", [P, M], F32, 92)[:])
+        parked = [hs[k][:, S : S + BANK] for k in range(6)] + [hs[7][:, 0:BANK], tile("parked7", [P, BANK], F32)[:]]
         silu = [[hs[0][:, S : S + BANK], hs[2][:, 0:BANK]]]
-        for k, at in zip(range(1, SLICES), (56, 58, 62, 63, 66, 68, 76)):
+        for k, at in zip(range(1, SLICES), (56, 58, 62, 64, 66, 68, 76)):
             own = placed("silu%d" % k, [P, S if k == 7 else BANK], F32, at)
             silu.append([hs[k - 1][:, S + BANK : 2 * S], own[:, 0:BANK]])
+        silu[4][0] = placed("silu40", [P, BANK], F32, 92)[:]
         wu_bf = {k: hs[k - 1][:, 0:BANK].bitcast(BF16) for k in (3, 6, 7)}
         wu_bf.update({k: tile("wu_bf%d" % k, [P, 1024], BF16)[:] for k in (0, 1)})
         wu_bf[2] = hs[1][:, 256:768].bitcast(BF16)
-        wu_bf[4] = placed("wu_bf4", [P, 1024], BF16, 70)[:]
-        wu_bf[5] = first[3].bitcast(BF16)
-        wu_w = {k: placed("wu_w%d" % k, [P, 256], U32, at) for k, at in ((3, 56), (4, 62), (6, 64), (7, 66))}
-        wu_w.update({k: tile("wu_w%d" % k, [P, 256], U32) for k in (0, 1, 2, 5)})
-        wu_sc = {k: tile("wu_sc%d" % k, [P, 256], U8) for k in range(SLICES)}
-        w2_bf = [placed("w2_bf0", [P, 4 * N], BF16, 70), tile("w2_bf1", [P, 4 * N], BF16)]
+        wu_bf45 = hs[5][:, BANK : S + BANK].bitcast(BF16)
+        wu_w = {k: placed("wu_w%d" % k, [P, 256], U32, at) for k, at in ((0, 46), (2, 46), (3, 56), (6, 64), (7, 66))}
+        wu_w[1] = tile("wu_w1", [P, 256], U32)
+        wu_sc = {k: tile("wu_sc%d" % k, [P, 256], U8) for k in (0, 1, 2, 3, 6, 7)}
+        wu_w45, wu_sc45 = placed("wu_w45", [P, 2, 256], U32, 61), tile("wu_sc45", [P, 2, 256], U8)
+        wu_w.update({k: wu_w45[:, k - 4, :] for k in (4, 5)})
+        wu_sc.update({k: wu_sc45[:, k - 4, :] for k in (4, 5)})
+        w2_bf = [placed("w2_bf0", [P, 4 * N], BF16, 57), tile("w2_bf1", [P, 4 * N], BF16)]
         w2_w = [placed("w2_w%d" % b, [P, N], U32, 77 + 2.5 * b) for b in range(2)]
         w2_sc = [tile("w2_sc%d" % b, [P, N], U8) for b in range(2)]
-        z_f0 = tile("z_f0", [P, 4, M], F32)
-        z_f = [
-            [z_f0[:, :, PART * u : PART * (u + 1)] for u in range(2)],
-            [
-                z_late[:, 0 : 4 * M].rearrange("p (t m) -> p t m", t=4)[:, :, 0:PART],
-                z_late[:, 3 * M + P :].rearrange("p (t m) -> p t m", t=4),
-            ],
-        ]
-        z_bf = [z_late[:, 3 * M + P :].bitcast(BF16), tile("z_bf1", [P, 4 * M], BF16)[:]]
+        z_f0 = z_late[:, 3 * M - P :].rearrange("p (t m) -> p t m", t=4)
+        z_f1 = {
+            0: z_late[:, 0 : 4 * M].rearrange("p (t m) -> p t m", t=4)[:, :, 0:PART],
+            256: z_late[:, 3 * M : 4 * M].rearrange("p (t m) -> p t m", t=4),
+            384: z_late[:, 4 * M : 5 * M].rearrange("p (t m) -> p t m", t=4),
+        }
+        z_bf = [tile("z_bf%d" % b, [P, 4 * M], BF16)[:] for b in range(2)]
         z_w = [placed("z_w0", [P, M], U32, 74.5), tile("z_w1", [P, M], U32)]
         z_sc = [tile("z_sc%d" % b, [P, M], U8) for b in range(2)]
-        res = [[tile("res%d%d" % (u, i), [P, BANK], F32) for i in range(2)] for u in range(2)]
+        res = {(m0, i): tile("res%d_%d" % (m0, i), [P, 4 // banks, m1 - m0], F32) for m0, m1, banks in PARTS for i in range(banks)}
         warm = tile("warm", [P, 16], F32)
         bank_a, bank_b, bank_o = {}, {}, {}
 
@@ -113,6 +116,7 @@ def tile_list_gated_token_merge_kernel(tc, tab_words, tab_scales, offs, wg_words
         nc.vector.memset(warm[:, 0:8], 0.0)
         nc.scalar.activation(warm[:, 8:16], warm[:, 0:8], ACT.Silu)
         nc.vector.memset(v_sc1[:].bitcast(I32), 0)
+        nc.vector.memset(hs[3][:, S + BANK : 2 * S], 0.0)
 
         def load_wg(dst, c0, c1):
             nc.sync.dma_start(dst[:], wg_words[:, :, 2 * c0 : 2 * c1].bitcast(I32).rearrange("a p n -> p a n"))
@@ -241,17 +245,17 @@ def tile_list_gated_token_merge_kernel(tc, tab_words, tab_scales, offs, wg_words
             for i in range(4):
                 nc.sync.dma_start(z_f0[32 * k : 32 * (k + 1), i, :], z_rows[k][i:P:4, :])
 
-        def pick_second_part(k, u):
-            picked = hs[k][:].indirect(pos2_sb[:, 16 * u : 16 * (u + 1)])
-            nc.vector.tensor_tensor(z_f[1][u][:, k - 4, :], picked, first[k][:, PART * u : PART * (u + 1)], ALU.add)
+        def pick_second_part(k, part):
+            m0, m1, banks = part
+            picked = hs[k][:].indirect(pos2_sb[:, m0 // 16 : m1 // 16])
+            nc.vector.tensor_tensor(z_f1[m0][:, k - 4, :], picked, first[k][:, m0:m1], ALU.add)
 
         def rounded_z(b, m0, m1):
             return z_bf[b][:, 4 * m0 : 4 * m1]
 
         def round_z(b, m0, m1, on_vector):
             dst = rounded_z(b, m0, m1).rearrange("p (c j t) -> p c t j", j=4, t=4)
-            u = m0 // PART
-            src = z_f[b][u][:, :, m0 - PART * u : m1 - PART * u].rearrange("p t (c j) -> p c t j", j=4)
+            src = (z_f1[m0] if b == 1 else z_f0[:, :, m0:m1]).rearrange("p t (c j) -> p c t j", j=4)
             if on_vector:
                 nc.vector.tensor_scalar(dst, src, W2, 0.0, ALU.mult, ALU.add)
             else:
@@ -260,28 +264,34 @@ def tile_list_gated_token_merge_kernel(tc, tab_words, tab_scales, offs, wg_words
         def quant_z(b, m0, m1):
             nc.vector.quantize_mx(z_w[b][:, m0:m1].bitcast(FP8X4), z_sc[b][:, m0:m1], rounded_z(b, m0, m1))
 
-        def down(b, u):
+        def down(b, part):
+            m0, m1, banks = part
+            each = 4 // banks
             if b == 0:
-                bank_o[u] = [bank("bank_o%d%d" % (u, i), "%d0%d" % (1 - u, i)) for i in range(2)]
+                tags = {0: ("100", "101"), 384: ("000",), 256: ("001", "110")}[m0]
+                bank_o[m0] = [bank("bank_o%d_%d" % (m0, i), tags[i]) for i in range(banks)]
             for n in range(4):
                 rows = slice(P * n, P * (n + 1))
                 nc.tensor.matmul_mx(
-                    bank_o[u][n // 2][:, PART * (n % 2) : PART * (n % 2 + 1)],
+                    bank_o[m0][n // each][:, (m1 - m0) * (n % each) : (m1 - m0) * (n % each + 1)],
                     lhsT=w2_w[b][:, rows].bitcast(FP8X4),
                     lhsT_scale=w2_sc[b][:, rows],
-                    rhs=z_w[b][:, PART * u : PART * (u + 1)].bitcast(FP8X4),
-                    rhs_scale=z_sc[b][:, PART * u : PART * (u + 1)],
-                    start=(b == 0 and n % 2 == 0),
-                    stop=(b == 1 and n % 2 == 1),
+                    rhs=z_w[b][:, m0:m1].bitcast(FP8X4),
+                    rhs_scale=z_sc[b][:, m0:m1],
+                    start=(b == 0 and n % each == 0),
+                    stop=(b == 1 and n % each == each - 1),
                 )
 
-        def store(u, i, on_vector):
+        def store(part, i, on_vector):
+            m0, m1, banks = part
+            each = 4 // banks
+            src = bank_o[m0][i][:, 0 : each * (m1 - m0)].rearrange("p (n m) -> p n m", n=each)
             if on_vector:
-                nc.vector.tensor_copy(res[u][i][:], bank_o[u][i][:])
+                nc.vector.tensor_copy(res[m0, i][:], src)
             else:
-                nc.scalar.copy(res[u][i][:], bank_o[u][i][:])
-            dst = out[2 * P * i : 2 * P * (i + 1), PART * u : PART * (u + 1)].rearrange("(n p) m -> p n m", p=P)
-            nc.sync.dma_start(dst, res[u][i][:].rearrange("p (n m) -> p n m", n=2))
+                nc.scalar.copy(res[m0, i][:], src)
+            dst = out[each * P * i : each * P * (i + 1), m0:m1].rearrange("(n p) m -> p n m", p=P)
+            nc.sync.dma_start(dst, res[m0, i][:])
 
         for a in range(2):
             for u in range(2):
@@ -308,73 +318,119 @@ def tile_list_gated_token_merge_kernel(tc, tab_words, tab_scales, offs, wg_words
         round_wu(1, 2, nc.scalar)
         quant_wu(2)
 
-        for a in range(2):
-            up_pass(1, 1, a)
-        park(1)
-        product_gpsimd(1)
-        for k in range(SLICES):
-            pick_first(k)
-            if k + 1 < SLICES:
-                for u in (0, 1) if k + 1 == 4 else (0,):
-                    for a in range(2):
-                        up_pass(k + 1, u, a)
-                    product_vector(k + 1, u)
-            if k + 2 < SLICES:
+        def gates(k):
+            for u in (1, 0):
                 for a in range(2):
-                    gate_pass(k + 2, 1, a)
-                if k + 2 != 4:
-                    for a in range(2):
-                        up_pass(k + 2, 1, a)
-                    park(k + 2)
-            if k < 4:
-                pick_second(k)
-            elif k + 1 < SLICES:
-                pick_second_part(k, 0)
-            if k == 2:
-                for a in range(2):
-                    for j in (4, 5):
-                        round_wu(a, j, nc.scalar)
-                quant_wu(4)
-                round_gpsimd(w2_bf[0][:, 1024:2048], w2_raw[0][:, :, 256:N])
-            elif k == 0:
-                for a in range(2):
-                    round_wu(a, 3, nc.scalar)
-            if k in (0, 2, 3, 4):
-                quant_wu(k + 3)
-            elif k == 6:
-                quant_w2(0)
-            elif k == 7:
-                quant_z(0, 0, M)
-                quant_w2(1)
-            if k + 2 < SLICES:
-                if k + 2 != 4:
-                    product_gpsimd(k + 2)
-                for a in range(2):
-                    gate_pass(k + 2, 0, a)
-            if k == 2:
-                for j in (6, 7):
-                    for a in range(2):
-                        round_wu(a, j, nc.scalar)
-            if k == 5:
-                round_w2(0, 0)
-                for u in range(2):
-                    round_z(0, PART * u, PART * (u + 1), False)
-                for u in range(2):
-                    round_w2(1, u)
+                    gate_pass(k, u, a)
 
-        pick_second_part(SLICES - 1, 0)
-        round_z(1, 0, PART, False)
+        def up_parked(k):
+            for a in range(2):
+                up_pass(k, 1, a)
+            park(k)
+            for a in range(2):
+                up_pass(k, 0, a)
+
+        def up_vector(k, u):
+            for a in range(2):
+                up_pass(k, u, a)
+            product_vector(k, u)
+
+        def round_both(k):
+            for a in range(2):
+                round_wu(a, k, nc.scalar)
+
+        up_parked(1)
+        product_gpsimd(1)
+        pick_first(0)
+        product_vector(1, 0)
+        for a in range(2):
+            gate_pass(2, 1, a)
+        up_parked(2)
+        pick_second(0)
+        round_both(3)
+        quant_wu(3)
+        product_gpsimd(2)
+        for a in range(2):
+            gate_pass(2, 0, a)
+
+        pick_first(1)
+        product_vector(2, 0)
+        gates(3)
+        gates(4)
+        up_parked(3)
+        pick_second(1)
+        product_gpsimd(3)
+        for a in range(2):
+            nc.scalar.copy(
+                wu_bf45.rearrange("p (t a g j i) -> p a t g i j", t=2, a=2, j=8, i=4)[:, a],
+                wu_late[a].rearrange("p i (g t j) -> p t g i j", t=4, j=8)[:, 0:2],
+            )
+
+        pick_first(2)
+        product_vector(3, 0)
+        pick_second(2)
+        both = "p t c -> p (t c)"
+        nc.vector.quantize_mx(wu_w45[:].rearrange(both).bitcast(FP8X4), wu_sc45[:].rearrange(both), wu_bf45)
+        round_gpsimd(w2_bf[0][:, 1024:2048], w2_raw[0][:, :, 256:N])
+        gates(5)
+        for k in (6, 7):
+            round_both(k)
+
+        pick_first(3)
         for u in range(2):
-            down(0, u)
-        for k in (5, 6, 7):
-            pick_second_part(k, 1)
+            up_vector(4, u)
+        up_parked(5)
+        pick_second(3)
+        quant_wu(6)
+        product_gpsimd(5)
+        gates(6)
+        round_w2(0, 0)
+
+        pick_first(4)
+        product_vector(5, 0)
+        up_parked(6)
+        pick_second_part(4, EARLY)
+        quant_wu(7)
+        product_gpsimd(6)
+        gates(7)
+
+        pick_first(5)
+        product_vector(6, 0)
+        up_parked(7)
+        pick_second_part(5, EARLY)
+        product_gpsimd(7)
+        for u in range(2):
+            round_w2(1, u)
+        round_z(0, 0, M, False)
+
+        pick_first(6)
+        product_vector(7, 0)
+        pick_second_part(6, EARLY)
+        quant_w2(0)
+        pick_first(7)
+        quant_w2(1)
+        quant_z(0, 0, M)
+
+        for part in PARTS:
+            down(0, part)
+        pick_second_part(7, EARLY)
+        round_z(1, 0, PART, False)
+        for k in range(4, SLICES):
+            pick_second_part(k, MIDDLE)
+        round_z(1, 384, M, False)
+        for k in (6, 7):
+            pick_second_part(k, LAST)
         quant_z(1, 0, PART)
-        down(1, 0)
+        down(1, EARLY)
         for i in range(2):
-            store(0, i, False)
-        pick_second_part(4, 1)
-        round_z(1, PART, M, True)
-        quant_z(1, PART, M)
-        down(1, 1)
+            store(EARLY, i, False)
+        for k in (4, 5):
+            pick_second_part(k, LAST)
+        round_z(1, PART, 384, True)
+        quant_z(1, 384, M)
+        down(1, MIDDLE)
+        quant_z(1, PART, 384)
+        down(1, LAST)
+        store(MIDDLE, 0, True)
         for i in range(2):
-            store(1, i, i == 0)
+            store(LAST, i, i == 1)

@@ -78,7 +78,8 @@ def tile_list_gated_token_merge_kernel(tc, tab_words, tab_scales, offs, wg_words
             silu.append([hs[k - 1][:, S + BANK : 2 * S], own[:, 0:BANK]])
         silu[4][0] = placed("silu40", [P, BANK], F32, 92)[:]
         wu_bf = {k: hs[k - 1][:, 0:BANK].bitcast(BF16) for k in (3, 6, 7)}
-        wu_bf.update({k: tile("wu_bf%d" % k, [P, 1024], BF16)[:] for k in (0, 1)})
+        wu_bf[0] = tile("wu_bf0", [P, 1024], BF16)[:]
+        wu_bf[1] = hs[1][:, 0:BANK].bitcast(BF16)
         wu_bf[2] = hs[1][:, 256:768].bitcast(BF16)
         wu_bf45 = hs[5][:, BANK : S + BANK].bitcast(BF16)
         wu_w = {k: placed("wu_w%d" % k, [P, 256], U32, at) for k, at in ((0, 46), (2, 46), (3, 56), (6, 64), (7, 66))}
@@ -93,7 +94,7 @@ def tile_list_gated_token_merge_kernel(tc, tab_words, tab_scales, offs, wg_words
         z_f0 = z_late[:, 3 * M - P :].rearrange("p (t m) -> p t m", t=4)
         z_f1 = {
             0: z_late[:, 0 : 4 * M].rearrange("p (t m) -> p t m", t=4)[:, :, 0:PART],
-            256: z_late[:, 3 * M : 4 * M].rearrange("p (t m) -> p t m", t=4),
+            256: z_late[:, 3 * M - 64 : 4 * M - 64].rearrange("p (t m) -> p t m", t=4),
             384: z_late[:, 4 * M : 5 * M].rearrange("p (t m) -> p t m", t=4),
         }
         z_bf = [tile("z_bf%d" % b, [P, 4 * M], BF16)[:] for b in range(2)]
@@ -291,7 +292,7 @@ def tile_list_gated_token_merge_kernel(tc, tab_words, tab_scales, offs, wg_words
             else:
                 nc.scalar.copy(res[m0, i][:], src)
             dst = out[each * P * i : each * P * (i + 1), m0:m1].rearrange("(n p) m -> p n m", p=P)
-            nc.sync.dma_start(dst, res[m0, i][:])
+            (nc.scalar if part is LAST and not on_vector else nc.sync).dma_start(dst, res[m0, i][:])
 
         for a in range(2):
             for u in range(2):
@@ -418,13 +419,12 @@ def tile_list_gated_token_merge_kernel(tc, tab_words, tab_scales, offs, wg_words
         for k in range(4, SLICES):
             pick_second_part(k, MIDDLE)
         round_z(1, 384, M, False)
-        for k in (6, 7):
-            pick_second_part(k, LAST)
+        pick_second_part(7, LAST)
         quant_z(1, 0, PART)
         down(1, EARLY)
         for i in range(2):
             store(EARLY, i, False)
-        for k in (4, 5):
+        for k in (4, 5, 6):
             pick_second_part(k, LAST)
         round_z(1, PART, 384, True)
         quant_z(1, 384, M)

@@ -166,14 +166,15 @@ def tile_list_gated_token_merge_kernel(tc, tab_words, tab_scales, offs, wg_words
 
         def round_wu(a, k, engine):
             dst = wu_bf[k][:, 512 * a : 512 * (a + 1)]
+            run = 2 if engine is nc.scalar else 4
             if k < 4:
                 src = wu_pair[a][:, :, P * k : P * (k + 1)] if k < 2 else wu_one[a, k]
                 if engine is nc.gpsimd:
                     return round_gpsimd(dst, src)
-                src = src.rearrange("p i (g h j) -> p g h i j", h=2, j=4)
+                src = src.rearrange("p i (g h j) -> p g h i j", h=8 // run, j=run)
             else:
-                src = wu_late[a].rearrange("p i (g t h j) -> p t g h i j", t=4, h=2, j=4)[:, k - 4]
-            dst = dst.rearrange("p (g h j i) -> p g h i j", h=2, j=4, i=4)
+                src = wu_late[a].rearrange("p i (g t h j) -> p t g h i j", t=4, h=8 // run, j=run)[:, k - 4]
+            dst = dst.rearrange("p (g h j i) -> p g h i j", h=8 // run, j=run, i=4)
             if engine is nc.scalar:
                 return nc.scalar.copy(dst, src)
             return nc.vector.tensor_copy(dst, src)
@@ -187,8 +188,8 @@ def tile_list_gated_token_merge_kernel(tc, tab_words, tab_scales, offs, wg_words
 
         def round_w2(b, u):
             nc.scalar.copy(
-                w2_bf[b][:, 1024 * u : 1024 * (u + 1)].rearrange("p (c j t) -> p c t j", j=4, t=4),
-                w2_raw[b][:, :, 256 * u : 256 * (u + 1)].rearrange("p t (c j) -> p c t j", j=4),
+                w2_bf[b][:, 1024 * u : 1024 * (u + 1)].rearrange("p (c j t) -> p c t j", j=2, t=4),
+                w2_raw[b][:, :, 256 * u : 256 * (u + 1)].rearrange("p t (c j) -> p c t j", j=2),
             )
 
         def round_gpsimd(dst, src):
@@ -255,8 +256,9 @@ def tile_list_gated_token_merge_kernel(tc, tab_words, tab_scales, offs, wg_words
             return z_bf[b][:, 4 * m0 : 4 * m1]
 
         def round_z(b, m0, m1, on_vector):
-            dst = rounded_z(b, m0, m1).rearrange("p (c j t) -> p c t j", j=4, t=4)
-            src = (z_f1[m0] if b == 1 else z_f0[:, :, m0:m1]).rearrange("p t (c j) -> p c t j", j=4)
+            run = 4 if on_vector else 2
+            dst = rounded_z(b, m0, m1).rearrange("p (c j t) -> p c t j", j=run, t=4)
+            src = (z_f1[m0] if b == 1 else z_f0[:, :, m0:m1]).rearrange("p t (c j) -> p c t j", j=run)
             if on_vector:
                 nc.vector.tensor_scalar(dst, src, W2, 0.0, ALU.mult, ALU.add)
             else:

@@ -43,7 +43,7 @@ def tile_list_gated_token_merge_kernel(tc, tab_words, tab_scales, offs, wg_words
         pos1_sb = tile("pos1_sb", [P, M // 16], U16)
         pos2_sb = tile("pos2_sb", [P, M // 16], U16)
 
-        tab_sc = placed("tab_sc", [P, T], U8, 1)
+        tab_sc = tile("tab_sc", [P, T], U8)
         tab_w = [tile("tab_w0", [P, T], I32), tile("tab_w1", [P, T], I32)]
         v_w = [[tile("v_w%d%d" % (a, u), [P, BANK], U32) for u in range(2)] for a in range(2)]
         v_sc = tile("v_sc", [P, S], U8)
@@ -57,14 +57,13 @@ def tile_list_gated_token_merge_kernel(tc, tab_words, tab_scales, offs, wg_words
         def raw_part(at, width):
             return raw[:, at : at + 4 * width].rearrange("p (i c) -> p i c", i=4)
 
-        wu_first = tile("wu_first", [P, 4, 256], F32)
-        wu_pair = [wu_first[:], raw_part(0, 256)]
         wu_one = {(a, k): raw_part(1024 + 512 * (2 * k + a - 4), P) for a, k in ((0, 2), (1, 2))}
         wu_one.update({(a, 3): placed("wu_one%d3" % a, [P, 4, P], F32, 48 + 2 * a)[:] for a in range(2)})
         wu_late = [raw_part(2048 + 2048 * a, PASS) for a in range(2)]
         w2_raw = [raw_part(6144 + 2048 * b, N) for b in range(2)]
         ring = [tile("hs%d" % r, [P, 2 * S], F32) for r in range(RING)]
         hs = [ring[k % RING] for k in range(SLICES + 2)]
+        wu_pair = [hs[0][:, S:].rearrange("p (i c) -> p i c", i=4), raw_part(0, 256)]
         first = [hs[k + 2][:, BANK:S] for k in range(4)] + [hs[k + 2][:, S - PART : S + PART] for k in (4, 5)]
         first[2] = placed("first2", [P, M], F32, 56)[:]
         first += [placed("first6", [P, M], F32, 66)[:], tile("first7", [P, M], F32)[:]]
@@ -72,10 +71,11 @@ def tile_list_gated_token_merge_kernel(tc, tab_words, tab_scales, offs, wg_words
         z_rows = [placed("z_rows0", [P, M], F32, 51)[:]] + [tile("z_rows%d" % k, [P, M], F32)[:] for k in (1, 2)]
         z_rows.append(placed("z_rows3", [P, M], F32, 92)[:])
         parked = [hs[k][:, S : S + BANK] for k in range(6)] + [hs[7][:, 0:BANK], tile("parked7", [P, BANK], F32)[:]]
-        silu = [[hs[0][:, S : S + BANK], hs[2][:, 0:BANK]]]
+        silu = [[hs[0][:, S : S + BANK], hs[0][:, S + BANK :]]]
         for k, at in zip(range(1, SLICES), (56, 58, 62, 64, 66, 68, 76)):
             own = placed("silu%d" % k, [P, S if k == 7 else BANK], F32, at)
             silu.append([hs[k - 1][:, S + BANK : 2 * S], own[:, 0:BANK]])
+        silu[1][0] = placed("silu10", [P, BANK], F32, 52.5)[:]
         silu[4][0] = placed("silu40", [P, BANK], F32, 92)[:]
         wu_bf = {k: hs[k - 1][:, 0:BANK].bitcast(BF16) for k in (3, 6, 7)}
         wu_bf[0] = tile("wu_bf0", [P, 1024], BF16)[:]
@@ -134,7 +134,7 @@ def tile_list_gated_token_merge_kernel(tc, tab_words, tab_scales, offs, wg_words
         load_wu(wu_pair[0], 0, 0, 256)
 
         nc.vector.tensor_copy(v_sc[:], tab_sc[:].indirect(offs_sb[:]))
-        nc.sync.dma_start(v_sc1[0:112, :].bitcast(I32), v_sc[16:P, :].bitcast(I32))
+        nc.scalar.dma_start(v_sc1[0:112, :].bitcast(I32), v_sc[16:P, :].bitcast(I32))
         for a in range(2):
             for u in range(2):
                 nc.vector.tensor_copy(v_w[a][u][:], tab_w[a][:].bitcast(U32).indirect(offs_sb[:, 32 * u : 32 * (u + 1)]))
@@ -296,11 +296,11 @@ def tile_list_gated_token_merge_kernel(tc, tab_words, tab_scales, offs, wg_words
             dst = out[each * P * i : each * P * (i + 1), m0:m1].rearrange("(n p) m -> p n m", p=P)
             (nc.scalar if part is LAST and not on_vector else nc.sync).dma_start(dst, res[m0, i][:])
 
+        round_wu(0, 0, nc.scalar)
+        round_wu(0, 1, nc.gpsimd)
         for a in range(2):
             for u in range(2):
                 gate_pass(0, u, a)
-        round_wu(0, 0, nc.scalar)
-        round_wu(0, 1, nc.gpsimd)
         quant_wu_pass(0, 0)
         for u in range(2):
             up_pass(0, u, 0)
@@ -372,8 +372,8 @@ def tile_list_gated_token_merge_kernel(tc, tab_words, tab_scales, offs, wg_words
         pick_first(2)
         product_vector(3, 0)
         pick_second(2)
-        both = "p t c -> p (t c)"
-        nc.vector.quantize_mx(wu_w45[:].rearrange(both).bitcast(FP8X4), wu_sc45[:].rearrange(both), wu_bf45)
+        for t in range(2):
+            nc.vector.quantize_mx(wu_w[4 + t].bitcast(FP8X4), wu_sc[4 + t], wu_bf45[:, 1024 * t : 1024 * (t + 1)])
         round_gpsimd(w2_bf[0][:, 1024:2048], w2_raw[0][:, :, 256:N])
         gates(5)
         for k in (6, 7):

@@ -298,9 +298,8 @@ def tile_list_gated_token_merge_kernel(tc, tab_words, tab_scales, offs, wg_words
 
         round_wu(0, 0, nc.scalar)
         round_wu(0, 1, nc.gpsimd)
-        for a in range(2):
-            for u in range(2):
-                gate_pass(0, u, a)
+        for k, u, a in ((0, 0, 0), (0, 1, 0), (1, 1, 0), (1, 0, 0), (0, 0, 1), (0, 1, 1)):
+            gate_pass(k, u, a)
         quant_wu_pass(0, 0)
         for u in range(2):
             up_pass(0, u, 0)
@@ -311,8 +310,7 @@ def tile_list_gated_token_merge_kernel(tc, tab_words, tab_scales, offs, wg_words
             up_pass(0, u, 1)
         quant_wu(1)
         for u in (1, 0):
-            for a in range(2):
-                gate_pass(1, u, a)
+            gate_pass(1, u, 1)
         order_wg_scales()
         order_wg()
         for u in range(2):

@@ -57,13 +57,14 @@ def tile_list_gated_token_merge_kernel(tc, tab_words, tab_scales, offs, wg_words
         def raw_part(at, width):
             return raw[:, at : at + 4 * width].rearrange("p (i c) -> p i c", i=4)
 
+        wu_first = tile("wu_first", [P, 4, 256], F32)
+        wu_pair = [wu_first[:], raw_part(0, 256)]
         wu_one = {(a, k): raw_part(1024 + 512 * (2 * k + a - 4), P) for a, k in ((0, 2), (1, 2))}
         wu_one.update({(a, 3): placed("wu_one%d3" % a, [P, 4, P], F32, 48 + 2 * a)[:] for a in range(2)})
         wu_late = [raw_part(2048 + 2048 * a, PASS) for a in range(2)]
         w2_raw = [raw_part(6144 + 2048 * b, N) for b in range(2)]
         ring = [tile("hs%d" % r, [P, 2 * S], F32) for r in range(RING)]
         hs = [ring[k % RING] for k in range(SLICES + 2)]
-        wu_pair = [hs[0][:, S:].rearrange("p (i c) -> p i c", i=4), raw_part(0, 256)]
         first = [hs[k + 2][:, BANK:S] for k in range(4)] + [hs[k + 2][:, S - PART : S + PART] for k in (4, 5)]
         first[2] = placed("first2", [P, M], F32, 56)[:]
         first += [placed("first6", [P, M], F32, 66)[:], tile("first7", [P, M], F32)[:]]
@@ -71,11 +72,10 @@ def tile_list_gated_token_merge_kernel(tc, tab_words, tab_scales, offs, wg_words
         z_rows = [placed("z_rows0", [P, M], F32, 51)[:]] + [tile("z_rows%d" % k, [P, M], F32)[:] for k in (1, 2)]
         z_rows.append(placed("z_rows3", [P, M], F32, 92)[:])
         parked = [hs[k][:, S : S + BANK] for k in range(6)] + [hs[7][:, 0:BANK], tile("parked7", [P, BANK], F32)[:]]
-        silu = [[hs[0][:, S : S + BANK], hs[0][:, S + BANK :]]]
+        silu = [[hs[0][:, S : S + BANK], hs[2][:, 0:BANK]]]
         for k, at in zip(range(1, SLICES), (56, 58, 62, 64, 66, 68, 76)):
             own = placed("silu%d" % k, [P, S if k == 7 else BANK], F32, at)
             silu.append([hs[k - 1][:, S + BANK : 2 * S], own[:, 0:BANK]])
-        silu[1][0] = placed("silu10", [P, BANK], F32, 52.5)[:]
         silu[4][0] = placed("silu40", [P, BANK], F32, 92)[:]
         wu_bf = {k: hs[k - 1][:, 0:BANK].bitcast(BF16) for k in (3, 6, 7)}
         wu_bf[0] = tile("wu_bf0", [P, 1024], BF16)[:]

@@ -48,7 +48,8 @@ def tile_list_gated_token_merge_kernel(tc, tab_words, tab_scales, offs, wg_words
         v_w = [[tile("v_w%d%d" % (a, u), [P, BANK], U32) for u in range(2)] for a in range(2)]
         v_sc = tile("v_sc", [P, S], U8)
         v_sc1 = tile("v_sc1", [P, S], U8)
-        wg_raw = [tile("wg_raw0", [P, 2, 256], I32), placed("wg_raw1", [P, 2, 256], I32, 0)]
+        wg_pair = [tile("wg_pair%d" % b, [P, 2, 128], I32) for b in range(2)]
+        wg_late = tile("wg_late", [P, 2, 256], I32)
         wg_w1 = tile("wg_w1", [P, 2, 256], I32)
         wg_sc_raw = tile("wg_sc_raw", [P, 2, 256], I32)
         wg_sc1 = tile("wg_sc1", [P, 2, 128], I32)
@@ -127,7 +128,7 @@ def tile_list_gated_token_merge_kernel(tc, tab_words, tab_scales, offs, wg_words
 
         for a in range(2):
             nc.sync.dma_start(tab_w[a][:], tab_words[a].rearrange("p n i -> p (n i)").bitcast(I32))
-        load_wg(wg_raw[0], 0, PASS)
+        load_wg(wg_pair[0], 0, 256)
         wg_rows_by_r = wg_scales.rearrange("a (q r) n -> r q a n", r=4)
         for r in range(4):
             nc.sync.dma_start(wg_sc_raw[r:P:32, :, :], wg_rows_by_r[r].bitcast(I32))
@@ -140,11 +141,12 @@ def tile_list_gated_token_merge_kernel(tc, tab_words, tab_scales, offs, wg_words
                 nc.vector.tensor_copy(v_w[a][u][:], tab_w[a][:].bitcast(U32).indirect(offs_sb[:, 32 * u : 32 * (u + 1)]))
 
         load_wu(wu_pair[1], 1, 0, 256)
-        load_wg(wg_raw[1], PASS, H)
-        nc.sync.dma_start(pos2_sb[:], pos2)
+        load_wg(wg_late, PASS, H)
+        load_wg(wg_pair[1], 256, PASS)
         for k in (2, 3):
             for a in range(2):
                 load_wu(wu_one[a, k], a, P * k, P * (k + 1))
+        nc.sync.dma_start(pos2_sb[:], pos2)
         for a in range(2):
             load_wu(wu_late[a], a, PASS, H)
         nc.sync.dma_start(w2_raw[0], w2[0:PASS, :].rearrange("(p t) n -> p t n", t=4))
@@ -155,7 +157,7 @@ def tile_list_gated_token_merge_kernel(tc, tab_words, tab_scales, offs, wg_words
         def order_wg():
             nc.vector.tensor_copy(
                 wg_w1[:].rearrange("p a (t g w) -> p a t g w", t=4, w=4),
-                wg_raw[1][:].rearrange("p a (g t w) -> p a t g w", t=4, w=4),
+                wg_late[:].rearrange("p a (g t w) -> p a t g w", t=4, w=4),
             )
 
         def order_wg_scales():
@@ -206,7 +208,7 @@ def tile_list_gated_token_merge_kernel(tc, tab_words, tab_scales, offs, wg_words
                 bank_b[k, u] = bank("bank_b%d%d" % (k, u), "%d%d%d" % (k >= 2, k % 2, u))
             nc.tensor.matmul_mx(
                 bank_b[k, u][:],
-                lhsT=(wg_raw[0], wg_w1)[b][:, a, 64 * t : 64 * (t + 1)].bitcast(FP4X4),
+                lhsT=(wg_w1[:, a, 64 * t : 64 * (t + 1)] if b else wg_pair[k // 2][:, a, 64 * (k % 2) : 64 * (k % 2 + 1)]).bitcast(FP4X4),
                 lhsT_scale=(wg_sc_raw, wg_sc1)[b][:, a, 32 * t : 32 * (t + 1)].bitcast(U8),
                 rhs=v_w[a][u][:].bitcast(FP8X4),
                 rhs_scale=(v_sc, v_sc1)[a][:, cols],

from contextlib import ExitStack

import concourse.mybir as mybir

K, H, N, T, S, M = 1024, 1024, 512, 2048, 1024, 512
FLOPS = 2 * (2 * K * H * S + H * N * M)

F32 = mybir.dt.float32
BF16 = mybir.dt.bfloat16
I32 = mybir.dt.int32
U32 = mybir.dt.uint32
U16 = mybir.dt.uint16
U8 = mybir.dt.uint8
FP8X4 = mybir.dt.float8_e4m3fn_x4
FP4X4 = mybir.dt.float4_e2m1fn_x4
ALU = mybir.AluOpType
ACT = mybir.ActivationFunctionType

P = 128
PASS = 512
BANK = 512
SLICES = H // P
PART = M // 2
W1, W2 = 0.7, 0.3
EARLY, MIDDLE, LAST = PARTS = (0, 256, 2), (384, 512, 1), (256, 384, 2)
RING = 4


def tile_list_gated_token_merge_kernel(tc, tab_words, tab_scales, offs, wg_words, wg_scales, wu, w2, pos1, pos2, out):
    nc = tc.nc
    with ExitStack() as ctx:
        sb = ctx.enter_context(tc.tile_pool(name="sb", bufs=1))
        shared = ctx.enter_context(tc.tile_pool(name="shared", bufs=1))
        ps = ctx.enter_context(tc.psum_pool(name="ps", bufs=1))

        def tile(name, shape, dtype, tag=None):
            return sb.tile(shape, dtype, name=name, tag=tag or name, align_bytes=64)

        def placed(name, shape, dtype, kib):
            return shared.tile(shape, dtype, name=name, align_bytes=64, offset=int(1024 * kib))

        offs_sb = tile("offs_sb", [P, S // 16], U16)
        pos1_sb = tile("pos1_sb", [P, M // 16], U16)
        pos2_sb = tile("pos2_sb", [P, M // 16], U16)

        tab_sc = tile("tab_sc", [P, T], U8)
        tab_w = [tile("tab_w0", [P, T], I32), tile("tab_w1", [P, T], I32)]
        v_w = [[tile("v_w%d%d" % (a, u), [P, BANK], U32) for u in range(2)] for a in range(2)]
        v_sc = tile("v_sc", [P, S], U8)
        v_sc1 = tile("v_sc1", [P, S], U8)
        wg_pair = [tile("wg_pair%d" % b, [P, 2, 128], I32) for b in range(2)]
        wg_late = tile("wg_late", [P, 2, 256], I32)
        wg_w1 = tile("wg_w1", [P, 2, 256], I32)
        wg_sc_raw = tile("wg_sc_raw", [P, 2, 256], I32)
        wg_sc1 = tile("wg_sc1", [P, 2, 128], I32)
        raw = placed("raw", [P, 10240], F32, 2)

        def raw_part(at, width):
            return raw[:, at : at + 4 * width].rearrange("p (i c) -> p i c", i=4)

        wu_first = tile("wu_first", [P, 4, 256], F32)
        wu_pair = [wu_first[:], raw_part(0, 256)]
        wu_one = {(a, k): raw_part(1024 + 512 * (2 * k + a - 4), P) for a, k in ((0, 2), (1, 2))}
        wu_one.update({(a, 3): placed("wu_one%d3" % a, [P, 4, P], F32, 48 + 2 * a)[:] for a in range(2)})
        wu_late = [raw_part(2048 + 2048 * a, PASS) for a in range(2)]
        w2_raw = [raw_part(6144 + 2048 * b, N) for b in range(2)]
        ring = [tile("hs%d" % r, [P, 2 * S], F32) for r in range(RING)]
        hs = [ring[k % RING] for k in range(SLICES + 2)]
        first = [hs[k + 2][:, BANK:S] for k in range(4)] + [hs[k + 2][:, S - PART : S + PART] for k in (4, 5)]
        first[2] = placed("first2", [P, M], F32, 56)[:]
        first += [placed("first6", [P, M], F32, 66)[:], tile("first7", [P, M], F32)[:]]
        z_late = tile("z_late", [P, 7 * M - P], F32)
        z_rows = [placed("z_rows0", [P, M], F32, 51)[:]] + [tile("z_rows%d" % k, [P, M], F32)[:] for k in (1, 2)]
        z_rows.append(placed("z_rows3", [P, M], F32, 92)[:])
        parked = [hs[k][:, S : S + BANK] for k in range(6)] + [hs[7][:, 0:BANK], tile("parked7", [P, BANK], F32)[:]]
        silu = [[hs[0][:, S : S + BANK], hs[2][:, 0:BANK]]]
        for k, at in zip(range(1, SLICES), (56, 58, 62, 64, 66, 68, 76)):
            own = placed("silu%d" % k, [P, S if k == 7 else BANK], F32, at)
            silu.append([hs[k - 1][:, S + BANK : 2 * S], own[:, 0:BANK]])
        silu[4][0] = placed("silu40", [P, BANK], F32, 92)[:]
        wu_bf = {k: hs[k - 1][:, 0:BANK].bitcast(BF16) for k in (3, 6, 7)}
        wu_bf[0] = tile("wu_bf0", [P, 1024], BF16)[:]
        wu_bf[1] = hs[1][:, 0:BANK].bitcast(BF16)
        wu_bf[2] = hs[1][:, 256:768].bitcast(BF16)
        wu_bf45 = hs[5][:, BANK : S + BANK].bitcast(BF16)
        wu_w = {k: placed("wu_w%d" % k, [P, 256], U32, at) for k, at in ((0, 46), (2, 46), (3, 56), (6, 64), (7, 66))}
        wu_w[1] = tile("wu_w1", [P, 256], U32)
        wu_sc = {k: tile("wu_sc%d" % k, [P, 256], U8) for k in (0, 1, 2, 3, 6, 7)}
        wu_w45, wu_sc45 = placed("wu_w45", [P, 2, 256], U32, 61), tile("wu_sc45", [P, 2, 256], U8)
        wu_w.update({k: wu_w45[:, k - 4, :] for k in (4, 5)})
        wu_sc.update({k: wu_sc45[:, k - 4, :] for k in (4, 5)})
        w2_bf = [placed("w2_bf0", [P, 4 * N], BF16, 57), tile("w2_bf1", [P, 4 * N], BF16)]
        w2_w = [placed("w2_w%d" % b, [P, N], U32, 77 + 2.5 * b) for b in range(2)]
        w2_sc = [tile("w2_sc%d" % b, [P, N], U8) for b in range(2)]
        z_f0 = z_late[:, 3 * M - P :].rearrange("p (t m) -> p t m", t=4)
        z_f1 = {
            0: z_late[:, 0 : 4 * M].rearrange("p (t m) -> p t m", t=4)[:, :, 0:PART],
            256: z_late[:, 3 * M - 64 : 4 * M - 64].rearrange("p (t m) -> p t m", t=4),
            384: z_late[:, 4 * M : 5 * M].rearrange("p (t m) -> p t m", t=4),
        }
        z_bf = [tile("z_bf%d" % b, [P, 4 * M], BF16)[:] for b in range(2)]
        z_w = [placed("z_w0", [P, M], U32, 74.5), tile("z_w1", [P, M], U32)]
        z_sc = [tile("z_sc%d" % b, [P, M], U8) for b in range(2)]
        res = {(m0, i): tile("res%d_%d" % (m0, i), [P, 4 // banks, m1 - m0], F32) for m0, m1, banks in PARTS for i in range(banks)}
        warm = tile("warm", [P, 16], F32)
        bank_a, bank_b, bank_o = {}, {}, {}

        def bank(name, tag):
            return ps.tile([P, BANK], F32, name=name, tag=tag)

        nc.vector.memset(tab_sc[:].bitcast(I32), 0)
        nc.vector.memset(wg_sc_raw[:], 0)
        for sb_list, dram_list in ((offs_sb, offs), (pos1_sb, pos1)):
            nc.sync.dma_start(sb_list[:], dram_list)
        rows_by_r = tab_scales.rearrange("a (q r) n -> r q a n", r=4)
        for r in range(4):
            nc.sync.dma_start(tab_sc[r:P:16, :].bitcast(I32), rows_by_r[r].bitcast(I32))
        nc.vector.memset(warm[:, 0:8], 0.0)
        nc.scalar.activation(warm[:, 8:16], warm[:, 0:8], ACT.Silu)
        nc.vector.memset(v_sc1[:].bitcast(I32), 0)
        nc.vector.memset(hs[3][:, S + BANK : 2 * S], 0.0)

        def load_wg(dst, c0, c1):
            nc.sync.dma_start(dst[:], wg_words[:, :, 2 * c0 : 2 * c1].bitcast(I32).rearrange("a p n -> p a n"))

        def load_wu(dst, a, c0, c1):
            nc.sync.dma_start(dst, wu[PASS * a : PASS * (a + 1), c0:c1].rearrange("(p i) c -> p i c", i=4))

        for a in range(2):
            nc.sync.dma_start(tab_w[a][:], tab_words[a].rearrange("p n i -> p (n i)").bitcast(I32))
        load_wg(wg_pair[0], 0, 256)
        wg_rows_by_r = wg_scales.rearrange("a (q r) n -> r q a n", r=4)
        for r in range(4):
            nc.sync.dma_start(wg_sc_raw[r:P:32, :, :], wg_rows_by_r[r].bitcast(I32))
        load_wu(wu_pair[0], 0, 0, 256)

        nc.vector.tensor_copy(v_sc[:], tab_sc[:].indirect(offs_sb[:]))
        nc.scalar.dma_start(v_sc1[0:112, :].bitcast(I32), v_sc[16:P, :].bitcast(I32))
        for a in range(2):
            for u in range(2):
                nc.vector.tensor_copy(v_w[a][u][:], tab_w[a][:].bitcast(U32).indirect(offs_sb[:, 32 * u : 32 * (u + 1)]))

        load_wu(wu_pair[1], 1, 0, 256)
        load_wg(wg_late, PASS, H)
        load_wg(wg_pair[1], 256, PASS)
        for k in (2, 3):
            for a in range(2):
                load_wu(wu_one[a, k], a, P * k, P * (k + 1))
        nc.sync.dma_start(pos2_sb[:], pos2)
        for a in range(2):
            load_wu(wu_late[a], a, PASS, H)
        nc.sync.dma_start(w2_raw[0], w2[0:PASS, :].rearrange("(p t) n -> p t n", t=4))
        w2_rows = w2[PASS:H, :].rearrange("(g t j) n -> t g j n", t=4, j=8)
        for t in range(4):
            nc.sync.dma_start(w2_raw[1][:, t, :], w2_rows[t])

        def order_wg():
            nc.vector.tensor_copy(
                wg_w1[:].rearrange("p a (t g w) -> p a t g w", t=4, w=4),
                wg_late[:].rearrange("p a (g t w) -> p a t g w", t=4, w=4),
            )

        def order_wg_scales():
            nc.vector.tensor_copy(
                wg_sc1[:].rearrange("p a (t g w) -> p a t g w", t=4, w=2),
                wg_sc_raw[:, :, 128:256].rearrange("p a (g t w) -> p a t g w", t=4, w=2),
            )

        def round_wu(a, k, engine):
            dst = wu_bf[k][:, 512 * a : 512 * (a + 1)]
            run = 2 if engine is nc.scalar else 4
            if k < 4:
                src = wu_pair[a][:, :, P * k : P * (k + 1)] if k < 2 else wu_one[a, k]
                if engine is nc.gpsimd:
                    return round_gpsimd(dst, src)
                src = src.rearrange("p i (g h j) -> p g h i j", h=8 // run, j=run)
            else:
                src = wu_late[a].rearrange("p i (g t h j) -> p t g h i j", t=4, h=8 // run, j=run)[:, k - 4]
            dst = dst.rearrange("p (g h j i) -> p g h i j", h=8 // run, j=run, i=4)
            if engine is nc.scalar:
                return nc.scalar.copy(dst, src)
            return nc.vector.tensor_copy(dst, src)

        def quant_wu_pass(k, a):
            cols = slice(P * a, P * (a + 1))
            nc.vector.quantize_mx(wu_w[k][:, cols].bitcast(FP8X4), wu_sc[k][:, cols], wu_bf[k][:, 512 * a : 512 * (a + 1)])

        def quant_wu(k):
            nc.vector.quantize_mx(wu_w[k][:].bitcast(FP8X4), wu_sc[k][:], wu_bf[k])

        def round_w2(b, u):
            nc.scalar.copy(
                w2_bf[b][:, 1024 * u : 1024 * (u + 1)].rearrange("p (c j t) -> p c t j", j=2, t=4),
                w2_raw[b][:, :, 256 * u : 256 * (u + 1)].rearrange("p t (c j) -> p c t j", j=2),
            )

        def round_gpsimd(dst, src):
            dst, src = dst.rearrange("p (c i) -> p c i", i=4), src.rearrange("p i c -> p c i")
            nc.gpsimd.tensor_scalar(dst, src, 1.0, 0.0, ALU.mult, ALU.add)

        def quant_w2(b):
            nc.vector.quantize_mx(w2_w[b][:].bitcast(FP8X4), w2_sc[b][:], w2_bf[b][:])

        def gate_pass(k, u, a):
            b, t = divmod(k, 4)
            cols = slice(BANK * u, BANK * (u + 1))
            if a == 0:
                bank_b[k, u] = bank("bank_b%d%d" % (k, u), "%d%d%d" % (k >= 2, k % 2, u))
            nc.tensor.matmul_mx(
                bank_b[k, u][:],
                lhsT=(wg_w1[:, a, 64 * t : 64 * (t + 1)] if b else wg_pair[k // 2][:, a, 64 * (k % 2) : 64 * (k % 2 + 1)]).bitcast(FP4X4),
                lhsT_scale=(wg_sc_raw, wg_sc1)[b][:, a, 32 * t : 32 * (t + 1)].bitcast(U8),
                rhs=v_w[a][u][:].bitcast(FP8X4),
                rhs_scale=(v_sc, v_sc1)[a][:, cols],
                start=(a == 0),
                stop=(a == 1),
            )
            if a == 1:
                nc.scalar.activation(silu[k][u], bank_b[k, u][:], ACT.Silu)

        def up_pass(k, u, a):
            cols = slice(P * a, P * (a + 1))
            if a == 0:
                bank_a[k, u] = bank("bank_a%d%d" % (k, u), "%d%d%d" % (k < 2, k % 2, u))
            nc.tensor.matmul_mx(
                bank_a[k, u][:],
                lhsT=wu_w[k][:, cols].bitcast(FP8X4),
                lhsT_scale=wu_sc[k][:, cols],
                rhs=v_w[a][u][:].bitcast(FP8X4),
                rhs_scale=(v_sc, v_sc1)[a][:, BANK * u : BANK * (u + 1)],
                start=(a == 0),
                stop=(a == 1),
            )

        def product_vector(k, u):
            nc.vector.tensor_tensor(hs[k][:, BANK * u : BANK * (u + 1)], bank_a[k, u][:], silu[k][u], ALU.mult)

        def park(k):
            nc.scalar.copy(parked[k], bank_a[k, 1][:])

        def product_gpsimd(k):
            nc.gpsimd.tensor_tensor(hs[k][:, BANK:S], parked[k], silu[k][1], ALU.mult)

        def pick_first(k):
            nc.vector.tensor_scalar(first[k], hs[k][:].indirect(pos1_sb[:]), W1 / W2, 0.0, ALU.mult, ALU.add)

        def pick_second(k):
            nc.vector.tensor_tensor(z_rows[k], hs[k][:].indirect(pos2_sb[:]), first[k], ALU.add)
            for i in range(4):
                nc.sync.dma_start(z_f0[32 * k : 32 * (k + 1), i, :], z_rows[k][i:P:4, :])

        def pick_second_part(k, part):
            m0, m1, banks = part
            picked = hs[k][:].indirect(pos2_sb[:, m0 // 16 : m1 // 16])
            nc.vector.tensor_tensor(z_f1[m0][:, k - 4, :], picked, first[k][:, m0:m1], ALU.add)

        def rounded_z(b, m0, m1):
            return z_bf[b][:, 4 * m0 : 4 * m1]

        def round_z(b, m0, m1, on_vector):
            run = 4 if on_vector else 2
            dst = rounded_z(b, m0, m1).rearrange("p (c j t) -> p c t j", j=run, t=4)
            src = (z_f1[m0] if b == 1 else z_f0[:, :, m0:m1]).rearrange("p t (c j) -> p c t j", j=run)
            if on_vector:
                nc.vector.tensor_scalar(dst, src, W2, 0.0, ALU.mult, ALU.add)
            else:
                nc.scalar.activation(dst, src, ACT.Copy, scale=W2)

        def quant_z(b, m0, m1):
            nc.vector.quantize_mx(z_w[b][:, m0:m1].bitcast(FP8X4), z_sc[b][:, m0:m1], rounded_z(b, m0, m1))

        def down(b, part):
            m0, m1, banks = part
            each = 4 // banks
            if b == 0:
                tags = {0: ("100", "101"), 384: ("000",), 256: ("001", "110")}[m0]
                bank_o[m0] = [bank("bank_o%d_%d" % (m0, i), tags[i]) for i in range(banks)]
            for n in range(4):
                rows = slice(P * n, P * (n + 1))
                nc.tensor.matmul_mx(
                    bank_o[m0][n // each][:, (m1 - m0) * (n % each) : (m1 - m0) * (n % each + 1)],
                    lhsT=w2_w[b][:, rows].bitcast(FP8X4),
                    lhsT_scale=w2_sc[b][:, rows],
                    rhs=z_w[b][:, m0:m1].bitcast(FP8X4),
                    rhs_scale=z_sc[b][:, m0:m1],
                    start=(b == 0 and n % each == 0),
                    stop=(b == 1 and n % each == each - 1),
                )

        def store(part, i, on_vector):
            m0, m1, banks = part
            each = 4 // banks
            src = bank_o[m0][i][:, 0 : each * (m1 - m0)].rearrange("p (n m) -> p n m", n=each)
            if on_vector:
                nc.vector.tensor_copy(res[m0, i][:], src)
            else:
                nc.scalar.copy(res[m0, i][:], src)
            dst = out[each * P * i : each * P * (i + 1), m0:m1].rearrange("(n p) m -> p n m", p=P)
            (nc.scalar if part is LAST and not on_vector else nc.sync).dma_start(dst, res[m0, i][:])

        round_wu(0, 0, nc.scalar)
        round_wu(0, 1, nc.gpsimd)
        for k, u, a in ((0, 0, 0), (0, 1, 0), (1, 1, 0), (1, 0, 0), (0, 0, 1), (0, 1, 1)):
            gate_pass(k, u, a)
        quant_wu_pass(0, 0)
        for u in range(2):
            up_pass(0, u, 0)
        for k in range(2):
            round_wu(1, k, nc.vector)
        quant_wu_pass(0, 1)
        for u in range(2):
            up_pass(0, u, 1)
        quant_wu(1)
        for u in (1, 0):
            gate_pass(1, u, 1)
        order_wg_scales()
        order_wg()
        for u in range(2):
            product_vector(0, u)
        round_wu(0, 2, nc.gpsimd)
        round_wu(1, 2, nc.scalar)
        quant_wu(2)

        def gates(k):
            for u in (1, 0):
                for a in range(2):
                    gate_pass(k, u, a)

        def up_parked(k):
            for a in range(2):
                up_pass(k, 1, a)
            park(k)
            for a in range(2):
                up_pass(k, 0, a)

        def up_vector(k, u):
            for a in range(2):
                up_pass(k, u, a)
            product_vector(k, u)

        def round_both(k):
            for a in range(2):
                round_wu(a, k, nc.scalar)

        up_parked(1)
        product_gpsimd(1)
        pick_first(0)
        product_vector(1, 0)
        for a in range(2):
            gate_pass(2, 1, a)
        up_parked(2)
        pick_second(0)
        round_both(3)
        quant_wu(3)
        product_gpsimd(2)
        for a in range(2):
            gate_pass(2, 0, a)

        pick_first(1)
        product_vector(2, 0)
        gates(3)
        gates(4)
        up_parked(3)
        pick_second(1)
        product_gpsimd(3)
        for a in range(2):
            nc.scalar.copy(
                wu_bf45.rearrange("p (t a g j i) -> p a t g i j", t=2, a=2, j=8, i=4)[:, a],
                wu_late[a].rearrange("p i (g t j) -> p t g i j", t=4, j=8)[:, 0:2],
            )

        pick_first(2)
        product_vector(3, 0)
        pick_second(2)
        for t in range(2):
            nc.vector.quantize_mx(wu_w[4 + t].bitcast(FP8X4), wu_sc[4 + t], wu_bf45[:, 1024 * t : 1024 * (t + 1)])
        round_gpsimd(w2_bf[0][:, 1024:2048], w2_raw[0][:, :, 256:N])
        gates(5)
        for k in (6, 7):
            round_both(k)

        pick_first(3)
        for u in range(2):
            up_vector(4, u)
        up_parked(5)
        pick_second(3)
        quant_wu(6)
        product_gpsimd(5)
        gates(6)
        round_w2(0, 0)

        pick_first(4)
        product_vector(5, 0)
        up_parked(6)
        pick_second_part(4, EARLY)
        quant_wu(7)
        product_gpsimd(6)
        gates(7)

        pick_first(5)
        product_vector(6, 0)
        up_parked(7)
        pick_second_part(5, EARLY)
        product_gpsimd(7)
        for u in range(2):
            round_w2(1, u)
        round_z(0, 0, M, False)

        pick_first(6)
        product_vector(7, 0)
        pick_second_part(6, EARLY)
        quant_w2(0)
        pick_first(7)
        quant_w2(1)
        quant_z(0, 0, M)

        for part in PARTS:
            down(0, part)
        pick_second_part(7, EARLY)
        round_z(1, 0, PART, False)
        for k in range(4, SLICES):
            pick_second_part(k, MIDDLE)
        round_z(1, 384, M, False)
        pick_second_part(7, LAST)
        quant_z(1, 0, PART)
        down(1, EARLY)
        for i in range(2):
            store(EARLY, i, False)
        for k in (4, 5, 6):
            pick_second_part(k, LAST)
        round_z(1, PART, 384, True)
        quant_z(1, 384, M)
        down(1, MIDDLE)
        quant_z(1, PART, 384)
        down(1, LAST)
        store(MIDDLE, 0, True)
        for i in range(2):
            store(LAST, i, i == 1)
